import numpy as np
import ml_dtypes


def mxq(x, axis, fmt="e4m3"):
    dtype, down = {"e4m3": (ml_dtypes.float8_e4m3fn, 7), "e5m2": (ml_dtypes.float8_e5m2, 14)}[fmt]
    v = np.moveaxis(np.asarray(x, np.float32).astype(ml_dtypes.bfloat16).astype(np.float64), axis, -1)
    blocks = v.reshape(v.shape[:-1] + (-1, 32))
    amax = np.abs(blocks).max(-1, keepdims=True)
    byte = np.maximum(np.where(amax > 0, np.frexp(amax)[1] - 1 + 127, 0) - down, 1)
    scale = np.exp2(byte - 127.0)
    codes = (blocks / scale).astype(np.float32).astype(dtype).astype(np.float64)
    return np.moveaxis((codes * scale).reshape(v.shape), -1, axis)


WIDE = False


def mx_kscale(k):
    if not WIDE:
        return np.ones(k)
    levels = np.array([10, -10, 5, -5, 0])
    if k % 512:
        return np.exp2(np.random.permutation(np.resize(levels, k // 32))).repeat(32)
    a = np.empty((k // 512, 16))
    for p in range(k // 512):
        a[p, :8] = np.random.permutation(np.resize(levels, 8))
        for g in range(8):
            far = levels[np.abs(levels - a[p, g]) >= 10]
            a[p, g + 8] = far[np.random.randint(len(far))]
    return np.exp2(a.ravel()).repeat(32)


def f64(x):
    return np.asarray(x).astype(np.float64)


def striped(idx):
    return np.tile(idx.reshape(-1, 16).T, (8, 1)).astype(np.uint16)


def unstriped(offs):
    return offs[:16].T.reshape(-1).astype(np.int64)


E2M1 = np.array([0.0, 0.5, 1.0, 1.5, 2.0, 3.0, 4.0, 6.0, -0.0, -0.5, -1.0, -1.5, -2.0, -3.0, -4.0, -6.0])


def pack_weight(w, fmt):
    k, n = w.shape
    w = f64(np.asarray(w, np.float32).astype(ml_dtypes.bfloat16)).reshape(k // 32, 32, n)
    amax = np.abs(w).max(1)
    if fmt == "e4m3":
        byte = np.frexp(amax)[1] - 1 + 127 - 7
    else:
        mant, ex = np.frexp(amax / 6.0)
        byte = np.where(mant > 0.5, ex, ex - 1) + 127
    byte = np.clip(np.where(amax > 0, byte, 1), 1, 254)
    scaled = (w * np.exp2(127.0 - byte)[:, None, :]).reshape(k, n).astype(np.float32)
    by_word = np.ascontiguousarray(scaled.reshape(k // 512, 128, 4, n).transpose(0, 1, 3, 2))
    if fmt == "e4m3":
        words = by_word.astype(ml_dtypes.float8_e4m3fn).view(np.uint8)
    else:
        c = by_word.astype(ml_dtypes.float4_e2m1fn).view(np.uint8) & 0xF
        words = (c[..., 0::2] | (c[..., 1::2] << 4)).reshape(k // 512, 128, 2 * n)
    return np.ascontiguousarray(words), np.ascontiguousarray(byte.astype(np.uint8).reshape(k // 512, 16, n))


def unpack_weight(words, scales, fmt):
    g, _, n = scales.shape
    words = np.ascontiguousarray(words).reshape(g, 128, n, -1)
    if fmt == "e4m3":
        vals = words.view(ml_dtypes.float8_e4m3fn).astype(np.float64)
    else:
        nib = np.empty((g, 128, n, 4), np.uint8)
        nib[..., 0::2] = words & 0xF
        nib[..., 1::2] = words >> 4
        vals = E2M1[nib]
    vals = vals * np.repeat(np.exp2(scales.astype(np.float64) - 127.0), 8, axis=1)[..., None]
    return vals.transpose(0, 1, 3, 2).reshape(g * 512, n)


def gelu(v):
    return 0.5 * v * (1.0 + np.tanh(np.sqrt(2.0 / np.pi) * (v + 0.044715 * v**3)))


K, T, S, T2, S2, N = 512, 4096, 1536, 2048, 1024, 512

def setup_inputs():
    n = np.random.standard_normal
    s = mx_kscale(K)[:, None]
    u = mx_kscale(S)[:, None]
    tab_words, tab_scales = pack_weight(n((K, T)) * s, "e4m3")
    tab2_words, tab2_scales = pack_weight(n((K, T2)) / np.sqrt(K) / s, "e4m3")
    w4_words, w4_scales = pack_weight(n((S, N)) / np.sqrt(S) / u, "e2m1")
    return {
        "tab_words": tab_words, "tab_scales": tab_scales,
        "tab2_words": tab2_words, "tab2_scales": tab2_scales,
        "offs": striped(np.random.permutation(T)[:S]),
        "offs2": striped(np.random.permutation(T2)[:S2]),
        "bid": (np.exp(0.3 * n(S)) * u[:, 0]).astype(np.float32),
        "w4_words": w4_words, "w4_scales": w4_scales,
        "wd": (0.6 * n((S, N)) / np.sqrt(S) / u).astype(np.float32),
        "b": (0.3 * n(N)).astype(np.float32),
    }

def reference(tab_words, tab_scales, tab2_words, tab2_scales, offs, offs2, bid, w4_words, w4_scales, wd, b):
    v = unpack_weight(tab_words, tab_scales, "e4m3")[:, unstriped(offs)]
    v2 = unpack_weight(tab2_words, tab2_scales, "e4m3")[:, unstriped(offs2)]
    a = v.T @ v2
    gate = 1.0 / (1.0 + np.exp(-a))
    h = a * gate * f64(bid)[:, None]
    hq = mxq(h, 0, "e4m3")
    w4 = unpack_weight(w4_words, w4_scales, "e2m1")
    wdq = mxq(f64(wd), 0, "e4m3")
    y = w4.T @ hq + wdq.T @ hq
    return y + f64(b)[:, None]

@@ -1,0 +1,204 @@
+from contextlib import ExitStack
+
+import concourse.mybir as mybir
+
+K, T, S, T2, S2, N = 512, 4096, 1536, 2048, 1024, 512
+FLOPS = 2 * K * S * S2 + 2 * 2 * S * N * S2
+
+F32 = mybir.dt.float32
+BF16 = mybir.dt.bfloat16
+I32 = mybir.dt.int32
+U32 = mybir.dt.uint32
+U16 = mybir.dt.uint16
+U8 = mybir.dt.uint8
+FP8X4 = mybir.dt.float8_e4m3fn_x4
+FP4X4 = mybir.dt.float4_e2m1fn_x4
+ACT = mybir.ActivationFunctionType
+ALU = mybir.AluOpType
+
+P = 128
+G = S // 512
+HALF = 512
+BLK = 256
+KOFF = 4
+
+
+def tile_list_keyword_campaign_values_kernel(
+    tc, tab_words, tab_scales, tab2_words, tab2_scales, offs, offs2, bid, w4_words, w4_scales, wd, b, out
+):
+    nc = tc.nc
+    with ExitStack() as ctx:
+        keep = ctx.enter_context(tc.tile_pool(name="keep", bufs=1))
+        ring = ctx.enter_context(tc.tile_pool(name="ring", bufs=3))
+        ps_a = ctx.enter_context(tc.psum_pool(name="ps_a", bufs=4))
+        ps_y = ctx.enter_context(tc.psum_pool(name="ps_y", bufs=1))
+
+        offs_t = keep.tile([P, S // 16], U16, name="offs_t")
+        offs2_t = keep.tile([P, S2 // 16], U16, name="offs2_t")
+        tabw = keep.tile([P, T], I32, name="tabw", align_bytes=64)
+        tab2w = keep.tile([P, T2], I32, name="tab2w", align_bytes=64)
+        tabs = keep.tile([P, T // 4], I32, name="tabs", align_bytes=64)
+        tab2s = keep.tile([P, T2 // 4], I32, name="tab2s", align_bytes=64)
+        w4w = keep.tile([P, G, 2 * N], U8, name="w4w", align_bytes=64)
+        w4s = keep.tile([P, G, N // 4], I32, name="w4s", align_bytes=64)
+        bid_t = keep.tile([P, G, 4], F32, name="bid_t", align_bytes=64)
+        b_t = keep.tile([P, 4], F32, name="b_t")
+        warm = keep.tile([P, 2], F32, name="warm")
+        wd_raw = [keep.tile([P, 4, N], F32, name="wd_raw%d" % g) for g in range(G)]
+
+        nc.vector.memset(tab2s[:], 0)
+        nc.vector.memset(tabs[:], 0)
+        nc.vector.memset(w4s[:], 0)
+        nc.vector.memset(warm[:, 0:1], 0.0)
+        nc.sync.dma_start(offs2_t[:], offs2)
+        nc.sync.dma_start(offs_t[:], offs)
+
+        nc.gpsimd.dma_start(tabw[:], tab_words[0].rearrange("p t i -> p (t i)").bitcast(I32))
+        nc.gpsimd.dma_start(tab2w[:], tab2_words[0].rearrange("p t i -> p (t i)").bitcast(I32))
+        nc.gpsimd.dma_start(bid_t[:], bid.rearrange("(g p t) -> p g t", g=G, t=4))
+        for g in range(G):
+            nc.gpsimd.dma_start(wd_raw[g][:], wd[512 * g : 512 * (g + 1), :].rearrange("(p t) n -> p t n", t=4))
+            if g == 0:
+                nc.gpsimd.dma_start(w4w[:].bitcast(I32), w4_words.rearrange("g p c -> p g c").bitcast(I32))
+        with nc.allow_non_contiguous_dma(reason="one bias value to a partition"):
+            nc.gpsimd.dma_start(b_t[:], b.rearrange("(c p) -> p c", p=P))
+
+        for q in range(4):
+            nc.sync.dma_start(tab2s[32 * q : 32 * q + 4, :], tab2_scales[0, 4 * q : 4 * q + 4, :].bitcast(I32))
+        for q in range(4):
+            nc.scalar.dma_start(
+                tabs[32 * q + KOFF : 32 * q + KOFF + 4, :], tab_scales[0, 4 * q : 4 * q + 4, :].bitcast(I32)
+            )
+        for q in range(4):
+            nc.sync.dma_start(
+                w4s[32 * q : 32 * q + 4, :, :],
+                w4_scales[:, 4 * q : 4 * q + 4, :].rearrange("g r c -> r g c").bitcast(I32),
+            )
+        nc.scalar.activation(warm[:, 1:2], warm[:, 0:1], ACT.Silu)
+
+        vw, vs, uw, us, wdq, wds = {}, {}, {}, {}, {}, {}
+
+        def gather_user_scales(hf):
+            us[hf] = keep.tile([P, HALF], U8, name="us%d" % hf, align_bytes=64)
+            nc.vector.tensor_copy(us[hf][:], tab2s[:].bitcast(U8).indirect(offs2_t[:, 32 * hf : 32 * (hf + 1)]))
+
+        def gather_user_words(hf):
+            uw[hf] = keep.tile([P, HALF], U32, name="uw%d" % hf, align_bytes=64)
+            nc.vector.tensor_copy(uw[hf][:], tab2w[:].bitcast(U32).indirect(offs2_t[:, 32 * hf : 32 * (hf + 1)]))
+
+        def gather_key_scales(g):
+            raw = keep.tile([P, 512], U8, name="vsraw%d" % g, align_bytes=64)
+            nc.vector.tensor_copy(raw[:], tabs[:].bitcast(U8).indirect(offs_t[:, 32 * g : 32 * (g + 1)]))
+            vs[g] = keep.tile([P, 512], U8, name="vs%d" % g, align_bytes=64)
+            nc.vector.tensor_copy(
+                vs[g][:].rearrange("p (t m) -> p t m", t=4), raw[:].rearrange("p (m t) -> p t m", t=4)
+            )
+
+        def gather_key_words(g):
+            vw[g] = keep.tile([P, 512], U32, name="vw%d" % g, align_bytes=64)
+            nc.vector.tensor_copy(
+                vw[g][:].rearrange("p (t m) -> p m t", t=4),
+                tabw[:].bitcast(U32).indirect(offs_t[:, 32 * g : 32 * (g + 1)]),
+            )
+
+        def quantise_wd(g):
+            wb = ring.tile([P, N, 4], BF16, name="wb", align_bytes=64)
+            for n0 in range(0, N, 256):
+                nc.scalar.copy(
+                    wb[:, n0 : n0 + 256, :].rearrange("p (c i) t -> p c t i", i=4),
+                    wd_raw[g][:, :, n0 : n0 + 256].rearrange("p t (c i) -> p c t i", i=4),
+                )
+            wdq[g] = keep.tile([P, N], U32, name="wdq%d" % g, align_bytes=64)
+            wds[g] = keep.tile([P, N], U8, name="wds%d" % g, align_bytes=64)
+            nc.vector.quantize_mx(
+                out=wdq[g][:].bitcast(FP8X4), scales=wds[g][:], in_=wb[:].rearrange("p n t -> p (n t)")
+            )
+
+        def scores(g, hf):
+            hb = ring.tile([P, HALF, 2, 2], BF16, name="hb", align_bytes=64)
+            for j0 in range(0, HALF, BLK):
+                cols = slice(j0, j0 + BLK)
+                sil = ring.tile([P, 2, BLK, 2], F32, name="sil", align_bytes=64)
+                for u in range(2):
+                    a_ps = ps_a.tile([P, 2, BLK], F32, name="a_ps")
+                    for e in range(2):
+                        m = slice(128 * (2 * u + e), 128 * (2 * u + e + 1))
+                        nc.tensor.matmul_mx(
+                            out=a_ps[:, e, :],
+                            lhsT=vw[g][:, m].bitcast(FP8X4),
+                            lhsT_scale=vs[g][KOFF:P, m],
+                            rhs=uw[hf][:, cols].bitcast(FP8X4),
+                            rhs_scale=us[hf][:, cols],
+                            start=True,
+                            stop=True,
+                        )
+                    nc.scalar.activation(sil[:, u, :, :], a_ps[:].rearrange("p e n -> p n e"), ACT.Silu)
+                nc.vector.tensor_tensor(
+                    hb[:, cols, :, :],
+                    sil[:].rearrange("p u n e -> p n u e"),
+                    bid_t[:, g, :].rearrange("p (u e) -> p u e", u=2).unsqueeze(1).to_broadcast([P, BLK, 2, 2]),
+                    ALU.mult,
+                )
+            hq = ring.tile([P, HALF], U32, name="hq", align_bytes=64)
+            hs = ring.tile([P, HALF], U8, name="hs", align_bytes=64)
+            nc.vector.quantize_mx(
+                out=hq[:].bitcast(FP8X4), scales=hs[:], in_=hb[:].rearrange("p n u e -> p (n u e)")
+            )
+            return hq, hs
+
+        def values(g, hq, hs, y_ps):
+            for c in range(4):
+                nc.tensor.matmul_mx(
+                    out=y_ps[c][:],
+                    lhsT=w4w[:, g, 256 * c : 256 * (c + 1)].bitcast(FP4X4),
+                    lhsT_scale=w4s[:, g, :].bitcast(U8)[:, 128 * c : 128 * (c + 1)],
+                    rhs=hq[:].bitcast(FP8X4),
+                    rhs_scale=hs[:],
+                    start=(g == 0),
+                    stop=False,
+                )
+                nc.tensor.matmul_mx(
+                    out=y_ps[c][:],
+                    lhsT=wdq[g][:, 128 * c : 128 * (c + 1)].bitcast(FP8X4),
+                    lhsT_scale=wds[g][:, 128 * c : 128 * (c + 1)],
+                    rhs=hq[:].bitcast(FP8X4),
+                    rhs_scale=hs[:],
+                    start=False,
+                    stop=(g == G - 1),
+                )
+
+        def finish(hf, y_ps):
+            for c in range(4):
+                o = ring.tile([P, HALF], F32, name="o", bufs=4)
+                if hf == 0 or c % 2 == 0:
+                    nc.scalar.activation(o[:], y_ps[c][:], ACT.Identity, bias=b_t[:, c : c + 1])
+                else:
+                    nc.vector.tensor_scalar(o[:], y_ps[c][:], b_t[:, c : c + 1], None, ALU.add)
+                nc.sync.dma_start(out[128 * c : 128 * (c + 1), HALF * hf : HALF * (hf + 1)], o[:])
+
+        gather_user_scales(0)
+        gather_key_scales(0)
+        gather_key_words(0)
+        gather_user_words(0)
+        units = [(g, hf) for hf in range(2) for g in range(G)]
+        pending = None
+        y_ps = None
+        for g, hf in units:
+            if hf == 0 and g > 0:
+                gather_key_scales(g)
+                gather_key_words(g)
+            if hf == 1 and g == 0:
+                gather_user_scales(1)
+                gather_user_words(1)
+            hq, hs = scores(g, hf)
+            if pending is not None:
+                values(*pending)
+                if pending[0] == G - 1:
+                    finish(0, pending[3])
+            if hf == 0:
+                quantise_wd(g)
+            if g == 0:
+                y_ps = [ps_y.tile([P, HALF], F32, name="y%d" % c) for c in range(4)]
+            pending = (g, hq, hs, y_ps)
+        values(*pending)
+        finish(1, pending[3])

@@ -17,10 +17,17 @@ ACT = mybir.ActivationFunctionType
 ALU = mybir.AluOpType
 
 P = 128
-G = S // 512
+PACK = 4
+PASS = P * PACK
+PASSES = S // PASS
+LIST_COLS = PASS // 16
+QUADRANTS = 4
 HALF = 512
-BLK = 256
-KOFF = 4
+BLOCK = 256
+N_TILES = N // P
+KEY_SCALE_ROW = 4
+CAST_COLS = 128
+CAST_ON_VECTOR = (2, 0)
 
 
 def tile_list_keyword_campaign_values_kernel(
@@ -30,175 +37,184 @@ def tile_list_keyword_campaign_values_kernel(
     with ExitStack() as ctx:
         keep = ctx.enter_context(tc.tile_pool(name="keep", bufs=1))
         ring = ctx.enter_context(tc.tile_pool(name="ring", bufs=3))
-        ps_a = ctx.enter_context(tc.psum_pool(name="ps_a", bufs=4))
-        ps_y = ctx.enter_context(tc.psum_pool(name="ps_y", bufs=1))
+        score_banks = ctx.enter_context(tc.psum_pool(name="score_banks", bufs=4))
+        value_banks = ctx.enter_context(tc.psum_pool(name="value_banks", bufs=1))
 
-        offs_t = keep.tile([P, S // 16], U16, name="offs_t")
-        offs2_t = keep.tile([P, S2 // 16], U16, name="offs2_t")
-        tabw = keep.tile([P, T], I32, name="tabw", align_bytes=64)
-        tab2w = keep.tile([P, T2], I32, name="tab2w", align_bytes=64)
-        tabs = keep.tile([P, T // 4], I32, name="tabs", align_bytes=64)
-        tab2s = keep.tile([P, T2 // 4], I32, name="tab2s", align_bytes=64)
-        w4w = keep.tile([P, G, 2 * N], U8, name="w4w", align_bytes=64)
-        w4s = keep.tile([P, G, N // 4], I32, name="w4s", align_bytes=64)
-        bid_t = keep.tile([P, G, 4], F32, name="bid_t", align_bytes=64)
-        b_t = keep.tile([P, 4], F32, name="b_t")
-        warm = keep.tile([P, 2], F32, name="warm")
-        wd_raw = [keep.tile([P, 4, N], F32, name="wd_raw%d" % g) for g in range(G)]
+        key_list = keep.tile([P, S // 16], U16, name="key_list")
+        user_list = keep.tile([P, S2 // 16], U16, name="user_list")
+        key_table = keep.tile([P, T], I32, name="key_table", align_bytes=64)
+        user_table = keep.tile([P, T2], I32, name="user_table", align_bytes=64)
+        key_table_scales = keep.tile([P, T // 4], I32, name="key_table_scales", align_bytes=64)
+        user_table_scales = keep.tile([P, T2 // 4], I32, name="user_table_scales", align_bytes=64)
+        w4_codes = keep.tile([P, PASSES, 2 * N], U8, name="w4_codes", align_bytes=64)
+        w4_scale_tile = keep.tile([P, PASSES, N // 4], I32, name="w4_scale_tile", align_bytes=64)
+        bid_tile = keep.tile([P, PASSES, PACK], F32, name="bid_tile", align_bytes=64)
+        bias_tile = keep.tile([P, N_TILES], F32, name="bias_tile")
+        wd_raw = [keep.tile([P, PACK, N], F32, name="wd_raw%d" % g) for g in range(PASSES)]
 
-        nc.vector.memset(tab2s[:], 0)
-        nc.vector.memset(tabs[:], 0)
-        nc.vector.memset(w4s[:], 0)
-        nc.vector.memset(warm[:, 0:1], 0.0)
-        nc.sync.dma_start(offs2_t[:], offs2)
-        nc.sync.dma_start(offs_t[:], offs)
+        def load_wd(g):
+            rows = wd[PASS * g : PASS * (g + 1), :]
+            nc.sync.dma_start(wd_raw[g][:], rows.rearrange("(p t) n -> p t n", t=PACK))
 
-        nc.gpsimd.dma_start(tabw[:], tab_words[0].rearrange("p t i -> p (t i)").bitcast(I32))
-        nc.gpsimd.dma_start(tab2w[:], tab2_words[0].rearrange("p t i -> p (t i)").bitcast(I32))
-        nc.gpsimd.dma_start(bid_t[:], bid.rearrange("(g p t) -> p g t", g=G, t=4))
-        for g in range(G):
-            nc.gpsimd.dma_start(wd_raw[g][:], wd[512 * g : 512 * (g + 1), :].rearrange("(p t) n -> p t n", t=4))
-            if g == 0:
-                nc.gpsimd.dma_start(w4w[:].bitcast(I32), w4_words.rearrange("g p c -> p g c").bitcast(I32))
-        with nc.allow_non_contiguous_dma(reason="one bias value to a partition"):
-            nc.gpsimd.dma_start(b_t[:], b.rearrange("(c p) -> p c", p=P))
+        nc.vector.memset(user_table_scales[:], 0)
+        nc.vector.memset(key_table_scales[:], 0)
+        nc.vector.memset(w4_scale_tile[:], 0)
 
-        for q in range(4):
-            nc.sync.dma_start(tab2s[32 * q : 32 * q + 4, :], tab2_scales[0, 4 * q : 4 * q + 4, :].bitcast(I32))
-        for q in range(4):
-            nc.scalar.dma_start(
-                tabs[32 * q + KOFF : 32 * q + KOFF + 4, :], tab_scales[0, 4 * q : 4 * q + 4, :].bitcast(I32)
-            )
-        for q in range(4):
+        nc.sync.dma_start(user_list[:], offs2)
+        nc.sync.dma_start(key_list[:], offs)
+        for q in range(QUADRANTS):
+            queue = nc.scalar if q < QUADRANTS // 2 else nc.sync
+            queue.dma_start(user_table_scales[32 * q : 32 * q + 4, :], tab2_scales[0, 4 * q : 4 * q + 4, :].bitcast(I32))
+        nc.sync.dma_start(user_table[:], tab2_words[0].rearrange("p t i -> p (t i)").bitcast(I32))
+        for q in range(QUADRANTS):
+            row = 32 * q + KEY_SCALE_ROW
+            nc.sync.dma_start(key_table_scales[row : row + 4, :], tab_scales[0, 4 * q : 4 * q + 4, :].bitcast(I32))
+        load_wd(0)
+        nc.sync.dma_start(key_table[:], tab_words[0].rearrange("p t i -> p (t i)").bitcast(I32))
+        nc.sync.dma_start(bid_tile[:], bid.rearrange("(g p t) -> p g t", g=PASSES, t=PACK))
+        load_wd(1)
+        for q in range(QUADRANTS):
             nc.sync.dma_start(
-                w4s[32 * q : 32 * q + 4, :, :],
+                w4_scale_tile[32 * q : 32 * q + 4, :, :],
                 w4_scales[:, 4 * q : 4 * q + 4, :].rearrange("g r c -> r g c").bitcast(I32),
             )
-        nc.scalar.activation(warm[:, 1:2], warm[:, 0:1], ACT.Silu)
+        nc.sync.dma_start(w4_codes[:].bitcast(I32), w4_words.rearrange("g p c -> p g c").bitcast(I32))
+        load_wd(2)
+        with nc.allow_non_contiguous_dma(reason="one bias value to a partition and campaign tile"):
+            nc.sync.dma_start(bias_tile[:], b.rearrange("(c p) -> p c", p=P))
 
-        vw, vs, uw, us, wdq, wds = {}, {}, {}, {}, {}, {}
+        user_scales = keep.tile([P, S2], U8, name="user_scales", align_bytes=64)
+        key_scales = keep.tile([P, S], U8, name="key_scales", align_bytes=64)
+        user_words, key_words, wd_codes, wd_scales, h_codes, h_scales, sums = {}, {}, {}, {}, {}, {}, {}
 
-        def gather_user_scales(hf):
-            us[hf] = keep.tile([P, HALF], U8, name="us%d" % hf, align_bytes=64)
-            nc.vector.tensor_copy(us[hf][:], tab2s[:].bitcast(U8).indirect(offs2_t[:, 32 * hf : 32 * (hf + 1)]))
+        def gather_user_words(half):
+            name = "user_words%d" % half
+            user_words[half] = keep.tile([P, HALF], U32, name=name, tag=name, align_bytes=64)
+            entries = user_list[:, LIST_COLS * half : LIST_COLS * (half + 1)]
+            nc.vector.tensor_copy(user_words[half][:], user_table[:].bitcast(U32).indirect(entries))
 
-        def gather_user_words(hf):
-            uw[hf] = keep.tile([P, HALF], U32, name="uw%d" % hf, align_bytes=64)
-            nc.vector.tensor_copy(uw[hf][:], tab2w[:].bitcast(U32).indirect(offs2_t[:, 32 * hf : 32 * (hf + 1)]))
-
-        def gather_key_scales(g):
-            raw = keep.tile([P, 512], U8, name="vsraw%d" % g, align_bytes=64)
-            nc.vector.tensor_copy(raw[:], tabs[:].bitcast(U8).indirect(offs_t[:, 32 * g : 32 * (g + 1)]))
-            vs[g] = keep.tile([P, 512], U8, name="vs%d" % g, align_bytes=64)
+        def gather_key_scales(g0, g1):
+            in_order = keep.tile([P, PASS * (g1 - g0)], U8, name="key_scales_in_order%d" % g0, align_bytes=64)
+            entries = key_list[:, LIST_COLS * g0 : LIST_COLS * g1]
+            nc.vector.tensor_copy(in_order[:], key_table_scales[:].bitcast(U8).indirect(entries))
             nc.vector.tensor_copy(
-                vs[g][:].rearrange("p (t m) -> p t m", t=4), raw[:].rearrange("p (m t) -> p t m", t=4)
+                key_scales[:, PASS * g0 : PASS * g1].rearrange("p (g t m) -> p g t m", t=PACK, m=P),
+                in_order[:].rearrange("p (g m t) -> p g t m", t=PACK, m=P),
             )
 
         def gather_key_words(g):
-            vw[g] = keep.tile([P, 512], U32, name="vw%d" % g, align_bytes=64)
+            key_words[g] = keep.tile([P, PASS], U32, name="key_words%d" % g, align_bytes=64)
+            entries = key_list[:, LIST_COLS * g : LIST_COLS * (g + 1)]
             nc.vector.tensor_copy(
-                vw[g][:].rearrange("p (t m) -> p m t", t=4),
-                tabw[:].bitcast(U32).indirect(offs_t[:, 32 * g : 32 * (g + 1)]),
+                key_words[g][:].rearrange("p (t m) -> p m t", t=PACK), key_table[:].bitcast(U32).indirect(entries)
             )
 
         def quantise_wd(g):
-            wb = ring.tile([P, N, 4], BF16, name="wb", align_bytes=64)
-            for n0 in range(0, N, 256):
-                nc.scalar.copy(
-                    wb[:, n0 : n0 + 256, :].rearrange("p (c i) t -> p c t i", i=4),
-                    wd_raw[g][:, :, n0 : n0 + 256].rearrange("p t (c i) -> p c t i", i=4),
-                )
-            wdq[g] = keep.tile([P, N], U32, name="wdq%d" % g, align_bytes=64)
-            wds[g] = keep.tile([P, N], U8, name="wds%d" % g, align_bytes=64)
+            rounded = ring.tile([P, N, PACK], BF16, name="wd_rounded", align_bytes=64)
+            for n0 in range(0, N, CAST_COLS):
+                dst = rounded[:, n0 : n0 + CAST_COLS, :].rearrange("p (c i) t -> p c t i", i=4)
+                src = wd_raw[g][:, :, n0 : n0 + CAST_COLS].rearrange("p t (c i) -> p c t i", i=4)
+                if (g, n0) == CAST_ON_VECTOR:
+                    nc.vector.tensor_copy(dst, src)
+                else:
+                    nc.scalar.copy(dst, src)
+            wd_codes[g] = keep.tile([P, N], U32, name="wd_codes%d" % g, align_bytes=64)
+            wd_scales[g] = keep.tile([P, N], U8, name="wd_scales%d" % g, align_bytes=64)
             nc.vector.quantize_mx(
-                out=wdq[g][:].bitcast(FP8X4), scales=wds[g][:], in_=wb[:].rearrange("p n t -> p (n t)")
+                out=wd_codes[g][:].bitcast(FP8X4), scales=wd_scales[g][:], in_=rounded[:].rearrange("p n t -> p (n t)")
             )
 
-        def scores(g, hf):
-            hb = ring.tile([P, HALF, 2, 2], BF16, name="hb", align_bytes=64)
-            for j0 in range(0, HALF, BLK):
-                cols = slice(j0, j0 + BLK)
-                sil = ring.tile([P, 2, BLK, 2], F32, name="sil", align_bytes=64)
+        def make_h(g, half, second_silu_tag="silu", quantise_cols=HALF):
+            h_rounded = ring.tile([P, HALF, 2, 2], BF16, name="h_rounded", align_bytes=64)
+            for j0 in range(0, HALF, BLOCK):
+                if j0 == 0 or second_silu_tag == "silu":
+                    silu = ring.tile([P, 2, BLOCK, 2], F32, name="silu", align_bytes=64, bufs=5)
+                else:
+                    silu = keep.tile([P, 2, BLOCK, 2], F32, name="silu_lent", tag=second_silu_tag, align_bytes=64)
+                users = slice(HALF * half + j0, HALF * half + j0 + BLOCK)
                 for u in range(2):
-                    a_ps = ps_a.tile([P, 2, BLK], F32, name="a_ps")
+                    scores = score_banks.tile([P, 2, BLOCK], F32, name="scores")
                     for e in range(2):
-                        m = slice(128 * (2 * u + e), 128 * (2 * u + e + 1))
+                        m0 = P * (2 * u + e)
                         nc.tensor.matmul_mx(
-                            out=a_ps[:, e, :],
-                            lhsT=vw[g][:, m].bitcast(FP8X4),
-                            lhsT_scale=vs[g][KOFF:P, m],
-                            rhs=uw[hf][:, cols].bitcast(FP8X4),
-                            rhs_scale=us[hf][:, cols],
+                            out=scores[:, e, :],
+                            lhsT=key_words[g][:, m0 : m0 + P].bitcast(FP8X4),
+                            lhsT_scale=key_scales[KEY_SCALE_ROW:P, PASS * g + m0 : PASS * g + m0 + P],
+                            rhs=user_words[half][:, j0 : j0 + BLOCK].bitcast(FP8X4),
+                            rhs_scale=user_scales[:, users],
                             start=True,
                             stop=True,
                         )
-                    nc.scalar.activation(sil[:, u, :, :], a_ps[:].rearrange("p e n -> p n e"), ACT.Silu)
+                    nc.scalar.activation(silu[:, u, :, :], scores[:].rearrange("p e n -> p n e"), ACT.Silu)
                 nc.vector.tensor_tensor(
-                    hb[:, cols, :, :],
-                    sil[:].rearrange("p u n e -> p n u e"),
-                    bid_t[:, g, :].rearrange("p (u e) -> p u e", u=2).unsqueeze(1).to_broadcast([P, BLK, 2, 2]),
+                    h_rounded[:, j0 : j0 + BLOCK, :, :],
+                    silu[:].rearrange("p u n e -> p n u e"),
+                    bid_tile[:, g, :].rearrange("p (u e) -> p u e", u=2).unsqueeze(1).to_broadcast([P, BLOCK, 2, 2]),
                     ALU.mult,
                 )
-            hq = ring.tile([P, HALF], U32, name="hq", align_bytes=64)
-            hs = ring.tile([P, HALF], U8, name="hs", align_bytes=64)
-            nc.vector.quantize_mx(
-                out=hq[:].bitcast(FP8X4), scales=hs[:], in_=hb[:].rearrange("p n u e -> p (n u e)")
-            )
-            return hq, hs
+            h_codes[g, half] = keep.tile([P, HALF], U32, name="h_codes%d%d" % (g, half), align_bytes=64)
+            h_scales[g, half] = keep.tile([P, HALF], U8, name="h_scales%d%d" % (g, half), align_bytes=64)
+            for j0 in range(0, HALF, quantise_cols):
+                nc.vector.quantize_mx(
+                    out=h_codes[g, half][:, j0 : j0 + quantise_cols].bitcast(FP8X4),
+                    scales=h_scales[g, half][:, j0 : j0 + quantise_cols],
+                    in_=h_rounded[:, j0 : j0 + quantise_cols, :, :].rearrange("p n u e -> p (n u e)"),
+                )
 
-        def values(g, hq, hs, y_ps):
-            for c in range(4):
+        def add_pass(g, half):
+            if g == 0:
+                sums[half] = [value_banks.tile([P, HALF], F32, name="values%d" % c) for c in range(N_TILES)]
+            for c in range(N_TILES):
+                campaigns = slice(P * c, P * (c + 1))
                 nc.tensor.matmul_mx(
-                    out=y_ps[c][:],
-                    lhsT=w4w[:, g, 256 * c : 256 * (c + 1)].bitcast(FP4X4),
-                    lhsT_scale=w4s[:, g, :].bitcast(U8)[:, 128 * c : 128 * (c + 1)],
-                    rhs=hq[:].bitcast(FP8X4),
-                    rhs_scale=hs[:],
+                    out=sums[half][c][:],
+                    lhsT=w4_codes[:, g, 2 * P * c : 2 * P * (c + 1)].bitcast(FP4X4),
+                    lhsT_scale=w4_scale_tile[:, g, :].bitcast(U8)[:, campaigns],
+                    rhs=h_codes[g, half][:].bitcast(FP8X4),
+                    rhs_scale=h_scales[g, half][:],
                     start=(g == 0),
                     stop=False,
                 )
                 nc.tensor.matmul_mx(
-                    out=y_ps[c][:],
-                    lhsT=wdq[g][:, 128 * c : 128 * (c + 1)].bitcast(FP8X4),
-                    lhsT_scale=wds[g][:, 128 * c : 128 * (c + 1)],
-                    rhs=hq[:].bitcast(FP8X4),
-                    rhs_scale=hs[:],
+                    out=sums[half][c][:],
+                    lhsT=wd_codes[g][:, campaigns].bitcast(FP8X4),
+                    lhsT_scale=wd_scales[g][:, campaigns],
+                    rhs=h_codes[g, half][:].bitcast(FP8X4),
+                    rhs_scale=h_scales[g, half][:],
                     start=False,
-                    stop=(g == G - 1),
+                    stop=(g == PASSES - 1),
                 )
 
-        def finish(hf, y_ps):
-            for c in range(4):
-                o = ring.tile([P, HALF], F32, name="o", bufs=4)
-                if hf == 0 or c % 2 == 0:
-                    nc.scalar.activation(o[:], y_ps[c][:], ACT.Identity, bias=b_t[:, c : c + 1])
+        def store(half):
+            for c in range(N_TILES):
+                result = ring.tile([P, HALF], F32, name="result", bufs=N_TILES)
+                if half == 0 or c % 2 == 0:
+                    nc.scalar.activation(result[:], sums[half][c][:], ACT.Identity, bias=bias_tile[:, c : c + 1])
                 else:
-                    nc.vector.tensor_scalar(o[:], y_ps[c][:], b_t[:, c : c + 1], None, ALU.add)
-                nc.sync.dma_start(out[128 * c : 128 * (c + 1), HALF * hf : HALF * (hf + 1)], o[:])
+                    nc.vector.tensor_scalar(result[:], sums[half][c][:], bias_tile[:, c : c + 1], None, ALU.add)
+                nc.sync.dma_start(out[P * c : P * (c + 1), HALF * half : HALF * (half + 1)], result[:])
 
-        gather_user_scales(0)
-        gather_key_scales(0)
-        gather_key_words(0)
+        nc.vector.tensor_copy(user_scales[:], user_table_scales[:].bitcast(U8).indirect(user_list[:]))
         gather_user_words(0)
-        units = [(g, hf) for hf in range(2) for g in range(G)]
-        pending = None
-        y_ps = None
-        for g, hf in units:
-            if hf == 0 and g > 0:
-                gather_key_scales(g)
-                gather_key_words(g)
-            if hf == 1 and g == 0:
-                gather_user_scales(1)
-                gather_user_words(1)
-            hq, hs = scores(g, hf)
-            if pending is not None:
-                values(*pending)
-                if pending[0] == G - 1:
-                    finish(0, pending[3])
-            if hf == 0:
-                quantise_wd(g)
-            if g == 0:
-                y_ps = [ps_y.tile([P, HALF], F32, name="y%d" % c) for c in range(4)]
-            pending = (g, hq, hs, y_ps)
-        values(*pending)
-        finish(1, pending[3])
+        gather_key_scales(0, 1)
+        gather_key_words(0)
+        make_h(0, 0, second_silu_tag="user_words1")
+        gather_key_scales(1, PASSES)
+        gather_key_words(1)
+        make_h(1, 0)
+        quantise_wd(0)
+        quantise_wd(1)
+        add_pass(0, 0)
+        gather_key_words(2)
+        make_h(2, 0)
+        quantise_wd(2)
+        gather_user_words(1)
+        make_h(0, 1)
+        make_h(1, 1)
+        add_pass(1, 0)
+        add_pass(2, 0)
+        store(0)
+        make_h(2, 1, quantise_cols=BLOCK)
+        for g in range(PASSES):
+            add_pass(g, 1)
+        store(1)

@@ -64,19 +64,18 @@ def tile_list_keyword_campaign_values_kernel(
         nc.sync.dma_start(key_list[:], offs)
         for q in range(QUADRANTS):
             queue = nc.scalar if q < QUADRANTS // 2 else nc.sync
-            queue.dma_start(user_table_scales[32 * q : 32 * q + 4, :], tab2_scales[0, 4 * q : 4 * q + 4, :].bitcast(I32))
+            queue.dma_start(user_table_scales[q:P:32, :], tab2_scales[0, q:16:4, :].bitcast(I32))
         nc.sync.dma_start(user_table[:], tab2_words[0].rearrange("p t i -> p (t i)").bitcast(I32))
         for q in range(QUADRANTS):
-            row = 32 * q + KEY_SCALE_ROW
-            nc.sync.dma_start(key_table_scales[row : row + 4, :], tab_scales[0, 4 * q : 4 * q + 4, :].bitcast(I32))
+            nc.sync.dma_start(key_table_scales[KEY_SCALE_ROW + q : P : 32, :], tab_scales[0, q:16:4, :].bitcast(I32))
         load_wd(0)
         nc.sync.dma_start(key_table[:], tab_words[0].rearrange("p t i -> p (t i)").bitcast(I32))
         nc.sync.dma_start(bid_tile[:], bid.rearrange("(g p t) -> p g t", g=PASSES, t=PACK))
         load_wd(1)
         for q in range(QUADRANTS):
             nc.sync.dma_start(
-                w4_scale_tile[32 * q : 32 * q + 4, :, :],
-                w4_scales[:, 4 * q : 4 * q + 4, :].rearrange("g r c -> r g c").bitcast(I32),
+                w4_scale_tile[q:P:32, :, :],
+                w4_scales[:, q:16:4, :].rearrange("g r c -> r g c").bitcast(I32),
             )
         nc.sync.dma_start(w4_codes[:].bitcast(I32), w4_words.rearrange("g p c -> p g c").bitcast(I32))
         load_wd(2)

@@ -26,8 +26,9 @@ HALF = 512
 BLOCK = 256
 N_TILES = N // P
 KEY_SCALE_ROW = 4
+SILU_BUFS = 5
+H_BUFS = 3
 CAST_COLS = 128
-CAST_ON_VECTOR = (2, 0)
 
 
 def tile_list_keyword_campaign_values_kernel(
@@ -50,11 +51,14 @@ def tile_list_keyword_campaign_values_kernel(
         w4_scale_tile = keep.tile([P, PASSES, N // 4], I32, name="w4_scale_tile", align_bytes=64)
         bid_tile = keep.tile([P, PASSES, PACK], F32, name="bid_tile", align_bytes=64)
         bias_tile = keep.tile([P, N_TILES], F32, name="bias_tile")
-        wd_raw = [keep.tile([P, PACK, N], F32, name="wd_raw%d" % g) for g in range(PASSES)]
+        wd_raw = {}
 
-        def load_wd(g):
-            rows = wd[PASS * g : PASS * (g + 1), :]
-            nc.sync.dma_start(wd_raw[g][:], rows.rearrange("(p t) n -> p t n", t=PACK))
+        def load_wd(g, n0=0, width=N):
+            raw = keep.tile([P, PACK, width], F32, name="wd_raw%d_%d" % (g, n0))
+            for n in range(0, width, CAST_COLS):
+                wd_raw[g, n0 + n] = raw[:, :, n : n + CAST_COLS]
+            rows = wd[PASS * g : PASS * (g + 1), n0 : n0 + width]
+            nc.sync.dma_start(raw[:], rows.rearrange("(p t) n -> p t n", t=PACK))
 
         nc.vector.memset(user_table_scales[:], 0)
         nc.vector.memset(key_table_scales[:], 0)
@@ -62,21 +66,24 @@ def tile_list_keyword_campaign_values_kernel(
 
         nc.sync.dma_start(user_list[:], offs2)
         nc.sync.dma_start(key_list[:], offs)
-        for q in range(QUADRANTS):
-            queue = nc.scalar if q < QUADRANTS // 2 else nc.sync
-            queue.dma_start(user_table_scales[q:P:32, :], tab2_scales[0, q:16:4, :].bitcast(I32))
+        nc.scalar.dma_start(user_table_scales[0:P:32, :], tab2_scales[0, 0:16:4, :].bitcast(I32))
+        nc.scalar.dma_start(user_table_scales[1:P:32, :], tab2_scales[0, 1:16:4, :].bitcast(I32))
+        nc.sync.dma_start(user_table_scales[2:P:32, :], tab2_scales[0, 2:16:4, :].bitcast(I32))
+        nc.sync.dma_start(user_table_scales[3:P:32, :], tab2_scales[0, 3:16:4, :].bitcast(I32))
         nc.sync.dma_start(user_table[:], tab2_words[0].rearrange("p t i -> p (t i)").bitcast(I32))
-        for q in range(QUADRANTS):
-            nc.sync.dma_start(key_table_scales[KEY_SCALE_ROW + q : P : 32, :], tab_scales[0, q:16:4, :].bitcast(I32))
+        nc.sync.dma_start(key_table_scales[KEY_SCALE_ROW + 0 : P : 32, :], tab_scales[0, 0:16:4, :].bitcast(I32))
+        nc.sync.dma_start(key_table_scales[KEY_SCALE_ROW + 1 : P : 32, :], tab_scales[0, 1:16:4, :].bitcast(I32))
+        nc.sync.dma_start(key_table_scales[KEY_SCALE_ROW + 2 : P : 32, :], tab_scales[0, 2:16:4, :].bitcast(I32))
+        nc.sync.dma_start(key_table_scales[KEY_SCALE_ROW + 3 : P : 32, :], tab_scales[0, 3:16:4, :].bitcast(I32))
         load_wd(0)
         nc.sync.dma_start(key_table[:], tab_words[0].rearrange("p t i -> p (t i)").bitcast(I32))
+        load_wd(1, 0, N // 2)
         nc.sync.dma_start(bid_tile[:], bid.rearrange("(g p t) -> p g t", g=PASSES, t=PACK))
-        load_wd(1)
-        for q in range(QUADRANTS):
-            nc.sync.dma_start(
-                w4_scale_tile[q:P:32, :, :],
-                w4_scales[:, q:16:4, :].rearrange("g r c -> r g c").bitcast(I32),
-            )
+        load_wd(1, N // 2, N // 2)
+        nc.sync.dma_start(w4_scale_tile[0:P:32, :, :], w4_scales[:, 0:16:4, :].rearrange("g r c -> r g c").bitcast(I32))
+        nc.sync.dma_start(w4_scale_tile[1:P:32, :, :], w4_scales[:, 1:16:4, :].rearrange("g r c -> r g c").bitcast(I32))
+        nc.sync.dma_start(w4_scale_tile[2:P:32, :, :], w4_scales[:, 2:16:4, :].rearrange("g r c -> r g c").bitcast(I32))
+        nc.sync.dma_start(w4_scale_tile[3:P:32, :, :], w4_scales[:, 3:16:4, :].rearrange("g r c -> r g c").bitcast(I32))
         nc.sync.dma_start(w4_codes[:].bitcast(I32), w4_words.rearrange("g p c -> p g c").bitcast(I32))
         load_wd(2)
         with nc.allow_non_contiguous_dma(reason="one bias value to a partition and campaign tile"):
@@ -84,13 +91,20 @@ def tile_list_keyword_campaign_values_kernel(
 
         user_scales = keep.tile([P, S2], U8, name="user_scales", align_bytes=64)
         key_scales = keep.tile([P, S], U8, name="key_scales", align_bytes=64)
+        added = []
         user_words, key_words, wd_codes, wd_scales, h_codes, h_scales, sums = {}, {}, {}, {}, {}, {}, {}
 
-        def gather_user_words(half):
-            name = "user_words%d" % half
-            user_words[half] = keep.tile([P, HALF], U32, name=name, tag=name, align_bytes=64)
-            entries = user_list[:, LIST_COLS * half : LIST_COLS * (half + 1)]
-            nc.vector.tensor_copy(user_words[half][:], user_table[:].bitcast(U32).indirect(entries))
+        def gather_user_scales(j0, width):
+            entries = user_list[:, j0 // 16 : (j0 + width) // 16]
+            nc.vector.tensor_copy(user_scales[:, j0 : j0 + width], user_table_scales[:].bitcast(U8).indirect(entries))
+
+        def gather_user_words(j0, width):
+            name = "user_words%d" % j0
+            words = keep.tile([P, width], U32, name=name, tag=name, align_bytes=64)
+            for j in range(0, width, P):
+                user_words[j0 + j] = words[:, j:width]
+            entries = user_list[:, j0 // 16 : (j0 + width) // 16]
+            nc.vector.tensor_copy(words[:], user_table[:].bitcast(U32).indirect(entries))
 
         def gather_key_scales(g0, g1):
             in_order = keep.tile([P, PASS * (g1 - g0)], U8, name="key_scales_in_order%d" % g0, align_bytes=64)
@@ -108,12 +122,12 @@ def tile_list_keyword_campaign_values_kernel(
                 key_words[g][:].rearrange("p (t m) -> p m t", t=PACK), key_table[:].bitcast(U32).indirect(entries)
             )
 
-        def quantise_wd(g):
+        def quantise_wd(g, on_vector=()):
             rounded = ring.tile([P, N, PACK], BF16, name="wd_rounded", align_bytes=64)
             for n0 in range(0, N, CAST_COLS):
                 dst = rounded[:, n0 : n0 + CAST_COLS, :].rearrange("p (c i) t -> p c t i", i=4)
-                src = wd_raw[g][:, :, n0 : n0 + CAST_COLS].rearrange("p t (c i) -> p c t i", i=4)
-                if (g, n0) == CAST_ON_VECTOR:
+                src = wd_raw[g, n0].rearrange("p t (c i) -> p c t i", i=4)
+                if n0 // CAST_COLS in on_vector:
                     nc.vector.tensor_copy(dst, src)
                 else:
                     nc.scalar.copy(dst, src)
@@ -123,97 +137,150 @@ def tile_list_keyword_campaign_values_kernel(
                 out=wd_codes[g][:].bitcast(FP8X4), scales=wd_scales[g][:], in_=rounded[:].rearrange("p n t -> p (n t)")
             )
 
-        def make_h(g, half, second_silu_tag="silu", quantise_cols=HALF):
-            h_rounded = ring.tile([P, HALF, 2, 2], BF16, name="h_rounded", align_bytes=64)
-            for j0 in range(0, HALF, BLOCK):
-                if j0 == 0 or second_silu_tag == "silu":
-                    silu = ring.tile([P, 2, BLOCK, 2], F32, name="silu", align_bytes=64, bufs=5)
+        def make_h(g, c0, width, block=BLOCK, quantise_cols=None, lent=None):
+            quantise_cols = quantise_cols or width
+            per_bank = HALF // block
+            banks = PACK // per_bank
+            h_rounded = ring.tile([P, width, banks, per_bank], BF16, name="h_rounded", align_bytes=64, bufs=H_BUFS)
+            h_codes[g, c0] = keep.tile([P, width], U32, name="h_codes%d_%d" % (g, c0), align_bytes=64)
+            h_scales[g, c0] = keep.tile([P, width], U8, name="h_scales%d_%d" % (g, c0), align_bytes=64)
+            for j0 in range(0, width, block):
+                if lent and j0 + block == width:
+                    silu = keep.tile([P, banks, block, per_bank], F32, name="silu_lent", tag=lent, align_bytes=64)
                 else:
-                    silu = keep.tile([P, 2, BLOCK, 2], F32, name="silu_lent", tag=second_silu_tag, align_bytes=64)
-                users = slice(HALF * half + j0, HALF * half + j0 + BLOCK)
-                for u in range(2):
-                    scores = score_banks.tile([P, 2, BLOCK], F32, name="scores")
-                    for e in range(2):
-                        m0 = P * (2 * u + e)
+                    silu = ring.tile([P, banks, block, per_bank], F32, name="silu", align_bytes=64, bufs=SILU_BUFS)
+                users = slice(c0 + j0, c0 + j0 + block)
+                for u in range(banks):
+                    scores = score_banks.tile([P, per_bank, block], F32, name="scores")
+                    for e in range(per_bank):
+                        m0 = P * (per_bank * u + e)
                         nc.tensor.matmul_mx(
                             out=scores[:, e, :],
                             lhsT=key_words[g][:, m0 : m0 + P].bitcast(FP8X4),
                             lhsT_scale=key_scales[KEY_SCALE_ROW:P, PASS * g + m0 : PASS * g + m0 + P],
-                            rhs=user_words[half][:, j0 : j0 + BLOCK].bitcast(FP8X4),
+                            rhs=user_words[c0 + j0][:, 0:block].bitcast(FP8X4),
                             rhs_scale=user_scales[:, users],
                             start=True,
                             stop=True,
                         )
                     nc.scalar.activation(silu[:, u, :, :], scores[:].rearrange("p e n -> p n e"), ACT.Silu)
                 nc.vector.tensor_tensor(
-                    h_rounded[:, j0 : j0 + BLOCK, :, :],
+                    h_rounded[:, j0 : j0 + block, :, :],
                     silu[:].rearrange("p u n e -> p n u e"),
-                    bid_tile[:, g, :].rearrange("p (u e) -> p u e", u=2).unsqueeze(1).to_broadcast([P, BLOCK, 2, 2]),
+                    bid_tile[:, g, :].rearrange("p (u e) -> p u e", u=banks).unsqueeze(1).to_broadcast([P, block, banks, per_bank]),
                     ALU.mult,
                 )
-            h_codes[g, half] = keep.tile([P, HALF], U32, name="h_codes%d%d" % (g, half), align_bytes=64)
-            h_scales[g, half] = keep.tile([P, HALF], U8, name="h_scales%d%d" % (g, half), align_bytes=64)
-            for j0 in range(0, HALF, quantise_cols):
-                nc.vector.quantize_mx(
-                    out=h_codes[g, half][:, j0 : j0 + quantise_cols].bitcast(FP8X4),
-                    scales=h_scales[g, half][:, j0 : j0 + quantise_cols],
-                    in_=h_rounded[:, j0 : j0 + quantise_cols, :, :].rearrange("p n u e -> p (n u e)"),
-                )
+                if (j0 + block) % quantise_cols == 0:
+                    q0 = j0 + block - quantise_cols
+                    nc.vector.quantize_mx(
+                        out=h_codes[g, c0][:, q0 : q0 + quantise_cols].bitcast(FP8X4),
+                        scales=h_scales[g, c0][:, q0 : q0 + quantise_cols],
+                        in_=h_rounded[:, q0 : q0 + quantise_cols, :, :].rearrange("p n u e -> p (n u e)"),
+                    )
 
-        def add_pass(g, half):
-            if g == 0:
-                sums[half] = [value_banks.tile([P, HALF], F32, name="values%d" % c) for c in range(N_TILES)]
+        def add_pass(kind, g, c0, j0, width, bank0, s0=0, sw=None):
+            per_bank = HALF // width
+            first = c0 + j0 not in sums
+            if first:
+                sums[c0 + j0] = [
+                    value_banks.tile([P, per_bank, width], F32, name="values%d" % (bank0 + k)) for k in range(N_TILES // per_bank)
+                ]
+            sw = sw or width
+            added.extend([c0 + j0] * (sw // P))
+            last = added.count(c0 + j0) == 2 * PASSES * width // P
+            cols_a_pass = P if kind == "w4" and sw != HALF else sw
             for c in range(N_TILES):
+                acc = sums[c0 + j0][c // per_bank][:, c % per_bank, :]
                 campaigns = slice(P * c, P * (c + 1))
+                if kind == "w4":
+                    codes = w4_codes[:, g, 2 * P * c : 2 * P * (c + 1)].bitcast(FP4X4)
+                    scales = w4_scale_tile[:, g, :].bitcast(U8)[:, campaigns]
+                else:
+                    codes, scales = wd_codes[g][:, campaigns].bitcast(FP8X4), wd_scales[g][:, campaigns]
+                for n0 in range(s0, s0 + sw, cols_a_pass):
+                    cols = slice(j0 + n0, j0 + n0 + cols_a_pass)
+                    nc.tensor.matmul_mx(
+                        out=acc[:, n0 : n0 + cols_a_pass],
+                        lhsT=codes,
+                        lhsT_scale=scales,
+                        rhs=h_codes[g, c0][:, cols].bitcast(FP8X4),
+                        rhs_scale=h_scales[g, c0][:, cols],
+                        start=(first and c % per_bank == 0 and n0 == s0),
+                        stop=(last and c % per_bank == per_bank - 1 and n0 + cols_a_pass == s0 + sw),
+                    )
+
+        def add_both(g, c0, j0, width, bank0):
+            per_bank = HALF // width
+            cols_a_pass = P if width != HALF else width
+            added.extend([c0 + j0] * (2 * width // P))
+            last = added.count(c0 + j0) == 2 * PASSES * width // P
+            first = c0 + j0 not in sums
+            if first:
+                sums[c0 + j0] = [
+                    value_banks.tile([P, per_bank, width], F32, name="values%d" % (bank0 + k)) for k in range(N_TILES // per_bank)
+                ]
+            for c in range(N_TILES):
+                acc = sums[c0 + j0][c // per_bank][:, c % per_bank, :]
+                campaigns = slice(P * c, P * (c + 1))
+                for n0 in range(0, width, cols_a_pass):
+                    cols = slice(j0 + n0, j0 + n0 + cols_a_pass)
+                    nc.tensor.matmul_mx(
+                        out=acc[:, n0 : n0 + cols_a_pass],
+                        lhsT=w4_codes[:, g, 2 * P * c : 2 * P * (c + 1)].bitcast(FP4X4),
+                        lhsT_scale=w4_scale_tile[:, g, :].bitcast(U8)[:, campaigns],
+                        rhs=h_codes[g, c0][:, cols].bitcast(FP8X4),
+                        rhs_scale=h_scales[g, c0][:, cols],
+                        start=(first and c % per_bank == 0 and n0 == 0),
+                        stop=False,
+                    )
                 nc.tensor.matmul_mx(
-                    out=sums[half][c][:],
-                    lhsT=w4_codes[:, g, 2 * P * c : 2 * P * (c + 1)].bitcast(FP4X4),
-                    lhsT_scale=w4_scale_tile[:, g, :].bitcast(U8)[:, campaigns],
-                    rhs=h_codes[g, half][:].bitcast(FP8X4),
-                    rhs_scale=h_scales[g, half][:],
-                    start=(g == 0),
-                    stop=False,
-                )
-                nc.tensor.matmul_mx(
-                    out=sums[half][c][:],
+                    out=acc,
                     lhsT=wd_codes[g][:, campaigns].bitcast(FP8X4),
                     lhsT_scale=wd_scales[g][:, campaigns],
-                    rhs=h_codes[g, half][:].bitcast(FP8X4),
-                    rhs_scale=h_scales[g, half][:],
+                    rhs=h_codes[g, c0][:, j0 : j0 + width].bitcast(FP8X4),
+                    rhs_scale=h_scales[g, c0][:, j0 : j0 + width],
                     start=False,
-                    stop=(g == PASSES - 1),
+                    stop=(last and c % per_bank == per_bank - 1),
                 )
 
-        def store(half):
-            for c in range(N_TILES):
-                result = ring.tile([P, HALF], F32, name="result", bufs=N_TILES)
-                if half == 0 or c % 2 == 0:
-                    nc.scalar.activation(result[:], sums[half][c][:], ACT.Identity, bias=bias_tile[:, c : c + 1])
+        def store(j0, width, on_vector=()):
+            per_bank = HALF // width
+            for k in range(N_TILES // per_bank):
+                result = ring.tile([P, per_bank, width], F32, name="result", bufs=N_TILES)
+                c0 = per_bank * k
+                if k not in on_vector:
+                    for e in range(per_bank):
+                        nc.scalar.activation(result[:, e, :], sums[j0][k][:, e, :], ACT.Identity, bias=bias_tile[:, c0 + e : c0 + e + 1])
+                elif per_bank == 1:
+                    nc.vector.tensor_scalar(result[:, 0, :], sums[j0][k][:, 0, :], bias_tile[:, c0 : c0 + 1], None, ALU.add)
                 else:
-                    nc.vector.tensor_scalar(result[:], sums[half][c][:], bias_tile[:, c : c + 1], None, ALU.add)
-                nc.sync.dma_start(out[P * c : P * (c + 1), HALF * half : HALF * (half + 1)], result[:])
+                    bias = bias_tile[:, c0 : c0 + per_bank].unsqueeze(2).to_broadcast([P, per_bank, width])
+                    nc.vector.tensor_tensor(result[:], sums[j0][k][:], bias, ALU.add)
+                rows = out[P * c0 : P * (c0 + per_bank), j0 : j0 + width]
+                nc.sync.dma_start(rows.rearrange("(c p) j -> p c j", p=P), result[:])
 
-        nc.vector.tensor_copy(user_scales[:], user_table_scales[:].bitcast(U8).indirect(user_list[:]))
-        gather_user_words(0)
+        gather_user_scales(0, 1024)
+        gather_user_words(0, 512)
         gather_key_scales(0, 1)
         gather_key_words(0)
-        make_h(0, 0, second_silu_tag="user_words1")
-        gather_key_scales(1, PASSES)
+        make_h(0, 0, 512)
+        gather_key_scales(1, 3)
         gather_key_words(1)
-        make_h(1, 0)
-        quantise_wd(0)
-        quantise_wd(1)
-        add_pass(0, 0)
+        make_h(1, 0, 512)
+        quantise_wd(0, ())
+        quantise_wd(1, ())
+        add_both(0, 0, 0, 512, 0)
         gather_key_words(2)
-        make_h(2, 0)
-        quantise_wd(2)
-        gather_user_words(1)
-        make_h(0, 1)
-        make_h(1, 1)
-        add_pass(1, 0)
-        add_pass(2, 0)
-        store(0)
-        make_h(2, 1, quantise_cols=BLOCK)
-        for g in range(PASSES):
-            add_pass(g, 1)
-        store(1)
+        make_h(2, 0, 512)
+        quantise_wd(2, (0,))
+        gather_user_words(512, 512)
+        make_h(0, 512, 512)
+        make_h(1, 512, 512)
+        add_both(1, 0, 0, 512, 0)
+        add_both(2, 0, 0, 512, 0)
+        store(0, 512, (3,))
+        make_h(2, 512, 512, block=256, quantise_cols=256)
+        add_both(0, 512, 0, 512, 0)
+        add_both(1, 512, 0, 512, 0)
+        add_both(2, 512, 0, 512, 0)
+        store(512, 512, (1, 3,))

@@ -28,6 +28,7 @@ N_TILES = N // P
 KEY_SCALE_ROW = 4
 SILU_BUFS = 5
 H_BUFS = 3
+SILU_BYTES = 4096
 CAST_COLS = 128
 
 
@@ -37,6 +38,7 @@ def tile_list_keyword_campaign_values_kernel(
     nc = tc.nc
     with ExitStack() as ctx:
         keep = ctx.enter_context(tc.tile_pool(name="keep", bufs=1))
+        shared = ctx.enter_context(tc.tile_pool(name="shared", bufs=1))
         ring = ctx.enter_context(tc.tile_pool(name="ring", bufs=3))
         score_banks = ctx.enter_context(tc.psum_pool(name="score_banks", bufs=4))
         value_banks = ctx.enter_context(tc.psum_pool(name="value_banks", bufs=1))
@@ -53,8 +55,11 @@ def tile_list_keyword_campaign_values_kernel(
         bias_tile = keep.tile([P, N_TILES], F32, name="bias_tile")
         wd_raw = {}
 
-        def load_wd(g, n0=0, width=N):
-            raw = keep.tile([P, PACK, width], F32, name="wd_raw%d_%d" % (g, n0))
+        def load_wd(g, n0=0, width=N, under_silu=False):
+            if under_silu:
+                raw = shared.tile([P, PACK, width], F32, name="wd_raw_early", offset=SILU_BYTES - 8 * width)
+            else:
+                raw = keep.tile([P, PACK, width], F32, name="wd_raw%d_%d" % (g, n0))
             for n in range(0, width, CAST_COLS):
                 wd_raw[g, n0 + n] = raw[:, :, n : n + CAST_COLS]
             rows = wd[PASS * g : PASS * (g + 1), n0 : n0 + width]
@@ -63,6 +68,9 @@ def tile_list_keyword_campaign_values_kernel(
         nc.vector.memset(user_table_scales[:], 0)
         nc.vector.memset(key_table_scales[:], 0)
         nc.vector.memset(w4_scale_tile[:], 0)
+        warm_up = keep.tile([P, 2], F32, name="warm_up")
+        nc.vector.memset(warm_up[:, 0:1], 0.0)
+        nc.scalar.activation(warm_up[:, 1:2], warm_up[:, 0:1], ACT.Silu)
 
         nc.sync.dma_start(user_list[:], offs2)
         nc.sync.dma_start(key_list[:], offs)
@@ -77,14 +85,14 @@ def tile_list_keyword_campaign_values_kernel(
         nc.sync.dma_start(key_table_scales[KEY_SCALE_ROW + 3 : P : 32, :], tab_scales[0, 3:16:4, :].bitcast(I32))
         load_wd(0)
         nc.sync.dma_start(key_table[:], tab_words[0].rearrange("p t i -> p (t i)").bitcast(I32))
-        load_wd(1, 0, N // 2)
+        load_wd(1, 0, 256, under_silu=True)
         nc.sync.dma_start(bid_tile[:], bid.rearrange("(g p t) -> p g t", g=PASSES, t=PACK))
-        load_wd(1, N // 2, N // 2)
         nc.sync.dma_start(w4_scale_tile[0:P:32, :, :], w4_scales[:, 0:16:4, :].rearrange("g r c -> r g c").bitcast(I32))
         nc.sync.dma_start(w4_scale_tile[1:P:32, :, :], w4_scales[:, 1:16:4, :].rearrange("g r c -> r g c").bitcast(I32))
         nc.sync.dma_start(w4_scale_tile[2:P:32, :, :], w4_scales[:, 2:16:4, :].rearrange("g r c -> r g c").bitcast(I32))
         nc.sync.dma_start(w4_scale_tile[3:P:32, :, :], w4_scales[:, 3:16:4, :].rearrange("g r c -> r g c").bitcast(I32))
         nc.sync.dma_start(w4_codes[:].bitcast(I32), w4_words.rearrange("g p c -> p g c").bitcast(I32))
+        load_wd(1, 256, 256)
         load_wd(2)
         with nc.allow_non_contiguous_dma(reason="one bias value to a partition and campaign tile"):
             nc.sync.dma_start(bias_tile[:], b.rearrange("(c p) -> p c", p=P))
@@ -92,6 +100,7 @@ def tile_list_keyword_campaign_values_kernel(
         user_scales = keep.tile([P, S2], U8, name="user_scales", align_bytes=64)
         key_scales = keep.tile([P, S], U8, name="key_scales", align_bytes=64)
         added = []
+        wd_rounded = {}
         user_words, key_words, wd_codes, wd_scales, h_codes, h_scales, sums = {}, {}, {}, {}, {}, {}, {}
 
         def gather_user_scales(j0, width):
@@ -122,19 +131,23 @@ def tile_list_keyword_campaign_values_kernel(
                 key_words[g][:].rearrange("p (t m) -> p m t", t=PACK), key_table[:].bitcast(U32).indirect(entries)
             )
 
-        def quantise_wd(g, on_vector=()):
-            rounded = ring.tile([P, N, PACK], BF16, name="wd_rounded", align_bytes=64)
-            for n0 in range(0, N, CAST_COLS):
-                dst = rounded[:, n0 : n0 + CAST_COLS, :].rearrange("p (c i) t -> p c t i", i=4)
+        def round_wd(g, quarters, on_vector=()):
+            if g not in wd_rounded:
+                wd_rounded[g] = ring.tile([P, N, PACK], BF16, name="wd_rounded", align_bytes=64)
+            for k in quarters:
+                n0 = CAST_COLS * k
+                dst = wd_rounded[g][:, n0 : n0 + CAST_COLS, :].rearrange("p (c i) t -> p c t i", i=4)
                 src = wd_raw[g, n0].rearrange("p t (c i) -> p c t i", i=4)
-                if n0 // CAST_COLS in on_vector:
+                if k in on_vector:
                     nc.vector.tensor_copy(dst, src)
                 else:
                     nc.scalar.copy(dst, src)
+
+        def quantise_wd(g):
             wd_codes[g] = keep.tile([P, N], U32, name="wd_codes%d" % g, align_bytes=64)
             wd_scales[g] = keep.tile([P, N], U8, name="wd_scales%d" % g, align_bytes=64)
             nc.vector.quantize_mx(
-                out=wd_codes[g][:].bitcast(FP8X4), scales=wd_scales[g][:], in_=rounded[:].rearrange("p n t -> p (n t)")
+                out=wd_codes[g][:].bitcast(FP8X4), scales=wd_scales[g][:], in_=wd_rounded[g][:].rearrange("p n t -> p (n t)")
             )
 
         def make_h(g, c0, width, block=BLOCK, quantise_cols=None, lent=None):
@@ -145,7 +158,9 @@ def tile_list_keyword_campaign_values_kernel(
             h_codes[g, c0] = keep.tile([P, width], U32, name="h_codes%d_%d" % (g, c0), align_bytes=64)
             h_scales[g, c0] = keep.tile([P, width], U8, name="h_scales%d_%d" % (g, c0), align_bytes=64)
             for j0 in range(0, width, block):
-                if lent and j0 + block == width:
+                if lent == "shared":
+                    silu = shared.tile([P, banks, block, per_bank], F32, name="silu_first%d" % j0, offset=SILU_BYTES * (j0 // block))
+                elif lent and j0 == width - block:
                     silu = keep.tile([P, banks, block, per_bank], F32, name="silu_lent", tag=lent, align_bytes=64)
                 else:
                     silu = ring.tile([P, banks, block, per_bank], F32, name="silu", align_bytes=64, bufs=SILU_BUFS)
@@ -263,16 +278,20 @@ def tile_list_keyword_campaign_values_kernel(
         gather_user_words(0, 512)
         gather_key_scales(0, 1)
         gather_key_words(0)
-        make_h(0, 0, 512)
+        round_wd(0, (0, 1, 2, 3,))
+        quantise_wd(0)
+        round_wd(1, (0, 1,))
+        make_h(0, 0, 512, block=256, quantise_cols=512, lent="shared")
         gather_key_scales(1, 3)
         gather_key_words(1)
         make_h(1, 0, 512)
-        quantise_wd(0, ())
-        quantise_wd(1, ())
+        round_wd(1, (2, 3,))
+        quantise_wd(1)
         add_both(0, 0, 0, 512, 0)
         gather_key_words(2)
         make_h(2, 0, 512)
-        quantise_wd(2, (0,))
+        round_wd(2, (0, 1, 2, 3,), (0,))
+        quantise_wd(2)
         gather_user_words(512, 512)
         make_h(0, 512, 512)
         make_h(1, 512, 512)

@@ -57,7 +57,7 @@ def tile_list_keyword_campaign_values_kernel(
 
         def load_wd(g, n0=0, width=N, under_silu=False):
             if under_silu:
-                raw = shared.tile([P, PACK, width], F32, name="wd_raw_early", offset=SILU_BYTES - 8 * width)
+                raw = shared.tile([P, PACK, width], F32, name="wd_raw_early", offset=SILU_BYTES - 4 * width)
             else:
                 raw = keep.tile([P, PACK, width], F32, name="wd_raw%d_%d" % (g, n0))
             for n in range(0, width, CAST_COLS):
@@ -144,13 +144,16 @@ def tile_list_keyword_campaign_values_kernel(
                     nc.scalar.copy(dst, src)
 
         def quantise_wd(g):
-            wd_codes[g] = keep.tile([P, N], U32, name="wd_codes%d" % g, align_bytes=64)
+            if g == 0:
+                wd_codes[g] = shared.tile([P, N], U32, name="wd_codes0", align_bytes=64, offset=SILU_BYTES)
+            else:
+                wd_codes[g] = keep.tile([P, N], U32, name="wd_codes%d" % g, align_bytes=64)
             wd_scales[g] = keep.tile([P, N], U8, name="wd_scales%d" % g, align_bytes=64)
             nc.vector.quantize_mx(
                 out=wd_codes[g][:].bitcast(FP8X4), scales=wd_scales[g][:], in_=wd_rounded[g][:].rearrange("p n t -> p (n t)")
             )
 
-        def make_h(g, c0, width, block=BLOCK, quantise_cols=None, lent=None):
+        def make_h(g, c0, width, block=BLOCK, quantise_cols=None, lent=None, product_cols=None):
             quantise_cols = quantise_cols or width
             per_bank = HALF // block
             banks = PACK // per_bank
@@ -159,7 +162,7 @@ def tile_list_keyword_campaign_values_kernel(
             h_scales[g, c0] = keep.tile([P, width], U8, name="h_scales%d_%d" % (g, c0), align_bytes=64)
             for j0 in range(0, width, block):
                 if lent == "shared":
-                    silu = shared.tile([P, banks, block, per_bank], F32, name="silu_first%d" % j0, offset=SILU_BYTES * (j0 // block))
+                    silu = shared.tile([P, banks, block, per_bank], F32, name="silu_first%d" % j0, offset=(SILU_BYTES + 4 * N) * (j0 // block))
                 elif lent and j0 == width - block:
                     silu = keep.tile([P, banks, block, per_bank], F32, name="silu_lent", tag=lent, align_bytes=64)
                 else:
@@ -179,19 +182,22 @@ def tile_list_keyword_campaign_values_kernel(
                             stop=True,
                         )
                     nc.scalar.activation(silu[:, u, :, :], scores[:].rearrange("p e n -> p n e"), ACT.Silu)
-                nc.vector.tensor_tensor(
-                    h_rounded[:, j0 : j0 + block, :, :],
-                    silu[:].rearrange("p u n e -> p n u e"),
-                    bid_tile[:, g, :].rearrange("p (u e) -> p u e", u=banks).unsqueeze(1).to_broadcast([P, block, banks, per_bank]),
-                    ALU.mult,
-                )
-                if (j0 + block) % quantise_cols == 0:
-                    q0 = j0 + block - quantise_cols
-                    nc.vector.quantize_mx(
-                        out=h_codes[g, c0][:, q0 : q0 + quantise_cols].bitcast(FP8X4),
-                        scales=h_scales[g, c0][:, q0 : q0 + quantise_cols],
-                        in_=h_rounded[:, q0 : q0 + quantise_cols, :, :].rearrange("p n u e -> p (n u e)"),
+                step = product_cols or block
+                bids = bid_tile[:, g, :].rearrange("p (u e) -> p u e", u=banks).unsqueeze(1)
+                for s0 in range(0, block, step):
+                    nc.vector.tensor_tensor(
+                        h_rounded[:, j0 + s0 : j0 + s0 + step, :, :],
+                        silu[:, :, s0 : s0 + step, :].rearrange("p u n e -> p n u e"),
+                        bids.to_broadcast([P, step, banks, per_bank]),
+                        ALU.mult,
                     )
+                    if (j0 + s0 + step) % quantise_cols == 0:
+                        q0 = j0 + s0 + step - quantise_cols
+                        nc.vector.quantize_mx(
+                            out=h_codes[g, c0][:, q0 : q0 + quantise_cols].bitcast(FP8X4),
+                            scales=h_scales[g, c0][:, q0 : q0 + quantise_cols],
+                            in_=h_rounded[:, q0 : q0 + quantise_cols, :, :].rearrange("p n u e -> p (n u e)"),
+                        )
 
         def add_pass(kind, g, c0, j0, width, bank0, s0=0, sw=None):
             per_bank = HALF // width
@@ -281,25 +287,30 @@ def tile_list_keyword_campaign_values_kernel(
         round_wd(0, (0, 1, 2, 3,))
         quantise_wd(0)
         round_wd(1, (0, 1,))
-        make_h(0, 0, 512, block=256, quantise_cols=512, lent="shared")
+        make_h(0, 0, 512, block=256, quantise_cols=256, lent="shared")
         gather_key_scales(1, 3)
         gather_key_words(1)
-        make_h(1, 0, 512)
+        make_h(1, 0, 512, block=256, quantise_cols=256)
         round_wd(1, (2, 3,))
         quantise_wd(1)
         add_both(0, 0, 0, 512, 0)
         gather_key_words(2)
-        make_h(2, 0, 512)
+        make_h(2, 0, 512, block=256, quantise_cols=256)
         round_wd(2, (0, 1, 2, 3,), (0,))
         quantise_wd(2)
         gather_user_words(512, 512)
-        make_h(0, 512, 512)
-        make_h(1, 512, 512)
+        make_h(0, 512, 512, block=256, quantise_cols=256)
+        make_h(1, 512, 512, block=256, quantise_cols=256)
         add_both(1, 0, 0, 512, 0)
         add_both(2, 0, 0, 512, 0)
-        store(0, 512, (3,))
-        make_h(2, 512, 512, block=256, quantise_cols=256)
-        add_both(0, 512, 0, 512, 0)
-        add_both(1, 512, 0, 512, 0)
-        add_both(2, 512, 0, 512, 0)
-        store(512, 512, (1, 3,))
+        store(0, 512, ())
+        make_h(2, 512, 256)
+        make_h(2, 768, 256, block=256, quantise_cols=128, product_cols=128)
+        add_both(0, 512, 0, 256, 0)
+        add_both(0, 512, 256, 256, 2)
+        add_both(1, 512, 0, 256, 0)
+        add_both(1, 512, 256, 256, 2)
+        add_both(2, 512, 0, 256, 0)
+        store(512, 256, (1,))
+        add_both(2, 768, 0, 256, 2)
+        store(768, 256, (1,))

@@ -21,15 +21,16 @@ PACK = 4
 PASS = P * PACK
 PASSES = S // PASS
 LIST_COLS = PASS // 16
-QUADRANTS = 4
-HALF = 512
-BLOCK = 256
+QUADRANT = 32
+ROWS = 4
+BANK = 512
+HALF = S2 // 2
+GROUP = 256
 N_TILES = N // P
 KEY_SCALE_ROW = 4
+QUARTER = N // 4
 SILU_BUFS = 5
-H_BUFS = 3
-SILU_BYTES = 4096
-CAST_COLS = 128
+SILU_BYTES = GROUP * PACK * 4
 
 
 def tile_list_keyword_campaign_values_kernel(
@@ -39,7 +40,7 @@ def tile_list_keyword_campaign_values_kernel(
     with ExitStack() as ctx:
         keep = ctx.enter_context(tc.tile_pool(name="keep", bufs=1))
         shared = ctx.enter_context(tc.tile_pool(name="shared", bufs=1))
-        ring = ctx.enter_context(tc.tile_pool(name="ring", bufs=3))
+        ring = ctx.enter_context(tc.tile_pool(name="ring", bufs=PASSES))
         score_banks = ctx.enter_context(tc.psum_pool(name="score_banks", bufs=4))
         value_banks = ctx.enter_context(tc.psum_pool(name="value_banks", bufs=1))
 
@@ -55,13 +56,13 @@ def tile_list_keyword_campaign_values_kernel(
         bias_tile = keep.tile([P, N_TILES], F32, name="bias_tile")
         wd_raw = {}
 
-        def load_wd(g, n0=0, width=N, under_silu=False):
+        def load_wd(g, n0, width, under_silu=False):
             if under_silu:
-                raw = shared.tile([P, PACK, width], F32, name="wd_raw_early", offset=SILU_BYTES - 4 * width)
+                raw = shared.tile([P, PACK, width], F32, name="wd_raw_early", offset=SILU_BYTES // 2)
             else:
                 raw = keep.tile([P, PACK, width], F32, name="wd_raw%d_%d" % (g, n0))
-            for n in range(0, width, CAST_COLS):
-                wd_raw[g, n0 + n] = raw[:, :, n : n + CAST_COLS]
+            for n in range(0, width, QUARTER):
+                wd_raw[g, n0 + n] = raw[:, :, n : n + QUARTER]
             rows = wd[PASS * g : PASS * (g + 1), n0 : n0 + width]
             nc.sync.dma_start(raw[:], rows.rearrange("(p t) n -> p t n", t=PACK))
 
@@ -74,45 +75,36 @@ def tile_list_keyword_campaign_values_kernel(
 
         nc.sync.dma_start(user_list[:], offs2)
         nc.sync.dma_start(key_list[:], offs)
-        nc.scalar.dma_start(user_table_scales[0:P:32, :], tab2_scales[0, 0:16:4, :].bitcast(I32))
-        nc.scalar.dma_start(user_table_scales[1:P:32, :], tab2_scales[0, 1:16:4, :].bitcast(I32))
-        nc.sync.dma_start(user_table_scales[2:P:32, :], tab2_scales[0, 2:16:4, :].bitcast(I32))
-        nc.sync.dma_start(user_table_scales[3:P:32, :], tab2_scales[0, 3:16:4, :].bitcast(I32))
+        for r in range(ROWS):
+            queue = nc.scalar if r < ROWS // 2 else nc.sync
+            queue.dma_start(user_table_scales[r:P:QUADRANT, :], tab2_scales[0, r:16:ROWS, :].bitcast(I32))
         nc.sync.dma_start(user_table[:], tab2_words[0].rearrange("p t i -> p (t i)").bitcast(I32))
-        nc.sync.dma_start(key_table_scales[KEY_SCALE_ROW + 0 : P : 32, :], tab_scales[0, 0:16:4, :].bitcast(I32))
-        nc.sync.dma_start(key_table_scales[KEY_SCALE_ROW + 1 : P : 32, :], tab_scales[0, 1:16:4, :].bitcast(I32))
-        nc.sync.dma_start(key_table_scales[KEY_SCALE_ROW + 2 : P : 32, :], tab_scales[0, 2:16:4, :].bitcast(I32))
-        nc.sync.dma_start(key_table_scales[KEY_SCALE_ROW + 3 : P : 32, :], tab_scales[0, 3:16:4, :].bitcast(I32))
-        load_wd(0)
+        for r in range(ROWS):
+            nc.sync.dma_start(key_table_scales[KEY_SCALE_ROW + r : P : QUADRANT, :], tab_scales[0, r:16:ROWS, :].bitcast(I32))
+        load_wd(0, 0, N)
         nc.sync.dma_start(key_table[:], tab_words[0].rearrange("p t i -> p (t i)").bitcast(I32))
-        load_wd(1, 0, 256, under_silu=True)
+        load_wd(1, 0, N // 2, under_silu=True)
         nc.sync.dma_start(bid_tile[:], bid.rearrange("(g p t) -> p g t", g=PASSES, t=PACK))
-        nc.sync.dma_start(w4_scale_tile[0:P:32, :, :], w4_scales[:, 0:16:4, :].rearrange("g r c -> r g c").bitcast(I32))
-        nc.sync.dma_start(w4_scale_tile[1:P:32, :, :], w4_scales[:, 1:16:4, :].rearrange("g r c -> r g c").bitcast(I32))
-        nc.sync.dma_start(w4_scale_tile[2:P:32, :, :], w4_scales[:, 2:16:4, :].rearrange("g r c -> r g c").bitcast(I32))
-        nc.sync.dma_start(w4_scale_tile[3:P:32, :, :], w4_scales[:, 3:16:4, :].rearrange("g r c -> r g c").bitcast(I32))
+        for r in range(ROWS):
+            nc.sync.dma_start(
+                w4_scale_tile[r:P:QUADRANT, :, :], w4_scales[:, r:16:ROWS, :].rearrange("g q c -> q g c").bitcast(I32)
+            )
         nc.sync.dma_start(w4_codes[:].bitcast(I32), w4_words.rearrange("g p c -> p g c").bitcast(I32))
-        load_wd(1, 256, 256)
-        load_wd(2)
+        load_wd(1, N // 2, N // 2)
+        load_wd(2, 0, N)
         with nc.allow_non_contiguous_dma(reason="one bias value to a partition and campaign tile"):
             nc.sync.dma_start(bias_tile[:], b.rearrange("(c p) -> p c", p=P))
 
         user_scales = keep.tile([P, S2], U8, name="user_scales", align_bytes=64)
         key_scales = keep.tile([P, S], U8, name="key_scales", align_bytes=64)
-        added = []
-        wd_rounded = {}
-        user_words, key_words, wd_codes, wd_scales, h_codes, h_scales, sums = {}, {}, {}, {}, {}, {}, {}
+        user_words, key_words, wd_rounded, wd_codes, wd_scales = {}, {}, {}, {}, {}
+        h_codes, h_scales, sums = {}, {}, {}
 
-        def gather_user_scales(j0, width):
-            entries = user_list[:, j0 // 16 : (j0 + width) // 16]
-            nc.vector.tensor_copy(user_scales[:, j0 : j0 + width], user_table_scales[:].bitcast(U8).indirect(entries))
-
-        def gather_user_words(j0, width):
-            name = "user_words%d" % j0
-            words = keep.tile([P, width], U32, name=name, tag=name, align_bytes=64)
-            for j in range(0, width, P):
-                user_words[j0 + j] = words[:, j:width]
-            entries = user_list[:, j0 // 16 : (j0 + width) // 16]
+        def gather_user_words(first_user):
+            words = keep.tile([P, HALF], U32, name="user_words%d" % first_user, align_bytes=64)
+            for j0 in range(0, HALF, GROUP):
+                user_words[first_user + j0] = words[:, j0 : j0 + GROUP]
+            entries = user_list[:, first_user // 16 : (first_user + HALF) // 16]
             nc.vector.tensor_copy(words[:], user_table[:].bitcast(U32).indirect(entries))
 
         def gather_key_scales(g0, g1):
@@ -131,186 +123,140 @@ def tile_list_keyword_campaign_values_kernel(
                 key_words[g][:].rearrange("p (t m) -> p m t", t=PACK), key_table[:].bitcast(U32).indirect(entries)
             )
 
-        def round_wd(g, quarters, on_vector=()):
+        def round_wd(g, n0, n1, copy):
             if g not in wd_rounded:
                 wd_rounded[g] = ring.tile([P, N, PACK], BF16, name="wd_rounded", align_bytes=64)
-            for k in quarters:
-                n0 = CAST_COLS * k
-                dst = wd_rounded[g][:, n0 : n0 + CAST_COLS, :].rearrange("p (c i) t -> p c t i", i=4)
-                src = wd_raw[g, n0].rearrange("p t (c i) -> p c t i", i=4)
-                if k in on_vector:
-                    nc.vector.tensor_copy(dst, src)
-                else:
-                    nc.scalar.copy(dst, src)
+            for n in range(n0, n1, QUARTER):
+                copy(
+                    wd_rounded[g][:, n : n + QUARTER, :].rearrange("p (c x) t -> p c t x", x=4),
+                    wd_raw[g, n].rearrange("p t (c x) -> p c t x", x=4),
+                )
 
         def quantise_wd(g):
-            if g == 0:
-                wd_codes[g] = shared.tile([P, N], U32, name="wd_codes0", align_bytes=64, offset=SILU_BYTES)
-            else:
-                wd_codes[g] = keep.tile([P, N], U32, name="wd_codes%d" % g, align_bytes=64)
+            wd_codes[g] = keep.tile([P, N], U32, name="wd_codes%d" % g, align_bytes=64)
             wd_scales[g] = keep.tile([P, N], U8, name="wd_scales%d" % g, align_bytes=64)
             nc.vector.quantize_mx(
                 out=wd_codes[g][:].bitcast(FP8X4), scales=wd_scales[g][:], in_=wd_rounded[g][:].rearrange("p n t -> p (n t)")
             )
 
-        def make_h(g, c0, width, block=BLOCK, quantise_cols=None, lent=None, product_cols=None):
-            quantise_cols = quantise_cols or width
-            per_bank = HALF // block
-            banks = PACK // per_bank
-            h_rounded = ring.tile([P, width, banks, per_bank], BF16, name="h_rounded", align_bytes=64, bufs=H_BUFS)
-            h_codes[g, c0] = keep.tile([P, width], U32, name="h_codes%d_%d" % (g, c0), align_bytes=64)
-            h_scales[g, c0] = keep.tile([P, width], U8, name="h_scales%d_%d" % (g, c0), align_bytes=64)
-            for j0 in range(0, width, block):
-                if lent == "shared":
-                    silu = shared.tile([P, banks, block, per_bank], F32, name="silu_first%d" % j0, offset=(SILU_BYTES + 4 * N) * (j0 // block))
-                elif lent and j0 == width - block:
-                    silu = keep.tile([P, banks, block, per_bank], F32, name="silu_lent", tag=lent, align_bytes=64)
+        def make_h(g, first_user, users, piece=GROUP):
+            h_rounded = ring.tile([P, users, 2, 2], BF16, name="h_rounded", align_bytes=64)
+            codes = keep.tile([P, users], U32, name="h_codes%d_%d" % (g, first_user), align_bytes=64)
+            scales = keep.tile([P, users], U8, name="h_scales%d_%d" % (g, first_user), align_bytes=64)
+            h_codes[g, first_user], h_scales[g, first_user] = codes, scales
+            for j0 in range(0, users, GROUP):
+                user0 = first_user + j0
+                if (g, first_user) == (0, 0):
+                    place = SILU_BYTES * (j0 // GROUP)
+                    silu = shared.tile([P, 2, GROUP, 2], F32, name="silu_first%d" % j0, offset=place)
                 else:
-                    silu = ring.tile([P, banks, block, per_bank], F32, name="silu", align_bytes=64, bufs=SILU_BUFS)
-                users = slice(c0 + j0, c0 + j0 + block)
-                for u in range(banks):
-                    scores = score_banks.tile([P, per_bank, block], F32, name="scores")
-                    for e in range(per_bank):
-                        m0 = P * (per_bank * u + e)
+                    silu = ring.tile([P, 2, GROUP, 2], F32, name="silu", align_bytes=64, bufs=SILU_BUFS)
+                for u in range(2):
+                    scores = score_banks.tile([P, 2, GROUP], F32, name="scores")
+                    for e in range(2):
+                        m0 = P * (2 * u + e)
                         nc.tensor.matmul_mx(
                             out=scores[:, e, :],
                             lhsT=key_words[g][:, m0 : m0 + P].bitcast(FP8X4),
                             lhsT_scale=key_scales[KEY_SCALE_ROW:P, PASS * g + m0 : PASS * g + m0 + P],
-                            rhs=user_words[c0 + j0][:, 0:block].bitcast(FP8X4),
-                            rhs_scale=user_scales[:, users],
+                            rhs=user_words[user0].bitcast(FP8X4),
+                            rhs_scale=user_scales[:, user0 : user0 + GROUP],
                             start=True,
                             stop=True,
                         )
                     nc.scalar.activation(silu[:, u, :, :], scores[:].rearrange("p e n -> p n e"), ACT.Silu)
-                step = product_cols or block
-                bids = bid_tile[:, g, :].rearrange("p (u e) -> p u e", u=banks).unsqueeze(1)
-                for s0 in range(0, block, step):
+                bids = bid_tile[:, g, :].rearrange("p (u e) -> p u e", u=2).unsqueeze(1).to_broadcast([P, piece, 2, 2])
+                for s0 in range(0, GROUP, piece):
+                    cols = slice(j0 + s0, j0 + s0 + piece)
                     nc.vector.tensor_tensor(
-                        h_rounded[:, j0 + s0 : j0 + s0 + step, :, :],
-                        silu[:, :, s0 : s0 + step, :].rearrange("p u n e -> p n u e"),
-                        bids.to_broadcast([P, step, banks, per_bank]),
-                        ALU.mult,
+                        h_rounded[:, cols, :, :], silu[:, :, s0 : s0 + piece, :].rearrange("p u n e -> p n u e"), bids, ALU.mult
                     )
-                    if (j0 + s0 + step) % quantise_cols == 0:
-                        q0 = j0 + s0 + step - quantise_cols
-                        nc.vector.quantize_mx(
-                            out=h_codes[g, c0][:, q0 : q0 + quantise_cols].bitcast(FP8X4),
-                            scales=h_scales[g, c0][:, q0 : q0 + quantise_cols],
-                            in_=h_rounded[:, q0 : q0 + quantise_cols, :, :].rearrange("p n u e -> p (n u e)"),
-                        )
-
-        def add_pass(kind, g, c0, j0, width, bank0, s0=0, sw=None):
-            per_bank = HALF // width
-            first = c0 + j0 not in sums
-            if first:
-                sums[c0 + j0] = [
-                    value_banks.tile([P, per_bank, width], F32, name="values%d" % (bank0 + k)) for k in range(N_TILES // per_bank)
-                ]
-            sw = sw or width
-            added.extend([c0 + j0] * (sw // P))
-            last = added.count(c0 + j0) == 2 * PASSES * width // P
-            cols_a_pass = P if kind == "w4" and sw != HALF else sw
-            for c in range(N_TILES):
-                acc = sums[c0 + j0][c // per_bank][:, c % per_bank, :]
-                campaigns = slice(P * c, P * (c + 1))
-                if kind == "w4":
-                    codes = w4_codes[:, g, 2 * P * c : 2 * P * (c + 1)].bitcast(FP4X4)
-                    scales = w4_scale_tile[:, g, :].bitcast(U8)[:, campaigns]
-                else:
-                    codes, scales = wd_codes[g][:, campaigns].bitcast(FP8X4), wd_scales[g][:, campaigns]
-                for n0 in range(s0, s0 + sw, cols_a_pass):
-                    cols = slice(j0 + n0, j0 + n0 + cols_a_pass)
-                    nc.tensor.matmul_mx(
-                        out=acc[:, n0 : n0 + cols_a_pass],
-                        lhsT=codes,
-                        lhsT_scale=scales,
-                        rhs=h_codes[g, c0][:, cols].bitcast(FP8X4),
-                        rhs_scale=h_scales[g, c0][:, cols],
-                        start=(first and c % per_bank == 0 and n0 == s0),
-                        stop=(last and c % per_bank == per_bank - 1 and n0 + cols_a_pass == s0 + sw),
+                    nc.vector.quantize_mx(
+                        out=codes[:, cols].bitcast(FP8X4),
+                        scales=scales[:, cols],
+                        in_=h_rounded[:, cols, :, :].rearrange("p n u e -> p (n u e)"),
                     )
 
-        def add_both(g, c0, j0, width, bank0):
-            per_bank = HALF // width
-            cols_a_pass = P if width != HALF else width
-            added.extend([c0 + j0] * (2 * width // P))
-            last = added.count(c0 + j0) == 2 * PASSES * width // P
-            first = c0 + j0 not in sums
-            if first:
-                sums[c0 + j0] = [
-                    value_banks.tile([P, per_bank, width], F32, name="values%d" % (bank0 + k)) for k in range(N_TILES // per_bank)
+        def add_pass(g, first_user, users, first_bank, h_first_user):
+            per_bank = BANK // users
+            if g == 0:
+                sums[first_user] = [
+                    value_banks.tile([P, per_bank, users], F32, name="values%d" % (first_bank + k))
+                    for k in range(N_TILES // per_bank)
                 ]
+            codes, scales = h_codes[g, h_first_user], h_scales[g, h_first_user]
+            j0 = first_user - h_first_user
+            w4_cols = BANK if users == BANK else P
             for c in range(N_TILES):
-                acc = sums[c0 + j0][c // per_bank][:, c % per_bank, :]
+                acc = sums[first_user][c // per_bank][:, c % per_bank, :]
                 campaigns = slice(P * c, P * (c + 1))
-                for n0 in range(0, width, cols_a_pass):
-                    cols = slice(j0 + n0, j0 + n0 + cols_a_pass)
+                for s0 in range(0, users, w4_cols):
+                    cols = slice(j0 + s0, j0 + s0 + w4_cols)
                     nc.tensor.matmul_mx(
-                        out=acc[:, n0 : n0 + cols_a_pass],
+                        out=acc[:, s0 : s0 + w4_cols],
                         lhsT=w4_codes[:, g, 2 * P * c : 2 * P * (c + 1)].bitcast(FP4X4),
                         lhsT_scale=w4_scale_tile[:, g, :].bitcast(U8)[:, campaigns],
-                        rhs=h_codes[g, c0][:, cols].bitcast(FP8X4),
-                        rhs_scale=h_scales[g, c0][:, cols],
-                        start=(first and c % per_bank == 0 and n0 == 0),
+                        rhs=codes[:, cols].bitcast(FP8X4),
+                        rhs_scale=scales[:, cols],
+                        start=(g == 0 and c % per_bank == 0 and s0 == 0),
                         stop=False,
                     )
                 nc.tensor.matmul_mx(
                     out=acc,
                     lhsT=wd_codes[g][:, campaigns].bitcast(FP8X4),
                     lhsT_scale=wd_scales[g][:, campaigns],
-                    rhs=h_codes[g, c0][:, j0 : j0 + width].bitcast(FP8X4),
-                    rhs_scale=h_scales[g, c0][:, j0 : j0 + width],
+                    rhs=codes[:, j0 : j0 + users].bitcast(FP8X4),
+                    rhs_scale=scales[:, j0 : j0 + users],
                     start=False,
-                    stop=(last and c % per_bank == per_bank - 1),
+                    stop=(g == PASSES - 1 and c % per_bank == per_bank - 1),
                 )
 
-        def store(j0, width, on_vector=()):
-            per_bank = HALF // width
+        def store(first_user, users):
+            per_bank = BANK // users
             for k in range(N_TILES // per_bank):
-                result = ring.tile([P, per_bank, width], F32, name="result", bufs=N_TILES)
-                c0 = per_bank * k
-                if k not in on_vector:
-                    for e in range(per_bank):
-                        nc.scalar.activation(result[:, e, :], sums[j0][k][:, e, :], ACT.Identity, bias=bias_tile[:, c0 + e : c0 + e + 1])
-                elif per_bank == 1:
-                    nc.vector.tensor_scalar(result[:, 0, :], sums[j0][k][:, 0, :], bias_tile[:, c0 : c0 + 1], None, ALU.add)
+                result = ring.tile([P, per_bank, users], F32, name="result", bufs=N_TILES)
+                bank, c0 = sums[first_user][k], per_bank * k
+                if users == GROUP and k == 1:
+                    bias = bias_tile[:, c0 : c0 + per_bank].unsqueeze(2).to_broadcast([P, per_bank, users])
+                    nc.vector.tensor_tensor(result[:], bank[:], bias, ALU.add)
                 else:
-                    bias = bias_tile[:, c0 : c0 + per_bank].unsqueeze(2).to_broadcast([P, per_bank, width])
-                    nc.vector.tensor_tensor(result[:], sums[j0][k][:], bias, ALU.add)
-                rows = out[P * c0 : P * (c0 + per_bank), j0 : j0 + width]
+                    for c in range(per_bank):
+                        nc.scalar.activation(result[:, c, :], bank[:, c, :], ACT.Identity, bias=bias_tile[:, c0 + c : c0 + c + 1])
+                rows = out[P * c0 : P * (c0 + per_bank), first_user : first_user + users]
                 nc.sync.dma_start(rows.rearrange("(c p) j -> p c j", p=P), result[:])
 
-        gather_user_scales(0, 1024)
-        gather_user_words(0, 512)
+        nc.vector.tensor_copy(user_scales[:], user_table_scales[:].bitcast(U8).indirect(user_list[:]))
+        gather_user_words(0)
         gather_key_scales(0, 1)
         gather_key_words(0)
-        round_wd(0, (0, 1, 2, 3,))
+        round_wd(0, 0, N, nc.scalar.copy)
         quantise_wd(0)
-        round_wd(1, (0, 1,))
-        make_h(0, 0, 512, block=256, quantise_cols=256, lent="shared")
-        gather_key_scales(1, 3)
+        round_wd(1, 0, N // 2, nc.scalar.copy)
+        make_h(0, 0, HALF)
+        gather_key_scales(1, PASSES)
         gather_key_words(1)
-        make_h(1, 0, 512, block=256, quantise_cols=256)
-        round_wd(1, (2, 3,))
+        make_h(1, 0, HALF)
+        round_wd(1, N // 2, N, nc.scalar.copy)
         quantise_wd(1)
-        add_both(0, 0, 0, 512, 0)
+        add_pass(0, 0, HALF, 0, 0)
         gather_key_words(2)
-        make_h(2, 0, 512, block=256, quantise_cols=256)
-        round_wd(2, (0, 1, 2, 3,), (0,))
+        make_h(2, 0, HALF)
+        round_wd(2, 0, QUARTER, nc.vector.tensor_copy)
+        round_wd(2, QUARTER, N, nc.scalar.copy)
         quantise_wd(2)
-        gather_user_words(512, 512)
-        make_h(0, 512, 512, block=256, quantise_cols=256)
-        make_h(1, 512, 512, block=256, quantise_cols=256)
-        add_both(1, 0, 0, 512, 0)
-        add_both(2, 0, 0, 512, 0)
-        store(0, 512, ())
-        make_h(2, 512, 256)
-        make_h(2, 768, 256, block=256, quantise_cols=128, product_cols=128)
-        add_both(0, 512, 0, 256, 0)
-        add_both(0, 512, 256, 256, 2)
-        add_both(1, 512, 0, 256, 0)
-        add_both(1, 512, 256, 256, 2)
-        add_both(2, 512, 0, 256, 0)
-        store(512, 256, (1,))
-        add_both(2, 768, 0, 256, 2)
-        store(768, 256, (1,))
+        gather_user_words(HALF)
+        make_h(0, HALF, HALF)
+        make_h(1, HALF, HALF)
+        add_pass(1, 0, HALF, 0, 0)
+        add_pass(2, 0, HALF, 0, 0)
+        store(0, HALF)
+        last_group = HALF + GROUP
+        make_h(2, HALF, GROUP)
+        make_h(2, last_group, GROUP, piece=GROUP // 2)
+        for g in range(PASSES - 1):
+            add_pass(g, HALF, GROUP, 0, HALF)
+            add_pass(g, last_group, GROUP, 2, HALF)
+        add_pass(2, HALF, GROUP, 0, HALF)
+        store(HALF, GROUP)
+        add_pass(2, last_group, GROUP, 2, last_group)
+        store(last_group, GROUP)

@@ -28,6 +28,7 @@ HALF = S2 // 2
 GROUP = 256
 N_TILES = N // P
 KEY_SCALE_ROW = 4
+KEY_LOAD_ROW = P - 16
 QUARTER = N // 4
 SILU_BUFS = 5
 SILU_BYTES = GROUP * PACK * 4
@@ -67,33 +68,20 @@ def tile_list_keyword_campaign_values_kernel(
             nc.sync.dma_start(raw[:], rows.rearrange("(p t) n -> p t n", t=PACK))
 
         nc.vector.memset(user_table_scales[:], 0)
-        nc.vector.memset(key_table_scales[:], 0)
+        nc.vector.memset(key_table_scales[0:KEY_LOAD_ROW, :], 0)
         nc.vector.memset(w4_scale_tile[:], 0)
         warm_up = keep.tile([P, 2], F32, name="warm_up")
         nc.vector.memset(warm_up[:, 0:1], 0.0)
-        nc.scalar.activation(warm_up[:, 1:2], warm_up[:, 0:1], ACT.Silu)
 
-        nc.sync.dma_start(user_list[:], offs2)
         nc.sync.dma_start(key_list[:], offs)
-        for r in range(ROWS):
-            queue = nc.scalar if r < ROWS // 2 else nc.sync
-            queue.dma_start(user_table_scales[r:P:QUADRANT, :], tab2_scales[0, r:16:ROWS, :].bitcast(I32))
+        nc.sync.dma_start(key_table_scales[KEY_LOAD_ROW : KEY_LOAD_ROW + 16, :], tab_scales[0].bitcast(I32))
+        nc.sync.dma_start(user_list[:], offs2)
         nc.sync.dma_start(user_table[:], tab2_words[0].rearrange("p t i -> p (t i)").bitcast(I32))
         for r in range(ROWS):
-            nc.sync.dma_start(key_table_scales[KEY_SCALE_ROW + r : P : QUADRANT, :], tab_scales[0, r:16:ROWS, :].bitcast(I32))
+            nc.sync.dma_start(user_table_scales[r:P:QUADRANT, :], tab2_scales[0, r:16:ROWS, :].bitcast(I32))
+        nc.scalar.activation(warm_up[:, 1:2], warm_up[:, 0:1], ACT.Silu)
         load_wd(0, 0, N)
         nc.sync.dma_start(key_table[:], tab_words[0].rearrange("p t i -> p (t i)").bitcast(I32))
-        load_wd(1, 0, N // 2, under_silu=True)
-        nc.sync.dma_start(bid_tile[:], bid.rearrange("(g p t) -> p g t", g=PASSES, t=PACK))
-        for r in range(ROWS):
-            nc.sync.dma_start(
-                w4_scale_tile[r:P:QUADRANT, :, :], w4_scales[:, r:16:ROWS, :].rearrange("g q c -> q g c").bitcast(I32)
-            )
-        nc.sync.dma_start(w4_codes[:].bitcast(I32), w4_words.rearrange("g p c -> p g c").bitcast(I32))
-        load_wd(1, N // 2, N // 2)
-        load_wd(2, 0, N)
-        with nc.allow_non_contiguous_dma(reason="one bias value to a partition and campaign tile"):
-            nc.sync.dma_start(bias_tile[:], b.rearrange("(c p) -> p c", p=P))
 
         user_scales = keep.tile([P, S2], U8, name="user_scales", align_bytes=64)
         key_scales = keep.tile([P, S], U8, name="key_scales", align_bytes=64)
@@ -107,14 +95,19 @@ def tile_list_keyword_campaign_values_kernel(
             entries = user_list[:, first_user // 16 : (first_user + HALF) // 16]
             nc.vector.tensor_copy(words[:], user_table[:].bitcast(U32).indirect(entries))
 
-        def gather_key_scales(g0, g1):
-            in_order = keep.tile([P, PASS * (g1 - g0)], U8, name="key_scales_in_order%d" % g0, align_bytes=64)
-            entries = key_list[:, LIST_COLS * g0 : LIST_COLS * g1]
-            nc.vector.tensor_copy(in_order[:], key_table_scales[:].bitcast(U8).indirect(entries))
-            nc.vector.tensor_copy(
-                key_scales[:, PASS * g0 : PASS * g1].rearrange("p (g t m) -> p g t m", t=PACK, m=P),
-                in_order[:].rearrange("p (g m t) -> p g t m", t=PACK, m=P),
-            )
+        def gather_key_scales():
+            in_order = keep.tile([P, S], U8, name="key_scales_in_order", align_bytes=64)
+            nc.vector.tensor_copy(in_order[:], key_table_scales[:].bitcast(U8).indirect(key_list[:]))
+            for g0, g1 in ((0, 2), (2, PASSES)):
+                nc.vector.tensor_copy(
+                    key_scales[:, PASS * g0 : PASS * g1].rearrange("p (g t m) -> p g t m", t=PACK, m=P),
+                    in_order[:, PASS * g0 : PASS * g1].rearrange("p (g m t) -> p g t m", t=PACK, m=P),
+                )
+            as_words = key_scales[:].bitcast(I32)
+            for r in range(ROWS):
+                nc.sync.dma_start(
+                    as_words[KEY_SCALE_ROW + r : P : QUADRANT, :], as_words[KEY_LOAD_ROW + r : KEY_LOAD_ROW + 16 : ROWS, :]
+                )
 
         def gather_key_words(g):
             key_words[g] = keep.tile([P, PASS], U32, name="key_words%d" % g, align_bytes=64)
@@ -148,7 +141,7 @@ def tile_list_keyword_campaign_values_kernel(
                 user0 = first_user + j0
                 if (g, first_user) == (0, 0):
                     place = SILU_BYTES * (j0 // GROUP)
-                    silu = shared.tile([P, 2, GROUP, 2], F32, name="silu_first%d" % j0, offset=place)
+                    silu = shared.tile([P, 2, GROUP, 2], F32, name="silu_first%d" % j0, align_bytes=64, offset=place)
                 else:
                     silu = ring.tile([P, 2, GROUP, 2], F32, name="silu", align_bytes=64, bufs=SILU_BUFS)
                 for u in range(2):
@@ -225,16 +218,27 @@ def tile_list_keyword_campaign_values_kernel(
                 rows = out[P * c0 : P * (c0 + per_bank), first_user : first_user + users]
                 nc.sync.dma_start(rows.rearrange("(c p) j -> p c j", p=P), result[:])
 
+        load_wd(1, 0, N // 2, under_silu=True)
+        gather_key_scales()
+        nc.sync.dma_start(bid_tile[:], bid.rearrange("(g p t) -> p g t", g=PASSES, t=PACK))
+        for r in range(ROWS):
+            nc.sync.dma_start(
+                w4_scale_tile[r:P:QUADRANT, :, :], w4_scales[:, r:16:ROWS, :].rearrange("g q c -> q g c").bitcast(I32)
+            )
+        nc.sync.dma_start(w4_codes[:].bitcast(I32), w4_words.rearrange("g p c -> p g c").bitcast(I32))
+        load_wd(1, N // 2, N // 2)
+        load_wd(2, 0, N)
+        with nc.allow_non_contiguous_dma(reason="one bias value to a partition and campaign tile"):
+            nc.sync.dma_start(bias_tile[:], b.rearrange("(c p) -> p c", p=P))
         nc.vector.tensor_copy(user_scales[:], user_table_scales[:].bitcast(U8).indirect(user_list[:]))
         gather_user_words(0)
-        gather_key_scales(0, 1)
         gather_key_words(0)
         round_wd(0, 0, N, nc.scalar.copy)
         quantise_wd(0)
         round_wd(1, 0, N // 2, nc.scalar.copy)
         make_h(0, 0, HALF)
-        gather_key_scales(1, PASSES)
         gather_key_words(1)
+        gather_user_words(HALF)
         make_h(1, 0, HALF)
         round_wd(1, N // 2, N, nc.scalar.copy)
         quantise_wd(1)
@@ -244,7 +248,6 @@ def tile_list_keyword_campaign_values_kernel(
         round_wd(2, 0, QUARTER, nc.vector.tensor_copy)
         round_wd(2, QUARTER, N, nc.scalar.copy)
         quantise_wd(2)
-        gather_user_words(HALF)
         make_h(0, HALF, HALF)
         make_h(1, HALF, HALF)
         add_pass(1, 0, HALF, 0, 0)

@@ -30,7 +30,8 @@ N_TILES = N // P
 KEY_SCALE_ROW = 4
 KEY_LOAD_ROW = P - 16
 QUARTER = N // 4
-SILU_BUFS = 5
+LENT_UNTIL = 20
+SILU_BUFS = 7
 SILU_BYTES = GROUP * PACK * 4
 
 
@@ -42,7 +43,7 @@ def tile_list_keyword_campaign_values_kernel(
         keep = ctx.enter_context(tc.tile_pool(name="keep", bufs=1))
         shared = ctx.enter_context(tc.tile_pool(name="shared", bufs=1))
         ring = ctx.enter_context(tc.tile_pool(name="ring", bufs=PASSES))
-        score_banks = ctx.enter_context(tc.psum_pool(name="score_banks", bufs=4))
+        score_banks = ctx.enter_context(tc.psum_pool(name="score_banks", bufs=2))
         value_banks = ctx.enter_context(tc.psum_pool(name="value_banks", bufs=1))
 
         key_list = keep.tile([P, S // 16], U16, name="key_list")
@@ -86,7 +87,7 @@ def tile_list_keyword_campaign_values_kernel(
         user_scales = keep.tile([P, S2], U8, name="user_scales", align_bytes=64)
         key_scales = keep.tile([P, S], U8, name="key_scales", align_bytes=64)
         user_words, key_words, wd_rounded, wd_codes, wd_scales = {}, {}, {}, {}, {}
-        h_codes, h_scales, sums = {}, {}, {}
+        silus, h_codes, h_scales, sums = {}, {}, {}, {}
 
         def gather_user_words(first_user):
             words = keep.tile([P, HALF], U32, name="user_words%d" % first_user, align_bytes=64)
@@ -132,20 +133,20 @@ def tile_list_keyword_campaign_values_kernel(
                 out=wd_codes[g][:].bitcast(FP8X4), scales=wd_scales[g][:], in_=wd_rounded[g][:].rearrange("p n t -> p (n t)")
             )
 
-        def make_h(g, first_user, users, piece=GROUP):
-            h_rounded = ring.tile([P, users, 2, 2], BF16, name="h_rounded", align_bytes=64)
-            codes = keep.tile([P, users], U32, name="h_codes%d_%d" % (g, first_user), align_bytes=64)
-            scales = keep.tile([P, users], U8, name="h_scales%d_%d" % (g, first_user), align_bytes=64)
-            h_codes[g, first_user], h_scales[g, first_user] = codes, scales
-            for j0 in range(0, users, GROUP):
-                user0 = first_user + j0
-                if (g, first_user) == (0, 0):
-                    place = SILU_BYTES * (j0 // GROUP)
-                    silu = shared.tile([P, 2, GROUP, 2], F32, name="silu_first%d" % j0, align_bytes=64, offset=place)
+        def make_silu(g, first_user, users):
+            for user0 in range(first_user, first_user + users, GROUP):
+                if g == 0 and user0 < HALF:
+                    place = SILU_BYTES * (user0 // GROUP)
+                    silu = shared.tile([P, 2, GROUP, 2], F32, name="silu_first%d" % user0, align_bytes=64, offset=place)
                 else:
                     silu = ring.tile([P, 2, GROUP, 2], F32, name="silu", align_bytes=64, bufs=SILU_BUFS)
+                made = 2 * len(silus)
+                silus[g, user0] = silu
                 for u in range(2):
-                    scores = score_banks.tile([P, 2, GROUP], F32, name="scores")
+                    if made % 4 == 2 and made < LENT_UNTIL:
+                        scores = value_banks.tile([P, 2, GROUP], F32, name="values%d" % (N_TILES + u))
+                    else:
+                        scores = score_banks.tile([P, 2, GROUP], F32, name="scores")
                     for e in range(2):
                         m0 = P * (2 * u + e)
                         nc.tensor.matmul_mx(
@@ -158,33 +159,34 @@ def tile_list_keyword_campaign_values_kernel(
                             stop=True,
                         )
                     nc.scalar.activation(silu[:, u, :, :], scores[:].rearrange("p e n -> p n e"), ACT.Silu)
-                bids = bid_tile[:, g, :].rearrange("p (u e) -> p u e", u=2).unsqueeze(1).to_broadcast([P, piece, 2, 2])
-                for s0 in range(0, GROUP, piece):
-                    cols = slice(j0 + s0, j0 + s0 + piece)
-                    nc.vector.tensor_tensor(
-                        h_rounded[:, cols, :, :], silu[:, :, s0 : s0 + piece, :].rearrange("p u n e -> p n u e"), bids, ALU.mult
-                    )
-                    nc.vector.quantize_mx(
-                        out=codes[:, cols].bitcast(FP8X4),
-                        scales=scales[:, cols],
-                        in_=h_rounded[:, cols, :, :].rearrange("p n u e -> p (n u e)"),
-                    )
 
-        def add_pass(g, first_user, users, first_bank, h_first_user):
-            per_bank = BANK // users
+        def make_h(g, first_user, users, piece=GROUP):
+            h_rounded = ring.tile([P, users, 2, 2], BF16, name="h_rounded", align_bytes=64, bufs=4)
+            codes = keep.tile([P, users], U32, name="h_codes%d_%d" % (g, first_user), align_bytes=64)
+            scales = keep.tile([P, users], U8, name="h_scales%d_%d" % (g, first_user), align_bytes=64)
+            h_codes[g, first_user], h_scales[g, first_user] = codes, scales
+            bids = bid_tile[:, g, :].rearrange("p (u e) -> p u e", u=2).unsqueeze(1).to_broadcast([P, piece, 2, 2])
+            for s0 in range(0, users, piece):
+                cols = slice(s0, s0 + piece)
+                silu = silus[g, first_user + s0 - s0 % GROUP][:, :, s0 % GROUP : s0 % GROUP + piece, :]
+                nc.vector.tensor_tensor(h_rounded[:, cols, :, :], silu.rearrange("p u n e -> p n u e"), bids, ALU.mult)
+                nc.vector.quantize_mx(
+                    out=codes[:, cols].bitcast(FP8X4),
+                    scales=scales[:, cols],
+                    in_=h_rounded[:, cols, :, :].rearrange("p n u e -> p (n u e)"),
+                )
+
+        def add_pass(g, first_user, users, banks):
+            per_bank = N_TILES // len(banks)
             if g == 0:
-                sums[first_user] = [
-                    value_banks.tile([P, per_bank, users], F32, name="values%d" % (first_bank + k))
-                    for k in range(N_TILES // per_bank)
-                ]
-            codes, scales = h_codes[g, h_first_user], h_scales[g, h_first_user]
-            j0 = first_user - h_first_user
+                sums[first_user] = [value_banks.tile([P, per_bank, users], F32, name="values%d" % k) for k in banks]
+            codes, scales = h_codes[g, first_user], h_scales[g, first_user]
             w4_cols = BANK if users == BANK else P
             for c in range(N_TILES):
                 acc = sums[first_user][c // per_bank][:, c % per_bank, :]
                 campaigns = slice(P * c, P * (c + 1))
                 for s0 in range(0, users, w4_cols):
-                    cols = slice(j0 + s0, j0 + s0 + w4_cols)
+                    cols = slice(s0, s0 + w4_cols)
                     nc.tensor.matmul_mx(
                         out=acc[:, s0 : s0 + w4_cols],
                         lhsT=w4_codes[:, g, 2 * P * c : 2 * P * (c + 1)].bitcast(FP4X4),
@@ -198,18 +200,18 @@ def tile_list_keyword_campaign_values_kernel(
                     out=acc,
                     lhsT=wd_codes[g][:, campaigns].bitcast(FP8X4),
                     lhsT_scale=wd_scales[g][:, campaigns],
-                    rhs=codes[:, j0 : j0 + users].bitcast(FP8X4),
-                    rhs_scale=scales[:, j0 : j0 + users],
+                    rhs=codes[:].bitcast(FP8X4),
+                    rhs_scale=scales[:],
                     start=False,
                     stop=(g == PASSES - 1 and c % per_bank == per_bank - 1),
                 )
 
-        def store(first_user, users):
-            per_bank = BANK // users
+        def store(first_user, users, last=False):
+            per_bank = N_TILES // len(sums[first_user])
             for k in range(N_TILES // per_bank):
-                result = ring.tile([P, per_bank, users], F32, name="result", bufs=N_TILES)
+                result = ring.tile([P, per_bank, users], F32, name="result", bufs=6)
                 bank, c0 = sums[first_user][k], per_bank * k
-                if users == GROUP and k == 1:
+                if last and k % 2 == 1:
                     bias = bias_tile[:, c0 : c0 + per_bank].unsqueeze(2).to_broadcast([P, per_bank, users])
                     nc.vector.tensor_tensor(result[:], bank[:], bias, ALU.add)
                 else:
@@ -236,30 +238,33 @@ def tile_list_keyword_campaign_values_kernel(
         round_wd(0, 0, N, nc.scalar.copy)
         quantise_wd(0)
         round_wd(1, 0, N // 2, nc.scalar.copy)
+        make_silu(0, 0, HALF)
         make_h(0, 0, HALF)
         gather_key_words(1)
         gather_user_words(HALF)
+        make_silu(1, 0, HALF)
         make_h(1, 0, HALF)
         round_wd(1, N // 2, N, nc.scalar.copy)
         quantise_wd(1)
-        add_pass(0, 0, HALF, 0, 0)
+        add_pass(0, 0, HALF, range(N_TILES))
         gather_key_words(2)
+        make_silu(2, 0, HALF)
         make_h(2, 0, HALF)
         round_wd(2, 0, QUARTER, nc.vector.tensor_copy)
         round_wd(2, QUARTER, N, nc.scalar.copy)
         quantise_wd(2)
-        make_h(0, HALF, HALF)
-        make_h(1, HALF, HALF)
-        add_pass(1, 0, HALF, 0, 0)
-        add_pass(2, 0, HALF, 0, 0)
-        store(0, HALF)
         last_group = HALF + GROUP
-        make_h(2, HALF, GROUP)
-        make_h(2, last_group, GROUP, piece=GROUP // 2)
-        for g in range(PASSES - 1):
-            add_pass(g, HALF, GROUP, 0, HALF)
-            add_pass(g, last_group, GROUP, 2, HALF)
-        add_pass(2, HALF, GROUP, 0, HALF)
+        for user0 in (HALF, last_group):
+            for g in range(PASSES):
+                make_silu(g, user0, GROUP)
+        add_pass(1, 0, HALF, range(N_TILES))
+        add_pass(2, 0, HALF, range(N_TILES))
+        store(0, HALF)
+        for g in range(PASSES):
+            make_h(g, HALF, GROUP)
+            add_pass(g, HALF, GROUP, (N_TILES, N_TILES + 1))
         store(HALF, GROUP)
-        add_pass(2, last_group, GROUP, 2, last_group)
-        store(last_group, GROUP)
+        for g in range(PASSES):
+            make_h(g, last_group, GROUP, piece=GROUP // 2 if g == PASSES - 1 else GROUP)
+            add_pass(g, last_group, GROUP, range(N_TILES))
+        store(last_group, GROUP, last=True)

@@ -31,7 +31,7 @@ KEY_SCALE_ROW = 4
 KEY_LOAD_ROW = P - 16
 QUARTER = N // 4
 LENT_UNTIL = 20
-SILU_BUFS = 7
+SILU_BUFS = 10
 SILU_BYTES = GROUP * PACK * 4
 
 
@@ -161,7 +161,10 @@ def tile_list_keyword_campaign_values_kernel(
                     nc.scalar.activation(silu[:, u, :, :], scores[:].rearrange("p e n -> p n e"), ACT.Silu)
 
         def make_h(g, first_user, users, piece=GROUP):
-            h_rounded = ring.tile([P, users, 2, 2], BF16, name="h_rounded", align_bytes=64, bufs=4)
+            if users == HALF:
+                h_rounded = keep.tile([P, users, 2, 2], BF16, name="h_rounded_wide", align_bytes=64)
+            else:
+                h_rounded = ring.tile([P, users, 2, 2], BF16, name="h_rounded", align_bytes=64, bufs=4)
             codes = keep.tile([P, users], U32, name="h_codes%d_%d" % (g, first_user), align_bytes=64)
             scales = keep.tile([P, users], U8, name="h_scales%d_%d" % (g, first_user), align_bytes=64)
             h_codes[g, first_user], h_scales[g, first_user] = codes, scales
@@ -176,7 +179,7 @@ def tile_list_keyword_campaign_values_kernel(
                     in_=h_rounded[:, cols, :, :].rearrange("p n u e -> p (n u e)"),
                 )
 
-        def add_pass(g, first_user, users, banks):
+        def add_pass(g, first_user, users, banks, with_w4=True, with_wd=True):
             per_bank = N_TILES // len(banks)
             if g == 0:
                 sums[first_user] = [value_banks.tile([P, per_bank, users], F32, name="values%d" % k) for k in banks]
@@ -185,7 +188,7 @@ def tile_list_keyword_campaign_values_kernel(
             for c in range(N_TILES):
                 acc = sums[first_user][c // per_bank][:, c % per_bank, :]
                 campaigns = slice(P * c, P * (c + 1))
-                for s0 in range(0, users, w4_cols):
+                for s0 in range(0, users if with_w4 else 0, w4_cols):
                     cols = slice(s0, s0 + w4_cols)
                     nc.tensor.matmul_mx(
                         out=acc[:, s0 : s0 + w4_cols],
@@ -196,15 +199,16 @@ def tile_list_keyword_campaign_values_kernel(
                         start=(g == 0 and c % per_bank == 0 and s0 == 0),
                         stop=False,
                     )
-                nc.tensor.matmul_mx(
-                    out=acc,
-                    lhsT=wd_codes[g][:, campaigns].bitcast(FP8X4),
-                    lhsT_scale=wd_scales[g][:, campaigns],
-                    rhs=codes[:].bitcast(FP8X4),
-                    rhs_scale=scales[:],
-                    start=False,
-                    stop=(g == PASSES - 1 and c % per_bank == per_bank - 1),
-                )
+                if with_wd:
+                    nc.tensor.matmul_mx(
+                        out=acc,
+                        lhsT=wd_codes[g][:, campaigns].bitcast(FP8X4),
+                        lhsT_scale=wd_scales[g][:, campaigns],
+                        rhs=codes[:].bitcast(FP8X4),
+                        rhs_scale=scales[:],
+                        start=False,
+                        stop=(g == PASSES - 1 and c % per_bank == per_bank - 1),
+                    )
 
         def store(first_user, users, last=False):
             per_bank = N_TILES // len(sums[first_user])
@@ -238,27 +242,30 @@ def tile_list_keyword_campaign_values_kernel(
         round_wd(0, 0, N, nc.scalar.copy)
         quantise_wd(0)
         round_wd(1, 0, N // 2, nc.scalar.copy)
-        make_silu(0, 0, HALF)
-        make_h(0, 0, HALF)
         gather_key_words(1)
-        gather_user_words(HALF)
-        make_silu(1, 0, HALF)
-        make_h(1, 0, HALF)
-        round_wd(1, N // 2, N, nc.scalar.copy)
-        quantise_wd(1)
-        add_pass(0, 0, HALF, range(N_TILES))
         gather_key_words(2)
-        make_silu(2, 0, HALF)
-        make_h(2, 0, HALF)
-        round_wd(2, 0, QUARTER, nc.vector.tensor_copy)
-        round_wd(2, QUARTER, N, nc.scalar.copy)
-        quantise_wd(2)
+        gather_user_words(HALF)
         last_group = HALF + GROUP
-        for user0 in (HALF, last_group):
-            for g in range(PASSES):
-                make_silu(g, user0, GROUP)
+        make_silu(0, 0, HALF)
+        make_silu(1, 0, HALF)
+        round_wd(1, N // 2, N, nc.scalar.copy)
+        make_silu(2, 0, HALF)
+        make_silu(0, HALF, GROUP)
+        round_wd(2, QUARTER, N, nc.scalar.copy)
+        make_silu(1, HALF, GROUP)
+        make_silu(2, HALF, GROUP)
+        for g in range(PASSES):
+            make_silu(g, last_group, GROUP)
+        make_h(0, 0, HALF)
+        add_pass(0, 0, HALF, range(N_TILES))
+        quantise_wd(1)
+        make_h(1, 0, HALF)
         add_pass(1, 0, HALF, range(N_TILES))
-        add_pass(2, 0, HALF, range(N_TILES))
+        make_h(2, 0, HALF)
+        add_pass(2, 0, HALF, range(N_TILES), with_wd=False)
+        round_wd(2, 0, QUARTER, nc.vector.tensor_copy)
+        quantise_wd(2)
+        add_pass(2, 0, HALF, range(N_TILES), with_w4=False)
         store(0, HALF)
         for g in range(PASSES):
             make_h(g, HALF, GROUP)

@@ -48,13 +48,13 @@ def tile_list_keyword_campaign_values_kernel(
 
         key_list = keep.tile([P, S // 16], U16, name="key_list")
         user_list = keep.tile([P, S2 // 16], U16, name="user_list")
-        key_table = keep.tile([P, T], I32, name="key_table", align_bytes=64)
-        user_table = keep.tile([P, T2], I32, name="user_table", align_bytes=64)
-        key_table_scales = keep.tile([P, T // 4], I32, name="key_table_scales", align_bytes=64)
-        user_table_scales = keep.tile([P, T2 // 4], I32, name="user_table_scales", align_bytes=64)
-        w4_codes = keep.tile([P, PASSES, 2 * N], U8, name="w4_codes", align_bytes=64)
-        w4_scale_tile = keep.tile([P, PASSES, N // 4], I32, name="w4_scale_tile", align_bytes=64)
-        bid_tile = keep.tile([P, PASSES, PACK], F32, name="bid_tile", align_bytes=64)
+        key_table = keep.tile([P, T], I32, name="key_table", align_bytes=256)
+        user_table = keep.tile([P, T2], I32, name="user_table", align_bytes=256)
+        key_table_scales = keep.tile([P, T // 4], I32, name="key_table_scales", align_bytes=256)
+        user_table_scales = keep.tile([P, T2 // 4], I32, name="user_table_scales", align_bytes=256)
+        w4_codes = keep.tile([P, PASSES, 2 * N], U8, name="w4_codes", align_bytes=256)
+        w4_scale_tile = keep.tile([P, PASSES, N // 4], I32, name="w4_scale_tile", align_bytes=256)
+        bid_tile = keep.tile([P, PASSES, PACK], F32, name="bid_tile", align_bytes=256)
         bias_tile = keep.tile([P, N_TILES], F32, name="bias_tile")
         wd_raw = {}
 
@@ -84,20 +84,20 @@ def tile_list_keyword_campaign_values_kernel(
         load_wd(0, 0, N)
         nc.sync.dma_start(key_table[:], tab_words[0].rearrange("p t i -> p (t i)").bitcast(I32))
 
-        user_scales = keep.tile([P, S2], U8, name="user_scales", align_bytes=64)
-        key_scales = keep.tile([P, S], U8, name="key_scales", align_bytes=64)
+        user_scales = keep.tile([P, S2], U8, name="user_scales", align_bytes=256)
+        key_scales = keep.tile([P, S], U8, name="key_scales", align_bytes=256)
         user_words, key_words, wd_rounded, wd_codes, wd_scales = {}, {}, {}, {}, {}
         silus, h_codes, h_scales, sums = {}, {}, {}, {}
 
         def gather_user_words(first_user):
-            words = keep.tile([P, HALF], U32, name="user_words%d" % first_user, align_bytes=64)
+            words = keep.tile([P, HALF], U32, name="user_words%d" % first_user, align_bytes=256)
             for j0 in range(0, HALF, GROUP):
                 user_words[first_user + j0] = words[:, j0 : j0 + GROUP]
             entries = user_list[:, first_user // 16 : (first_user + HALF) // 16]
             nc.vector.tensor_copy(words[:], user_table[:].bitcast(U32).indirect(entries))
 
         def gather_key_scales():
-            in_order = keep.tile([P, S], U8, name="key_scales_in_order", align_bytes=64)
+            in_order = keep.tile([P, S], U8, name="key_scales_in_order", align_bytes=256)
             nc.vector.tensor_copy(in_order[:], key_table_scales[:].bitcast(U8).indirect(key_list[:]))
             for g0, g1 in ((0, 2), (2, PASSES)):
                 nc.vector.tensor_copy(
@@ -111,7 +111,7 @@ def tile_list_keyword_campaign_values_kernel(
                 )
 
         def gather_key_words(g):
-            key_words[g] = keep.tile([P, PASS], U32, name="key_words%d" % g, align_bytes=64)
+            key_words[g] = keep.tile([P, PASS], U32, name="key_words%d" % g, align_bytes=256)
             entries = key_list[:, LIST_COLS * g : LIST_COLS * (g + 1)]
             nc.vector.tensor_copy(
                 key_words[g][:].rearrange("p (t m) -> p m t", t=PACK), key_table[:].bitcast(U32).indirect(entries)
@@ -119,7 +119,7 @@ def tile_list_keyword_campaign_values_kernel(
 
         def round_wd(g, n0, n1, copy):
             if g not in wd_rounded:
-                wd_rounded[g] = ring.tile([P, N, PACK], BF16, name="wd_rounded", align_bytes=64)
+                wd_rounded[g] = ring.tile([P, N, PACK], BF16, name="wd_rounded", align_bytes=256)
             for n in range(n0, n1, QUARTER):
                 copy(
                     wd_rounded[g][:, n : n + QUARTER, :].rearrange("p (c x) t -> p c t x", x=4),
@@ -127,8 +127,8 @@ def tile_list_keyword_campaign_values_kernel(
                 )
 
         def quantise_wd(g):
-            wd_codes[g] = keep.tile([P, N], U32, name="wd_codes%d" % g, align_bytes=64)
-            wd_scales[g] = keep.tile([P, N], U8, name="wd_scales%d" % g, align_bytes=64)
+            wd_codes[g] = keep.tile([P, N], U32, name="wd_codes%d" % g, align_bytes=256)
+            wd_scales[g] = keep.tile([P, N], U8, name="wd_scales%d" % g, align_bytes=256)
             nc.vector.quantize_mx(
                 out=wd_codes[g][:].bitcast(FP8X4), scales=wd_scales[g][:], in_=wd_rounded[g][:].rearrange("p n t -> p (n t)")
             )
@@ -137,9 +137,9 @@ def tile_list_keyword_campaign_values_kernel(
             for user0 in range(first_user, first_user + users, GROUP):
                 if g == 0 and user0 < HALF:
                     place = SILU_BYTES * (user0 // GROUP)
-                    silu = shared.tile([P, 2, GROUP, 2], F32, name="silu_first%d" % user0, align_bytes=64, offset=place)
+                    silu = shared.tile([P, 2, GROUP, 2], F32, name="silu_first%d" % user0, align_bytes=256, offset=place)
                 else:
-                    silu = ring.tile([P, 2, GROUP, 2], F32, name="silu", align_bytes=64, bufs=SILU_BUFS)
+                    silu = ring.tile([P, 2, GROUP, 2], F32, name="silu", align_bytes=256, bufs=SILU_BUFS)
                 made = 2 * len(silus)
                 silus[g, user0] = silu
                 for u in range(2):
@@ -162,11 +162,11 @@ def tile_list_keyword_campaign_values_kernel(
 
         def make_h(g, first_user, users, piece=GROUP):
             if users == HALF:
-                h_rounded = keep.tile([P, users, 2, 2], BF16, name="h_rounded_wide", align_bytes=64)
+                h_rounded = keep.tile([P, users, 2, 2], BF16, name="h_rounded_wide", align_bytes=256)
             else:
-                h_rounded = ring.tile([P, users, 2, 2], BF16, name="h_rounded", align_bytes=64, bufs=4)
-            codes = keep.tile([P, users], U32, name="h_codes%d_%d" % (g, first_user), align_bytes=64)
-            scales = keep.tile([P, users], U8, name="h_scales%d_%d" % (g, first_user), align_bytes=64)
+                h_rounded = ring.tile([P, users, 2, 2], BF16, name="h_rounded", align_bytes=256, bufs=4)
+            codes = keep.tile([P, users], U32, name="h_codes%d_%d" % (g, first_user), align_bytes=256)
+            scales = keep.tile([P, users], U8, name="h_scales%d_%d" % (g, first_user), align_bytes=256)
             h_codes[g, first_user], h_scales[g, first_user] = codes, scales
             bids = bid_tile[:, g, :].rearrange("p (u e) -> p u e", u=2).unsqueeze(1).to_broadcast([P, piece, 2, 2])
             for s0 in range(0, users, piece):

@@ -1,6 +1,7 @@
 from contextlib import ExitStack
 
 import concourse.mybir as mybir
+from concourse.masks import make_identity
 
 K, T, S, T2, S2, N = 512, 4096, 1536, 2048, 1024, 512
 FLOPS = 2 * K * S * S2 + 2 * 2 * S * N * S2
@@ -30,9 +31,11 @@ N_TILES = N // P
 KEY_SCALE_ROW = 4
 KEY_LOAD_ROW = P - 16
 QUARTER = N // 4
-LENT_UNTIL = 20
-SILU_BUFS = 10
+SHARE = 128
+H_BYTES = GROUP * PACK * 2
 SILU_BYTES = GROUP * PACK * 4
+VALUE_BANKS = ((0, 1, 2, 3), (4, 0, 1, 2))
+SCORE_BANKS = [4, 5, 6, 0, 1, 2, 3] + [4, 5, 6] * 4 + [5, 6, 5, 6, 5]
 
 
 def tile_list_keyword_campaign_values_kernel(
@@ -43,8 +46,8 @@ def tile_list_keyword_campaign_values_kernel(
         keep = ctx.enter_context(tc.tile_pool(name="keep", bufs=1))
         shared = ctx.enter_context(tc.tile_pool(name="shared", bufs=1))
         ring = ctx.enter_context(tc.tile_pool(name="ring", bufs=PASSES))
-        score_banks = ctx.enter_context(tc.psum_pool(name="score_banks", bufs=2))
-        value_banks = ctx.enter_context(tc.psum_pool(name="value_banks", bufs=1))
+        h_slots = ctx.enter_context(tc.tile_pool(name="h_slots", bufs=1))
+        banks = ctx.enter_context(tc.psum_pool(name="banks", bufs=1))
 
         key_list = keep.tile([P, S // 16], U16, name="key_list")
         user_list = keep.tile([P, S2 // 16], U16, name="user_list")
@@ -54,23 +57,23 @@ def tile_list_keyword_campaign_values_kernel(
         user_table_scales = keep.tile([P, T2 // 4], I32, name="user_table_scales", align_bytes=256)
         w4_codes = keep.tile([P, PASSES, 2 * N], U8, name="w4_codes", align_bytes=256)
         w4_scale_tile = keep.tile([P, PASSES, N // 4], I32, name="w4_scale_tile", align_bytes=256)
-        bid_tile = keep.tile([P, PASSES, PACK], F32, name="bid_tile", align_bytes=256)
+        bid_tile = keep.tile([P, P], F32, name="bid_tile", align_bytes=256)
+        identity = keep.tile([P, P], F32, name="identity", align_bytes=256)
         bias_tile = keep.tile([P, N_TILES], F32, name="bias_tile")
         wd_raw = {}
 
-        def load_wd(g, n0, width, under_silu=False):
-            if under_silu:
-                raw = shared.tile([P, PACK, width], F32, name="wd_raw_early", offset=SILU_BYTES // 2)
-            else:
-                raw = keep.tile([P, PACK, width], F32, name="wd_raw%d_%d" % (g, n0))
-            for n in range(0, width, QUARTER):
-                wd_raw[g, n0 + n] = raw[:, :, n : n + QUARTER]
+        def load_wd(g, n0, width):
+            raw = keep.tile([P, PACK, width], F32, name="wd_raw%d_%d" % (g, n0))
+            for n in range(n0, n0 + width, QUARTER):
+                wd_raw[g, n // QUARTER] = raw, n0
             rows = wd[PASS * g : PASS * (g + 1), n0 : n0 + width]
             nc.sync.dma_start(raw[:], rows.rearrange("(p t) n -> p t n", t=PACK))
 
         nc.vector.memset(user_table_scales[:], 0)
         nc.vector.memset(key_table_scales[0:KEY_LOAD_ROW, :], 0)
         nc.vector.memset(w4_scale_tile[:], 0)
+        nc.vector.memset(bid_tile[:], 0.0)
+        make_identity(nc, identity[:])
         warm_up = keep.tile([P, 2], F32, name="warm_up")
         nc.vector.memset(warm_up[:, 0:1], 0.0)
 
@@ -83,6 +86,9 @@ def tile_list_keyword_campaign_values_kernel(
         nc.scalar.activation(warm_up[:, 1:2], warm_up[:, 0:1], ACT.Silu)
         load_wd(0, 0, N)
         nc.sync.dma_start(key_table[:], tab_words[0].rearrange("p t i -> p (t i)").bitcast(I32))
+        nc.sync.dma_start(
+            bid_tile[:, 0 : PASSES * PACK].rearrange("p (g t) -> p g t", t=PACK), bid.rearrange("(g p t) -> p g t", g=PASSES, t=PACK)
+        )
 
         user_scales = keep.tile([P, S2], U8, name="user_scales", align_bytes=256)
         key_scales = keep.tile([P, S], U8, name="key_scales", align_bytes=256)
@@ -117,161 +123,254 @@ def tile_list_keyword_campaign_values_kernel(
                 key_words[g][:].rearrange("p (t m) -> p m t", t=PACK), key_table[:].bitcast(U32).indirect(entries)
             )
 
-        def round_wd(g, n0, n1, copy):
-            if g not in wd_rounded:
-                wd_rounded[g] = ring.tile([P, N, PACK], BF16, name="wd_rounded", align_bytes=256)
-            for n in range(n0, n1, QUARTER):
-                copy(
-                    wd_rounded[g][:, n : n + QUARTER, :].rearrange("p (c x) t -> p c t x", x=4),
-                    wd_raw[g, n].rearrange("p t (c x) -> p c t x", x=4),
+        def rounded_tile(g, q0, q1, behind_step=None):
+            name, shape = "wd_rounded%d_%d" % (g, q0), [P, QUARTER * (q1 - q0), PACK]
+            if behind_step is None:
+                tile = keep.tile(shape, BF16, name=name, align_bytes=256)
+            else:
+                tile = shared.tile(shape, BF16, name=name, align_bytes=256, offset=silu_place(behind_step) + SILU_BYTES + SILU_BYTES // 2)
+            for q in range(q0, q1):
+                wd_rounded[g, q] = tile, q0, q1
+
+        def round_wd(g, q0, q1, copy):
+            raw, raw0 = wd_raw[g, q0]
+            tile, first, last = wd_rounded[g, q0]
+            rounded = tile[:, QUARTER * (q0 - first) : QUARTER * (q1 - first), :]
+            rows = raw[:, :, QUARTER * q0 - raw0 : QUARTER * q1 - raw0]
+            if copy is None:
+                nc.gpsimd.tensor_scalar(rounded, rows.rearrange("p t n -> p n t"), 1.0, 0.0, ALU.mult, ALU.add)
+            else:
+                copy(rounded.rearrange("p (c x) t -> p c t x", x=4), rows.rearrange("p t (c x) -> p c t x", x=4))
+
+        def place_bids():
+            turned = banks.tile([P, P], F32, name="bank4")
+            nc.tensor.transpose(turned[:], bid_tile[:], identity[:])
+            turned_copy = keep.tile([P, P], F32, name="bids_turned", align_bytes=256)
+            nc.scalar.copy(turned_copy[:], turned[:])
+            nc.tensor.transpose(bid_bank[:], turned_copy[:], identity[:])
+            for g in range(PASSES):
+                nc.scalar.copy(
+                    bid_rows[:, g, :, :], bid_tile[:, PACK * g : PACK * (g + 1)].unsqueeze(1).to_broadcast([P, SHARE, PACK])
                 )
 
-        def quantise_wd(g):
-            wd_codes[g] = keep.tile([P, N], U32, name="wd_codes%d" % g, align_bytes=256)
-            wd_scales[g] = keep.tile([P, N], U8, name="wd_scales%d" % g, align_bytes=256)
+        bid_bank = banks.tile([P, P], F32, name="bid_bank")
+        bid_rows = keep.tile([P, PASSES, SHARE, PACK], F32, name="bid_rows", align_bytes=256)
+
+        def quantise_wd(g, q0, step=None):
+            if g not in wd_codes:
+                if step is None:
+                    wd_codes[g] = keep.tile([P, N], U32, name="wd_codes%d" % g, align_bytes=256)
+                else:
+                    wd_codes[g] = shared.tile([P, N], U32, name="wd_codes%d" % g, align_bytes=256, offset=silu_place(step) + SILU_BYTES)
+                wd_scales[g] = keep.tile([P, N], U8, name="wd_scales%d" % g, align_bytes=256)
+            tile, first, last = wd_rounded[g, q0]
+            n0, n1 = QUARTER * first, QUARTER * last
             nc.vector.quantize_mx(
-                out=wd_codes[g][:].bitcast(FP8X4), scales=wd_scales[g][:], in_=wd_rounded[g][:].rearrange("p n t -> p (n t)")
+                out=wd_codes[g][:, n0:n1].bitcast(FP8X4),
+                scales=wd_scales[g][:, n0:n1],
+                in_=tile[:].rearrange("p n t -> p (n t)"),
             )
 
-        def make_silu(g, first_user, users):
-            for user0 in range(first_user, first_user + users, GROUP):
-                if g == 0 and user0 < HALF:
-                    place = SILU_BYTES * (user0 // GROUP)
-                    silu = shared.tile([P, 2, GROUP, 2], F32, name="silu_first%d" % user0, align_bytes=256, offset=place)
-                else:
-                    silu = ring.tile([P, 2, GROUP, 2], F32, name="silu", align_bytes=256, bufs=SILU_BUFS)
-                made = 2 * len(silus)
-                silus[g, user0] = silu
-                for u in range(2):
-                    if made % 4 == 2 and made < LENT_UNTIL:
-                        scores = value_banks.tile([P, 2, GROUP], F32, name="values%d" % (N_TILES + u))
-                    else:
-                        scores = score_banks.tile([P, 2, GROUP], F32, name="scores")
-                    for e in range(2):
-                        m0 = P * (2 * u + e)
-                        nc.tensor.matmul_mx(
-                            out=scores[:, e, :],
-                            lhsT=key_words[g][:, m0 : m0 + P].bitcast(FP8X4),
-                            lhsT_scale=key_scales[KEY_SCALE_ROW:P, PASS * g + m0 : PASS * g + m0 + P],
-                            rhs=user_words[user0].bitcast(FP8X4),
-                            rhs_scale=user_scales[:, user0 : user0 + GROUP],
-                            start=True,
-                            stop=True,
-                        )
-                    nc.scalar.activation(silu[:, u, :, :], scores[:].rearrange("p e n -> p n e"), ACT.Silu)
+        def silu_place(step):
+            return 2 * SILU_BYTES * step
 
-        def make_h(g, first_user, users, piece=GROUP):
-            if users == HALF:
-                h_rounded = keep.tile([P, users, 2, 2], BF16, name="h_rounded_wide", align_bytes=256)
-            else:
-                h_rounded = ring.tile([P, users, 2, 2], BF16, name="h_rounded", align_bytes=256, bufs=4)
-            codes = keep.tile([P, users], U32, name="h_codes%d_%d" % (g, first_user), align_bytes=256)
-            scales = keep.tile([P, users], U8, name="h_scales%d_%d" % (g, first_user), align_bytes=256)
-            h_codes[g, first_user], h_scales[g, first_user] = codes, scales
-            bids = bid_tile[:, g, :].rearrange("p (u e) -> p u e", u=2).unsqueeze(1).to_broadcast([P, piece, 2, 2])
-            for s0 in range(0, users, piece):
-                cols = slice(s0, s0 + piece)
-                silu = silus[g, first_user + s0 - s0 % GROUP][:, :, s0 % GROUP : s0 % GROUP + piece, :]
-                nc.vector.tensor_tensor(h_rounded[:, cols, :, :], silu.rearrange("p u n e -> p n u e"), bids, ALU.mult)
-                nc.vector.quantize_mx(
-                    out=codes[:, cols].bitcast(FP8X4),
-                    scales=scales[:, cols],
-                    in_=h_rounded[:, cols, :, :].rearrange("p n u e -> p (n u e)"),
-                )
+        def score_bank(shape):
+            bank = banks.tile(shape, F32, name="bank%d" % SCORE_BANKS[len(scored)])
+            scored.append(bank)
+            return bank
 
-        def add_pass(g, first_user, users, banks, with_w4=True, with_wd=True):
-            per_bank = N_TILES // len(banks)
-            if g == 0:
-                sums[first_user] = [value_banks.tile([P, per_bank, users], F32, name="values%d" % k) for k in banks]
-            codes, scales = h_codes[g, first_user], h_scales[g, first_user]
-            w4_cols = BANK if users == BANK else P
-            for c in range(N_TILES):
-                acc = sums[first_user][c // per_bank][:, c % per_bank, :]
+        def score(out_ap, g, t, user0, users):
+            m0 = P * t
+            half0 = user0 - user0 % GROUP
+            nc.tensor.matmul_mx(
+                out=out_ap,
+                lhsT=key_words[g][:, m0 : m0 + P].bitcast(FP8X4),
+                lhsT_scale=key_scales[KEY_SCALE_ROW:P, PASS * g + m0 : PASS * g + m0 + P],
+                rhs=user_words[half0][:, user0 - half0 : user0 - half0 + users].bitcast(FP8X4),
+                rhs_scale=user_scales[:, user0 : user0 + users],
+                start=True,
+                stop=True,
+            )
+
+        def silu_of_quad(step, part):
+            g, first_user = step % PASSES, HALF * (step // PASSES)
+            silu = shared.tile([P, P, PACK], F32, name="silu%d_%d" % (step, part), align_bytes=256, offset=silu_place(step) + SILU_BYTES // 2 * part)
+            silus[step, part] = silu
+            scores = score_bank([P, PACK, P])
+            for t in range(PACK):
+                score(scores[:, t, :], g, t, first_user + P * part, P)
+            nc.scalar.activation(silu[:], scores[:].rearrange("p t n -> p n t"), ACT.Silu)
+
+        def silu_of_pairs(step):
+            g, first_user = step % PASSES, HALF * (step // PASSES)
+            silu = shared.tile([P, 2, GROUP, 2], F32, name="silu%d_2" % step, align_bytes=256, offset=silu_place(step) + SILU_BYTES)
+            silus[step, 2] = silu
+            for u in range(2):
+                scores = score_bank([P, 2, GROUP])
+                for e in range(2):
+                    score(scores[:, e, :], g, 2 * u + e, first_user + GROUP, GROUP)
+                nc.scalar.activation(silu[:, u, :, :], scores[:].rearrange("p e n -> p n e"), ACT.Silu)
+
+        def make_silu(step):
+            if step == 0:
+                silu_of_pairs(step)
+            silu_of_quad(step, 0)
+            if step > 0:
+                silu_of_pairs(step)
+            silu_of_quad(step, 1)
+
+        def multiply(step):
+            g = step % PASSES
+            pairs = h_slots.tile([P, GROUP, 2, 2], BF16, name="h_pairs", align_bytes=256)
+            quads = h_slots.tile([P, GROUP, PACK], BF16, name="h_quads", align_bytes=256)
+            h_rounded[step] = pairs, quads
+            bids = bid_bank[:, PACK * g : PACK * (g + 1)]
+            nc.gpsimd.tensor_tensor(quads[:, 0:SHARE, :], silus[step, 0][:], bid_rows[:, g, :, :], ALU.mult)
+            nc.vector.tensor_tensor(
+                pairs[:],
+                silus[step, 2][:].rearrange("p u n e -> p n u e"),
+                bids.rearrange("p (u e) -> p u e", u=2).unsqueeze(1).to_broadcast([P, GROUP, 2, 2]),
+                ALU.mult,
+            )
+            nc.vector.tensor_tensor(quads[:, SHARE:GROUP, :], silus[step, 1][:], bids.unsqueeze(1).to_broadcast([P, P, PACK]), ALU.mult)
+
+        def quantise_h(step):
+            pairs, quads = h_rounded[step]
+            codes = keep.tile([P, HALF], U32, name="h_codes%d" % step, align_bytes=256)
+            scales = keep.tile([P, HALF], U8, name="h_scales%d" % step, align_bytes=256)
+            h_codes[step], h_scales[step] = codes, scales
+            nc.vector.quantize_mx(
+                out=codes[:, GROUP:HALF].bitcast(FP8X4), scales=scales[:, GROUP:HALF], in_=pairs[:].rearrange("p n u e -> p (n u e)")
+            )
+            nc.vector.quantize_mx(
+                out=codes[:, 0:GROUP].bitcast(FP8X4), scales=scales[:, 0:GROUP], in_=quads[:].rearrange("p n t -> p (n t)")
+            )
+
+        def add_pass(step, with_w4=True, with_wd=True, tiles=range(N_TILES)):
+            g, half = step % PASSES, step // PASSES
+            for c in tiles:
+                if (half, c) not in sums:
+                    sums[half, c] = banks.tile([P, HALF], F32, name="bank%d" % VALUE_BANKS[half][c])
                 campaigns = slice(P * c, P * (c + 1))
-                for s0 in range(0, users if with_w4 else 0, w4_cols):
-                    cols = slice(s0, s0 + w4_cols)
+                if with_w4:
                     nc.tensor.matmul_mx(
-                        out=acc[:, s0 : s0 + w4_cols],
+                        out=sums[half, c][:],
                         lhsT=w4_codes[:, g, 2 * P * c : 2 * P * (c + 1)].bitcast(FP4X4),
                         lhsT_scale=w4_scale_tile[:, g, :].bitcast(U8)[:, campaigns],
-                        rhs=codes[:, cols].bitcast(FP8X4),
-                        rhs_scale=scales[:, cols],
-                        start=(g == 0 and c % per_bank == 0 and s0 == 0),
+                        rhs=h_codes[step][:].bitcast(FP8X4),
+                        rhs_scale=h_scales[step][:],
+                        start=(step == PASSES),
                         stop=False,
                     )
                 if with_wd:
                     nc.tensor.matmul_mx(
-                        out=acc,
+                        out=sums[half, c][:],
                         lhsT=wd_codes[g][:, campaigns].bitcast(FP8X4),
                         lhsT_scale=wd_scales[g][:, campaigns],
-                        rhs=codes[:].bitcast(FP8X4),
-                        rhs_scale=scales[:],
+                        rhs=h_codes[step][:].bitcast(FP8X4),
+                        rhs_scale=h_scales[step][:],
                         start=False,
-                        stop=(g == PASSES - 1 and c % per_bank == per_bank - 1),
+                        stop=(g == PASSES - 1),
                     )
 
-        def store(first_user, users, last=False):
-            per_bank = N_TILES // len(sums[first_user])
-            for k in range(N_TILES // per_bank):
-                result = ring.tile([P, per_bank, users], F32, name="result", bufs=6)
-                bank, c0 = sums[first_user][k], per_bank * k
-                if last and k % 2 == 1:
-                    bias = bias_tile[:, c0 : c0 + per_bank].unsqueeze(2).to_broadcast([P, per_bank, users])
-                    nc.vector.tensor_tensor(result[:], bank[:], bias, ALU.add)
-                else:
-                    for c in range(per_bank):
-                        nc.scalar.activation(result[:, c, :], bank[:, c, :], ACT.Identity, bias=bias_tile[:, c0 + c : c0 + c + 1])
-                rows = out[P * c0 : P * (c0 + per_bank), first_user : first_user + users]
-                nc.sync.dma_start(rows.rearrange("(c p) j -> p c j", p=P), result[:])
+        def add_first_pass():
+            for c in range(N_TILES):
+                sums[0, c] = banks.tile([P, HALF], F32, name="bank%d" % VALUE_BANKS[0][c])
+            for cols in (slice(GROUP, HALF), slice(0, GROUP)):
+                for c in range(N_TILES):
+                    campaigns = slice(P * c, P * (c + 1))
+                    nc.tensor.matmul_mx(
+                        out=sums[0, c][:, cols],
+                        lhsT=wd_codes[0][:, campaigns].bitcast(FP8X4),
+                        lhsT_scale=wd_scales[0][:, campaigns],
+                        rhs=h_codes[0][:, cols].bitcast(FP8X4),
+                        rhs_scale=h_scales[0][:, cols],
+                        start=(cols.start == GROUP),
+                        stop=False,
+                    )
+            add_pass(0, with_wd=False)
 
-        load_wd(1, 0, N // 2, under_silu=True)
+        def store(half, on_vector, piece, tiles=range(N_TILES)):
+            for c in tiles:
+                for j0 in range(0, HALF, piece):
+                    name = "result%d_%d_%d" % (half, c, j0)
+                    if (half, c) == (0, N_TILES - 1):
+                        result = shared.tile([P, piece], F32, name=name, align_bytes=256, offset=silu_place(2 * PASSES - 1))
+                    else:
+                        result = keep.tile([P, piece], F32, name=name)
+                    bank = sums[half, c][:, j0 : j0 + piece]
+                    if c in on_vector:
+                        nc.vector.tensor_scalar(result[:], bank, bias_tile[:, c : c + 1], None, ALU.add)
+                    else:
+                        nc.scalar.activation(result[:], bank, ACT.Identity, bias=bias_tile[:, c : c + 1])
+                    nc.sync.dma_start(out[P * c : P * (c + 1), HALF * half + j0 : HALF * half + j0 + piece], result[:])
+
+        def load_w4():
+            for r in range(ROWS):
+                nc.sync.dma_start(
+                    w4_scale_tile[r:P:QUADRANT, :, :], w4_scales[:, r:16:ROWS, :].rearrange("g q c -> q g c").bitcast(I32)
+                )
+            nc.sync.dma_start(w4_codes[:].bitcast(I32), w4_words.rearrange("g p c -> p g c").bitcast(I32))
+
+        def load_bias():
+            with nc.allow_non_contiguous_dma(reason="one bias value to a partition and campaign tile"):
+                nc.sync.dma_start(bias_tile[:], b.rearrange("(c p) -> p c", p=P))
+
+        scored, h_rounded = [], {}
         gather_key_scales()
-        nc.sync.dma_start(bid_tile[:], bid.rearrange("(g p t) -> p g t", g=PASSES, t=PACK))
-        for r in range(ROWS):
-            nc.sync.dma_start(
-                w4_scale_tile[r:P:QUADRANT, :, :], w4_scales[:, r:16:ROWS, :].rearrange("g q c -> q g c").bitcast(I32)
-            )
-        nc.sync.dma_start(w4_codes[:].bitcast(I32), w4_words.rearrange("g p c -> p g c").bitcast(I32))
+        load_wd(1, 0, N // 2)
         load_wd(1, N // 2, N // 2)
-        load_wd(2, 0, N)
-        with nc.allow_non_contiguous_dma(reason="one bias value to a partition and campaign tile"):
-            nc.sync.dma_start(bias_tile[:], b.rearrange("(c p) -> p c", p=P))
+        load_w4()
+        load_wd(2, 0, N // 2)
+        load_wd(2, N // 2, N // 2)
+        load_bias()
+        place_bids()
         nc.vector.tensor_copy(user_scales[:], user_table_scales[:].bitcast(U8).indirect(user_list[:]))
         gather_user_words(0)
         gather_key_words(0)
-        round_wd(0, 0, N, nc.scalar.copy)
-        quantise_wd(0)
-        round_wd(1, 0, N // 2, nc.scalar.copy)
+        rounded_tile(0, 0, 4)
+        round_wd(0, 0, 2, nc.scalar.copy)
+        round_wd(0, 2, 4, nc.scalar.copy)
+        quantise_wd(0, 0)
+        rounded_tile(1, 0, 2)
+        round_wd(1, 0, 1, None)
+        round_wd(1, 1, 2, None)
         gather_key_words(1)
         gather_key_words(2)
         gather_user_words(HALF)
-        last_group = HALF + GROUP
-        make_silu(0, 0, HALF)
-        make_silu(1, 0, HALF)
-        round_wd(1, N // 2, N, nc.scalar.copy)
-        make_silu(2, 0, HALF)
-        make_silu(0, HALF, GROUP)
-        round_wd(2, QUARTER, N, nc.scalar.copy)
-        make_silu(1, HALF, GROUP)
-        make_silu(2, HALF, GROUP)
-        for g in range(PASSES):
-            make_silu(g, last_group, GROUP)
-        make_h(0, 0, HALF)
-        add_pass(0, 0, HALF, range(N_TILES))
-        quantise_wd(1)
-        make_h(1, 0, HALF)
-        add_pass(1, 0, HALF, range(N_TILES))
-        make_h(2, 0, HALF)
-        add_pass(2, 0, HALF, range(N_TILES), with_wd=False)
-        round_wd(2, 0, QUARTER, nc.vector.tensor_copy)
-        quantise_wd(2)
-        add_pass(2, 0, HALF, range(N_TILES), with_w4=False)
-        store(0, HALF)
-        for g in range(PASSES):
-            make_h(g, HALF, GROUP)
-            add_pass(g, HALF, GROUP, (N_TILES, N_TILES + 1))
-        store(HALF, GROUP)
-        for g in range(PASSES):
-            make_h(g, last_group, GROUP, piece=GROUP // 2 if g == PASSES - 1 else GROUP)
-            add_pass(g, last_group, GROUP, range(N_TILES))
-        store(last_group, GROUP, last=True)
+        make_silu(0)
+        make_silu(1)
+        make_silu(2)
+        rounded_tile(2, 0, 4)
+        round_wd(2, 0, 2, nc.scalar.copy)
+        round_wd(2, 2, 4, nc.scalar.copy)
+        make_silu(3)
+        make_silu(4)
+        make_silu(5)
+        multiply(0)
+        quantise_h(0)
+        add_first_pass()
+        multiply(1)
+        rounded_tile(1, 2, 4, 1)
+        round_wd(1, 2, 4, nc.vector.tensor_copy)
+        quantise_wd(1, 0, 1)
+        quantise_wd(1, 2, 1)
+        quantise_h(1)
+        add_pass(1)
+        multiply(2)
+        quantise_wd(2, 0, 2)
+        quantise_h(2)
+        add_pass(2)
+        multiply(3)
+        store(0, (0,), HALF, range(3))
+        quantise_h(3)
+        add_pass(3)
+        for step in range(4, 6):
+            multiply(step)
+            quantise_h(step)
+        store(0, (), HALF, (3,))
+        add_pass(4, tiles=range(3))
+        add_pass(5, tiles=range(2))
+        add_pass(4, tiles=(3,))
+        add_pass(5, tiles=range(2, 4))
+        store(1, (1, 3), GROUP)

@@ -24,18 +24,25 @@ PASSES = S // PASS
 LIST_COLS = PASS // 16
 QUADRANT = 32
 ROWS = 4
-BANK = 512
 HALF = S2 // 2
-GROUP = 256
+GROUP = HALF // 2
+STEPS = 2 * PASSES
+LAST = STEPS - 1
 N_TILES = N // P
-KEY_SCALE_ROW = 4
-KEY_LOAD_ROW = P - 16
 QUARTER = N // 4
-SHARE = 128
-H_BYTES = GROUP * PACK * 2
+KEY_LOAD_ROW = P - 16
+KEY_SCALE_ROW = 4
+BID_STEP = 8
 SILU_BYTES = GROUP * PACK * 4
-VALUE_BANKS = ((0, 1, 2, 3), (4, 0, 1, 2))
-SCORE_BANKS = [4, 5, 6, 0, 1, 2, 3] + [4, 5, 6] * 4 + [5, 6, 5, 6, 5]
+SCORE_BANKS = 3
+TILES_OF_SCORES = 4 * STEPS
+SECOND_HALF_BANKS = (0, 1, 6, 2)
+
+
+def bank_of_scores(index):
+    if SCORE_BANKS <= index < SCORE_BANKS + N_TILES:
+        return index - SCORE_BANKS
+    return N_TILES + (index if index < SCORE_BANKS else index - N_TILES) % SCORE_BANKS
 
 
 def tile_list_keyword_campaign_values_kernel(
@@ -45,7 +52,6 @@ def tile_list_keyword_campaign_values_kernel(
     with ExitStack() as ctx:
         keep = ctx.enter_context(tc.tile_pool(name="keep", bufs=1))
         shared = ctx.enter_context(tc.tile_pool(name="shared", bufs=1))
-        ring = ctx.enter_context(tc.tile_pool(name="ring", bufs=PASSES))
         h_slots = ctx.enter_context(tc.tile_pool(name="h_slots", bufs=1))
         banks = ctx.enter_context(tc.psum_pool(name="banks", bufs=1))
 
@@ -78,7 +84,7 @@ def tile_list_keyword_campaign_values_kernel(
         nc.vector.memset(warm_up[:, 0:1], 0.0)
 
         nc.sync.dma_start(key_list[:], offs)
-        nc.sync.dma_start(key_table_scales[KEY_LOAD_ROW : KEY_LOAD_ROW + 16, :], tab_scales[0].bitcast(I32))
+        nc.sync.dma_start(key_table_scales[KEY_LOAD_ROW:P, :], tab_scales[0].bitcast(I32))
         nc.sync.dma_start(user_list[:], offs2)
         nc.sync.dma_start(user_table[:], tab2_words[0].rearrange("p t i -> p (t i)").bitcast(I32))
         for r in range(ROWS):
@@ -87,20 +93,20 @@ def tile_list_keyword_campaign_values_kernel(
         load_wd(0, 0, N)
         nc.sync.dma_start(key_table[:], tab_words[0].rearrange("p t i -> p (t i)").bitcast(I32))
         nc.sync.dma_start(
-            bid_tile[:, 0 : PASSES * PACK].rearrange("p (g t) -> p g t", t=PACK), bid.rearrange("(g p t) -> p g t", g=PASSES, t=PACK)
+            bid_tile[:, 0 : PASSES * BID_STEP].rearrange("p (g x) -> p g x", x=BID_STEP)[:, :, 0:PACK],
+            bid.rearrange("(g p t) -> p g t", g=PASSES, t=PACK),
         )
 
         user_scales = keep.tile([P, S2], U8, name="user_scales", align_bytes=256)
         key_scales = keep.tile([P, S], U8, name="key_scales", align_bytes=256)
         user_words, key_words, wd_rounded, wd_codes, wd_scales = {}, {}, {}, {}, {}
-        silus, h_codes, h_scales, sums = {}, {}, {}, {}
+        quad_silus, pair_silus, h_rounded, h_codes, h_scales, sums = {}, {}, {}, {}, {}, {}
+        scored = []
 
-        def gather_user_words(first_user):
-            words = keep.tile([P, HALF], U32, name="user_words%d" % first_user, align_bytes=256)
-            for j0 in range(0, HALF, GROUP):
-                user_words[first_user + j0] = words[:, j0 : j0 + GROUP]
-            entries = user_list[:, first_user // 16 : (first_user + HALF) // 16]
-            nc.vector.tensor_copy(words[:], user_table[:].bitcast(U32).indirect(entries))
+        def gather_user_words(half):
+            user_words[half] = keep.tile([P, HALF], U32, name="user_words%d" % half, align_bytes=256)
+            entries = user_list[:, LIST_COLS * half : LIST_COLS * (half + 1)]
+            nc.vector.tensor_copy(user_words[half][:], user_table[:].bitcast(U32).indirect(entries))
 
         def gather_key_scales():
             in_order = keep.tile([P, S], U8, name="key_scales_in_order", align_bytes=256)
@@ -112,9 +118,7 @@ def tile_list_keyword_campaign_values_kernel(
                 )
             as_words = key_scales[:].bitcast(I32)
             for r in range(ROWS):
-                nc.sync.dma_start(
-                    as_words[KEY_SCALE_ROW + r : P : QUADRANT, :], as_words[KEY_LOAD_ROW + r : KEY_LOAD_ROW + 16 : ROWS, :]
-                )
+                nc.sync.dma_start(as_words[KEY_SCALE_ROW + r : P : QUADRANT, :], as_words[KEY_LOAD_ROW + r : P : ROWS, :])
 
         def gather_key_words(g):
             key_words[g] = keep.tile([P, PASS], U32, name="key_words%d" % g, align_bytes=256)
@@ -123,207 +127,200 @@ def tile_list_keyword_campaign_values_kernel(
                 key_words[g][:].rearrange("p (t m) -> p m t", t=PACK), key_table[:].bitcast(U32).indirect(entries)
             )
 
-        def rounded_tile(g, q0, q1, behind_step=None):
+        def quads_place(step):
+            return 2 * SILU_BYTES * step
+
+        def pairs_place(step):
+            return quads_place(step) + SILU_BYTES
+
+        def rounded_tile(g, q0, q1, over_silus=False):
             name, shape = "wd_rounded%d_%d" % (g, q0), [P, QUARTER * (q1 - q0), PACK]
-            if behind_step is None:
-                tile = keep.tile(shape, BF16, name=name, align_bytes=256)
+            if over_silus:
+                tile = shared.tile(shape, BF16, name=name, align_bytes=256, offset=pairs_place(g) + SILU_BYTES // 2)
             else:
-                tile = shared.tile(shape, BF16, name=name, align_bytes=256, offset=silu_place(behind_step) + SILU_BYTES + SILU_BYTES // 2)
+                tile = keep.tile(shape, BF16, name=name, align_bytes=256)
             for q in range(q0, q1):
                 wd_rounded[g, q] = tile, q0, q1
 
-        def round_wd(g, q0, q1, copy):
+        def rounding_operands(g, q0, q1):
             raw, raw0 = wd_raw[g, q0]
-            tile, first, last = wd_rounded[g, q0]
+            tile, first = wd_rounded[g, q0][0:2]
             rounded = tile[:, QUARTER * (q0 - first) : QUARTER * (q1 - first), :]
-            rows = raw[:, :, QUARTER * q0 - raw0 : QUARTER * q1 - raw0]
-            if copy is None:
-                nc.gpsimd.tensor_scalar(rounded, rows.rearrange("p t n -> p n t"), 1.0, 0.0, ALU.mult, ALU.add)
-            else:
-                copy(rounded.rearrange("p (c x) t -> p c t x", x=4), rows.rearrange("p t (c x) -> p c t x", x=4))
+            return rounded, raw[:, :, QUARTER * q0 - raw0 : QUARTER * q1 - raw0]
+
+        def round_wd(g, q0, q1, copy):
+            rounded, rows = rounding_operands(g, q0, q1)
+            copy(rounded.rearrange("p (c x) t -> p c t x", x=4), rows.rearrange("p t (c x) -> p c t x", x=4))
+
+        def round_wd_on_gpsimd(g, q):
+            rounded, rows = rounding_operands(g, q, q + 1)
+            nc.gpsimd.tensor_scalar(rounded, rows.rearrange("p t n -> p n t"), 1.0, 0.0, ALU.mult, ALU.add)
+
+        bid_bank = banks.tile([P, P], F32, name="bid_bank")
+        bid_rows = keep.tile([P, PASSES, P, PACK], F32, name="bid_rows", align_bytes=256)
+
+        def bids_of(tile, g):
+            return tile[:, BID_STEP * g : BID_STEP * g + PACK]
 
         def place_bids():
-            turned = banks.tile([P, P], F32, name="bank4")
+            turned = banks.tile([P, P], F32, name="bank%d" % bank_of_scores(0))
             nc.tensor.transpose(turned[:], bid_tile[:], identity[:])
             turned_copy = keep.tile([P, P], F32, name="bids_turned", align_bytes=256)
             nc.scalar.copy(turned_copy[:], turned[:])
             nc.tensor.transpose(bid_bank[:], turned_copy[:], identity[:])
             for g in range(PASSES):
-                nc.scalar.copy(
-                    bid_rows[:, g, :, :], bid_tile[:, PACK * g : PACK * (g + 1)].unsqueeze(1).to_broadcast([P, SHARE, PACK])
-                )
+                nc.scalar.copy(bid_rows[:, g, :, :], bids_of(bid_tile, g).unsqueeze(1).to_broadcast([P, P, PACK]))
 
-        bid_bank = banks.tile([P, P], F32, name="bid_bank")
-        bid_rows = keep.tile([P, PASSES, SHARE, PACK], F32, name="bid_rows", align_bytes=256)
-
-        def quantise_wd(g, q0, step=None):
+        def quantise_wd(g, q0):
             if g not in wd_codes:
-                if step is None:
-                    wd_codes[g] = keep.tile([P, N], U32, name="wd_codes%d" % g, align_bytes=256)
+                name = "wd_codes%d" % g
+                if g == 0:
+                    wd_codes[g] = keep.tile([P, N], U32, name=name, align_bytes=256)
                 else:
-                    wd_codes[g] = shared.tile([P, N], U32, name="wd_codes%d" % g, align_bytes=256, offset=silu_place(step) + SILU_BYTES)
+                    wd_codes[g] = shared.tile([P, N], U32, name=name, align_bytes=256, offset=pairs_place(g))
                 wd_scales[g] = keep.tile([P, N], U8, name="wd_scales%d" % g, align_bytes=256)
             tile, first, last = wd_rounded[g, q0]
-            n0, n1 = QUARTER * first, QUARTER * last
+            campaigns = slice(QUARTER * first, QUARTER * last)
             nc.vector.quantize_mx(
-                out=wd_codes[g][:, n0:n1].bitcast(FP8X4),
-                scales=wd_scales[g][:, n0:n1],
+                out=wd_codes[g][:, campaigns].bitcast(FP8X4),
+                scales=wd_scales[g][:, campaigns],
                 in_=tile[:].rearrange("p n t -> p (n t)"),
             )
 
-        def silu_place(step):
-            return 2 * SILU_BYTES * step
+        def score_tile(step, slots, user0, users):
+            g, half = step % PASSES, step // PASSES
+            scores = banks.tile([P, len(slots), users], F32, name="bank%d" % bank_of_scores(len(scored)))
+            scored.append(scores)
+            for k, t in enumerate(slots):
+                nc.tensor.matmul_mx(
+                    out=scores[:, k, :],
+                    lhsT=key_words[g][:, P * t : P * (t + 1)].bitcast(FP8X4),
+                    lhsT_scale=key_scales[KEY_SCALE_ROW:P, PASS * g + P * t : PASS * g + P * (t + 1)],
+                    rhs=user_words[half][:, user0 : user0 + users].bitcast(FP8X4),
+                    rhs_scale=user_scales[:, HALF * half + user0 : HALF * half + user0 + users],
+                    start=True,
+                    stop=True,
+                )
+            return scores[:].rearrange("p t n -> p n t")
 
-        def score_bank(shape):
-            bank = banks.tile(shape, F32, name="bank%d" % SCORE_BANKS[len(scored)])
-            scored.append(bank)
-            return bank
+        def score_quad(step, part):
+            if step not in quad_silus:
+                name = "quad_silus%d" % step
+                quad_silus[step] = shared.tile([P, GROUP, PACK], F32, name=name, align_bytes=256, offset=quads_place(step))
+            return quad_silus[step][:, P * part : P * (part + 1), :], score_tile(step, range(PACK), P * part, P)
 
-        def score(out_ap, g, t, user0, users):
-            m0 = P * t
-            half0 = user0 - user0 % GROUP
-            nc.tensor.matmul_mx(
-                out=out_ap,
-                lhsT=key_words[g][:, m0 : m0 + P].bitcast(FP8X4),
-                lhsT_scale=key_scales[KEY_SCALE_ROW:P, PASS * g + m0 : PASS * g + m0 + P],
-                rhs=user_words[half0][:, user0 - half0 : user0 - half0 + users].bitcast(FP8X4),
-                rhs_scale=user_scales[:, user0 : user0 + users],
-                start=True,
-                stop=True,
-            )
+        def score_pair(step, u):
+            if step not in pair_silus:
+                name = "pair_silus%d" % step
+                pair_silus[step] = shared.tile([P, 2, GROUP, 2], F32, name=name, align_bytes=256, offset=pairs_place(step))
+            return pair_silus[step][:, u, :, :], score_tile(step, (2 * u, 2 * u + 1), GROUP, GROUP)
 
-        def silu_of_quad(step, part):
-            g, first_user = step % PASSES, HALF * (step // PASSES)
-            silu = shared.tile([P, P, PACK], F32, name="silu%d_%d" % (step, part), align_bytes=256, offset=silu_place(step) + SILU_BYTES // 2 * part)
-            silus[step, part] = silu
-            scores = score_bank([P, PACK, P])
-            for t in range(PACK):
-                score(scores[:, t, :], g, t, first_user + P * part, P)
-            nc.scalar.activation(silu[:], scores[:].rearrange("p t n -> p n t"), ACT.Silu)
+        def apply_silu(silu_and_scores):
+            nc.scalar.activation(*silu_and_scores, ACT.Silu)
 
-        def silu_of_pairs(step):
-            g, first_user = step % PASSES, HALF * (step // PASSES)
-            silu = shared.tile([P, 2, GROUP, 2], F32, name="silu%d_2" % step, align_bytes=256, offset=silu_place(step) + SILU_BYTES)
-            silus[step, 2] = silu
-            for u in range(2):
-                scores = score_bank([P, 2, GROUP])
-                for e in range(2):
-                    score(scores[:, e, :], g, 2 * u + e, first_user + GROUP, GROUP)
-                nc.scalar.activation(silu[:, u, :, :], scores[:].rearrange("p e n -> p n e"), ACT.Silu)
-
-        def make_silu(step):
-            if step == 0:
-                silu_of_pairs(step)
-            silu_of_quad(step, 0)
+        def make_silus(step):
             if step > 0:
-                silu_of_pairs(step)
-            silu_of_quad(step, 1)
+                apply_silu(score_quad(step, 0))
+            apply_silu(score_pair(step, 0))
+            apply_silu(score_pair(step, 1))
+            if step == 0:
+                apply_silu(score_quad(step, 0))
+            apply_silu(score_quad(step, 1))
 
         def multiply(step):
             g = step % PASSES
             pairs = h_slots.tile([P, GROUP, 2, 2], BF16, name="h_pairs", align_bytes=256)
             quads = h_slots.tile([P, GROUP, PACK], BF16, name="h_quads", align_bytes=256)
             h_rounded[step] = pairs, quads
-            bids = bid_bank[:, PACK * g : PACK * (g + 1)]
-            nc.gpsimd.tensor_tensor(quads[:, 0:SHARE, :], silus[step, 0][:], bid_rows[:, g, :, :], ALU.mult)
+            bids = bids_of(bid_bank, g)
+            nc.gpsimd.tensor_tensor(quads[:, 0:P, :], quad_silus[step][:, 0:P, :], bid_rows[:, g, :, :], ALU.mult)
             nc.vector.tensor_tensor(
                 pairs[:],
-                silus[step, 2][:].rearrange("p u n e -> p n u e"),
+                pair_silus[step][:].rearrange("p u n e -> p n u e"),
                 bids.rearrange("p (u e) -> p u e", u=2).unsqueeze(1).to_broadcast([P, GROUP, 2, 2]),
                 ALU.mult,
             )
-            nc.vector.tensor_tensor(quads[:, SHARE:GROUP, :], silus[step, 1][:], bids.unsqueeze(1).to_broadcast([P, P, PACK]), ALU.mult)
+            nc.vector.tensor_tensor(
+                quads[:, P:GROUP, :], quad_silus[step][:, P:GROUP, :], bids.unsqueeze(1).to_broadcast([P, P, PACK]), ALU.mult
+            )
 
         def quantise_h(step):
             pairs, quads = h_rounded[step]
-            codes = keep.tile([P, HALF], U32, name="h_codes%d" % step, align_bytes=256)
-            scales = keep.tile([P, HALF], U8, name="h_scales%d" % step, align_bytes=256)
-            h_codes[step], h_scales[step] = codes, scales
-            nc.vector.quantize_mx(
-                out=codes[:, GROUP:HALF].bitcast(FP8X4), scales=scales[:, GROUP:HALF], in_=pairs[:].rearrange("p n u e -> p (n u e)")
-            )
-            nc.vector.quantize_mx(
-                out=codes[:, 0:GROUP].bitcast(FP8X4), scales=scales[:, 0:GROUP], in_=quads[:].rearrange("p n t -> p (n t)")
+            h_codes[step] = keep.tile([P, HALF], U32, name="h_codes%d" % step, align_bytes=256)
+            h_scales[step] = keep.tile([P, HALF], U8, name="h_scales%d" % step, align_bytes=256)
+            for users, rounded in (
+                (slice(GROUP, HALF), pairs[:].rearrange("p n u e -> p (n u e)")),
+                (slice(0, GROUP), quads[:].rearrange("p n t -> p (n t)")),
+            ):
+                nc.vector.quantize_mx(out=h_codes[step][:, users].bitcast(FP8X4), scales=h_scales[step][:, users], in_=rounded)
+
+        def add_w4(step, c, opens):
+            g = step % PASSES
+            nc.tensor.matmul_mx(
+                out=sums[step // PASSES, c][:],
+                lhsT=w4_codes[:, g, 2 * P * c : 2 * P * (c + 1)].bitcast(FP4X4),
+                lhsT_scale=w4_scale_tile[:, g, :].bitcast(U8)[:, P * c : P * (c + 1)],
+                rhs=h_codes[step][:].bitcast(FP8X4),
+                rhs_scale=h_scales[step][:],
+                start=opens,
+                stop=False,
             )
 
-        def add_pass(step, with_w4=True, with_wd=True, tiles=range(N_TILES)):
-            g, half = step % PASSES, step // PASSES
-            for c in tiles:
-                if (half, c) not in sums:
-                    sums[half, c] = banks.tile([P, HALF], F32, name="bank%d" % VALUE_BANKS[half][c])
-                campaigns = slice(P * c, P * (c + 1))
-                if with_w4:
-                    nc.tensor.matmul_mx(
-                        out=sums[half, c][:],
-                        lhsT=w4_codes[:, g, 2 * P * c : 2 * P * (c + 1)].bitcast(FP4X4),
-                        lhsT_scale=w4_scale_tile[:, g, :].bitcast(U8)[:, campaigns],
-                        rhs=h_codes[step][:].bitcast(FP8X4),
-                        rhs_scale=h_scales[step][:],
-                        start=(step == PASSES),
-                        stop=False,
-                    )
-                if with_wd:
-                    nc.tensor.matmul_mx(
-                        out=sums[half, c][:],
-                        lhsT=wd_codes[g][:, campaigns].bitcast(FP8X4),
-                        lhsT_scale=wd_scales[g][:, campaigns],
-                        rhs=h_codes[step][:].bitcast(FP8X4),
-                        rhs_scale=h_scales[step][:],
-                        start=False,
-                        stop=(g == PASSES - 1),
-                    )
+        def add_wd(step, c, users, opens):
+            g = step % PASSES
+            nc.tensor.matmul_mx(
+                out=sums[step // PASSES, c][:, users],
+                lhsT=wd_codes[g][:, P * c : P * (c + 1)].bitcast(FP8X4),
+                lhsT_scale=wd_scales[g][:, P * c : P * (c + 1)],
+                rhs=h_codes[step][:, users].bitcast(FP8X4),
+                rhs_scale=h_scales[step][:, users],
+                start=opens,
+                stop=(g == PASSES - 1),
+            )
 
         def add_first_pass():
             for c in range(N_TILES):
-                sums[0, c] = banks.tile([P, HALF], F32, name="bank%d" % VALUE_BANKS[0][c])
-            for cols in (slice(GROUP, HALF), slice(0, GROUP)):
+                sums[0, c] = banks.tile([P, HALF], F32, name="bank%d" % c)
+            for users in (slice(GROUP, HALF), slice(0, GROUP)):
                 for c in range(N_TILES):
-                    campaigns = slice(P * c, P * (c + 1))
-                    nc.tensor.matmul_mx(
-                        out=sums[0, c][:, cols],
-                        lhsT=wd_codes[0][:, campaigns].bitcast(FP8X4),
-                        lhsT_scale=wd_scales[0][:, campaigns],
-                        rhs=h_codes[0][:, cols].bitcast(FP8X4),
-                        rhs_scale=h_scales[0][:, cols],
-                        start=(cols.start == GROUP),
-                        stop=False,
-                    )
-            add_pass(0, with_wd=False)
+                    add_wd(0, c, users, opens=(users.start == GROUP))
+            for c in range(N_TILES):
+                add_w4(0, c, opens=False)
 
-        def store(half, on_vector, piece, tiles=range(N_TILES)):
+        def add_pass(step, tiles=range(N_TILES)):
             for c in tiles:
-                for j0 in range(0, HALF, piece):
-                    name = "result%d_%d_%d" % (half, c, j0)
-                    if (half, c) == (0, N_TILES - 1):
-                        result = shared.tile([P, piece], F32, name=name, align_bytes=256, offset=silu_place(2 * PASSES - 1))
-                    else:
-                        result = keep.tile([P, piece], F32, name=name)
-                    bank = sums[half, c][:, j0 : j0 + piece]
-                    if c in on_vector:
-                        nc.vector.tensor_scalar(result[:], bank, bias_tile[:, c : c + 1], None, ALU.add)
-                    else:
-                        nc.scalar.activation(result[:], bank, ACT.Identity, bias=bias_tile[:, c : c + 1])
-                    nc.sync.dma_start(out[P * c : P * (c + 1), HALF * half + j0 : HALF * half + j0 + piece], result[:])
+                if step == PASSES:
+                    sums[1, c] = banks.tile([P, HALF], F32, name="bank%d" % SECOND_HALF_BANKS[c])
+                add_w4(step, c, opens=(step == PASSES))
+                add_wd(step, c, slice(0, HALF), opens=False)
 
-        def load_w4():
-            for r in range(ROWS):
-                nc.sync.dma_start(
-                    w4_scale_tile[r:P:QUADRANT, :, :], w4_scales[:, r:16:ROWS, :].rearrange("g q c -> q g c").bitcast(I32)
-                )
-            nc.sync.dma_start(w4_codes[:].bitcast(I32), w4_words.rearrange("g p c -> p g c").bitcast(I32))
+        def store(half, c, on_vector=False, piece=HALF):
+            for j0 in range(0, HALF, piece):
+                name = "result%d_%d_%d" % (half, c, j0)
+                if (half, c) == (0, N_TILES - 1):
+                    result = shared.tile([P, piece], F32, name=name, align_bytes=256, offset=quads_place(LAST))
+                else:
+                    result = keep.tile([P, piece], F32, name=name)
+                bank = sums[half, c][:, j0 : j0 + piece]
+                if on_vector:
+                    nc.vector.tensor_scalar(result[:], bank, bias_tile[:, c : c + 1], None, ALU.add)
+                else:
+                    nc.scalar.activation(result[:], bank, ACT.Identity, bias=bias_tile[:, c : c + 1])
+                nc.sync.dma_start(out[P * c : P * (c + 1), HALF * half + j0 : HALF * half + j0 + piece], result[:])
 
-        def load_bias():
-            with nc.allow_non_contiguous_dma(reason="one bias value to a partition and campaign tile"):
-                nc.sync.dma_start(bias_tile[:], b.rearrange("(c p) -> p c", p=P))
-
-        scored, h_rounded = [], {}
         gather_key_scales()
         load_wd(1, 0, N // 2)
         load_wd(1, N // 2, N // 2)
-        load_w4()
+        for r in range(ROWS):
+            nc.sync.dma_start(
+                w4_scale_tile[r:P:QUADRANT, :, :], w4_scales[:, r:16:ROWS, :].rearrange("g q c -> q g c").bitcast(I32)
+            )
+        nc.sync.dma_start(w4_codes[:].bitcast(I32), w4_words.rearrange("g p c -> p g c").bitcast(I32))
         load_wd(2, 0, N // 2)
         load_wd(2, N // 2, N // 2)
-        load_bias()
+        with nc.allow_non_contiguous_dma(reason="one bias value to a partition and campaign tile"):
+            nc.sync.dma_start(bias_tile[:], b.rearrange("(c p) -> p c", p=P))
+
         place_bids()
         nc.vector.tensor_copy(user_scales[:], user_table_scales[:].bitcast(U8).indirect(user_list[:]))
         gather_user_words(0)
@@ -333,44 +330,46 @@ def tile_list_keyword_campaign_values_kernel(
         round_wd(0, 2, 4, nc.scalar.copy)
         quantise_wd(0, 0)
         rounded_tile(1, 0, 2)
-        round_wd(1, 0, 1, None)
-        round_wd(1, 1, 2, None)
+        round_wd_on_gpsimd(1, 0)
+        round_wd_on_gpsimd(1, 1)
         gather_key_words(1)
         gather_key_words(2)
-        gather_user_words(HALF)
-        make_silu(0)
-        make_silu(1)
-        make_silu(2)
-        rounded_tile(2, 0, 4)
+        gather_user_words(1)
+
+        for step in range(PASSES):
+            make_silus(step)
+        rounded_tile(2, 0, 2)
         round_wd(2, 0, 2, nc.scalar.copy)
-        round_wd(2, 2, 4, nc.scalar.copy)
-        make_silu(3)
-        make_silu(4)
-        make_silu(5)
+        for step in range(PASSES, LAST):
+            make_silus(step)
+        last_scores = [score_quad(LAST, 0), score_pair(LAST, 0), score_pair(LAST, 1)]
+
         multiply(0)
         quantise_h(0)
         add_first_pass()
-        multiply(1)
-        rounded_tile(1, 2, 4, 1)
-        round_wd(1, 2, 4, nc.vector.tensor_copy)
-        quantise_wd(1, 0, 1)
-        quantise_wd(1, 2, 1)
-        quantise_h(1)
-        add_pass(1)
-        multiply(2)
-        quantise_wd(2, 0, 2)
-        quantise_h(2)
-        add_pass(2)
-        multiply(3)
-        store(0, (0,), HALF, range(3))
-        quantise_h(3)
-        add_pass(3)
-        for step in range(4, 6):
+        for step in range(1, PASSES):
+            multiply(step)
+            rounded_tile(step, 2, 4, over_silus=True)
+            round_wd(step, 2, 4, nc.vector.tensor_copy)
+            quantise_wd(step, 0)
+            quantise_wd(step, 2)
+            quantise_h(step)
+            add_pass(step)
+        multiply(PASSES)
+        store(0, 0)
+        store(0, 1)
+        quantise_h(PASSES)
+        for silu_and_scores in last_scores:
+            apply_silu(silu_and_scores)
+        store(0, 2)
+        apply_silu(score_quad(LAST, 1))
+        add_pass(PASSES)
+        for step in (LAST - 1, LAST):
             multiply(step)
             quantise_h(step)
-        store(0, (), HALF, (3,))
-        add_pass(4, tiles=range(3))
-        add_pass(5, tiles=range(2))
-        add_pass(4, tiles=(3,))
-        add_pass(5, tiles=range(2, 4))
-        store(1, (1, 3), GROUP)
+        store(0, N_TILES - 1)
+        for tiles in (range(N_TILES - 1), (N_TILES - 1,)):
+            add_pass(LAST - 1, tiles)
+            add_pass(LAST, tiles)
+        for c in range(N_TILES):
+            store(1, c, on_vector=(c % 2 == 1), piece=GROUP)

@@ -29,20 +29,24 @@ GROUP = HALF // 2
 STEPS = 2 * PASSES
 LAST = STEPS - 1
 N_TILES = N // P
-QUARTER = N // 4
+SIDE = N // 2
 KEY_LOAD_ROW = P - 16
 KEY_SCALE_ROW = 4
-BID_STEP = 8
-SILU_BYTES = GROUP * PACK * 4
 SCORE_BANKS = 3
-TILES_OF_SCORES = 4 * STEPS
-SECOND_HALF_BANKS = (0, 1, 6, 2)
+TABLE_AT = STEPS * 8192
+BID_STEP = 8
+SHARE = 160
+SHARES = (128, 128, 128, 128, 128, 128)
+FIRST = (("p", 0), ("q", 0), ("p", 1), ("q", 1))
+WIDE = (("q", 0), ("q", 1), ("p", 0), ("p", 1))
+PLAIN = (("q", 0), ("p", 0), ("p", 1), ("q", 1))
+SECOND_HALF_BANKS = (0, 1, 2, 3)
 
 
 def bank_of_scores(index):
-    if SCORE_BANKS <= index < SCORE_BANKS + N_TILES:
-        return index - SCORE_BANKS
-    return N_TILES + (index if index < SCORE_BANKS else index - N_TILES) % SCORE_BANKS
+    if index < N_TILES:
+        return index
+    return N_TILES + (index - N_TILES) % SCORE_BANKS
 
 
 def tile_list_keyword_campaign_values_kernel(
@@ -57,7 +61,7 @@ def tile_list_keyword_campaign_values_kernel(
 
         key_list = keep.tile([P, S // 16], U16, name="key_list")
         user_list = keep.tile([P, S2 // 16], U16, name="user_list")
-        key_table = keep.tile([P, T], I32, name="key_table", align_bytes=256)
+        key_table = shared.tile([P, T], I32, name="key_table", align_bytes=256, offset=TABLE_AT)
         user_table = keep.tile([P, T2], I32, name="user_table", align_bytes=256)
         key_table_scales = keep.tile([P, T // 4], I32, name="key_table_scales", align_bytes=256)
         user_table_scales = keep.tile([P, T2 // 4], I32, name="user_table_scales", align_bytes=256)
@@ -68,17 +72,15 @@ def tile_list_keyword_campaign_values_kernel(
         bias_tile = keep.tile([P, N_TILES], F32, name="bias_tile")
         wd_raw = {}
 
-        def load_wd(g, n0, width):
-            raw = keep.tile([P, PACK, width], F32, name="wd_raw%d_%d" % (g, n0))
-            for n in range(n0, n0 + width, QUARTER):
-                wd_raw[g, n // QUARTER] = raw, n0
-            rows = wd[PASS * g : PASS * (g + 1), n0 : n0 + width]
-            nc.sync.dma_start(raw[:], rows.rearrange("(p t) n -> p t n", t=PACK))
+        def load_wd(g, side):
+            wd_raw[g, side] = keep.tile([P, PACK, SIDE], F32, name="wd_raw%d_%d" % (g, side), align_bytes=256)
+            rows = wd[PASS * g : PASS * (g + 1), SIDE * side : SIDE * (side + 1)]
+            nc.sync.dma_start(wd_raw[g, side][:], rows.rearrange("(p t) n -> p t n", t=PACK))
 
         nc.vector.memset(user_table_scales[:], 0)
         nc.vector.memset(key_table_scales[0:KEY_LOAD_ROW, :], 0)
-        nc.vector.memset(w4_scale_tile[:], 0)
         nc.vector.memset(bid_tile[:], 0.0)
+        nc.vector.memset(w4_scale_tile[:], 0)
         make_identity(nc, identity[:])
         warm_up = keep.tile([P, 2], F32, name="warm_up")
         nc.vector.memset(warm_up[:, 0:1], 0.0)
@@ -89,13 +91,12 @@ def tile_list_keyword_campaign_values_kernel(
         nc.sync.dma_start(user_table[:], tab2_words[0].rearrange("p t i -> p (t i)").bitcast(I32))
         for r in range(ROWS):
             nc.sync.dma_start(user_table_scales[r:P:QUADRANT, :], tab2_scales[0, r:16:ROWS, :].bitcast(I32))
-        nc.scalar.activation(warm_up[:, 1:2], warm_up[:, 0:1], ACT.Silu)
-        load_wd(0, 0, N)
         nc.sync.dma_start(key_table[:], tab_words[0].rearrange("p t i -> p (t i)").bitcast(I32))
         nc.sync.dma_start(
             bid_tile[:, 0 : PASSES * BID_STEP].rearrange("p (g x) -> p g x", x=BID_STEP)[:, :, 0:PACK],
             bid.rearrange("(g p t) -> p g t", g=PASSES, t=PACK),
         )
+        nc.scalar.activation(warm_up[:, 1:2], warm_up[:, 0:1], ACT.Silu)
 
         user_scales = keep.tile([P, S2], U8, name="user_scales", align_bytes=256)
         key_scales = keep.tile([P, S], U8, name="key_scales", align_bytes=256)
@@ -103,10 +104,16 @@ def tile_list_keyword_campaign_values_kernel(
         quad_silus, pair_silus, h_rounded, h_codes, h_scales, sums = {}, {}, {}, {}, {}, {}
         scored = []
 
-        def gather_user_words(half):
-            user_words[half] = keep.tile([P, HALF], U32, name="user_words%d" % half, align_bytes=256)
-            entries = user_list[:, LIST_COLS * half : LIST_COLS * (half + 1)]
-            nc.vector.tensor_copy(user_words[half][:], user_table[:].bitcast(U32).indirect(entries))
+        def gather_user_words(half, user0, users, offset=None):
+            name = "user_words%d_%d" % (half, user0)
+            if offset is None:
+                words = keep.tile([P, users], U32, name=name, align_bytes=256)
+            else:
+                words = shared.tile([P, users], U32, name=name, align_bytes=256, offset=offset)
+            for u in range(user0, user0 + users, GROUP):
+                user_words[half, u // GROUP] = words[:, u - user0 : u - user0 + GROUP]
+            first = (HALF * half + user0) // 16
+            nc.vector.tensor_copy(words[:], user_table[:].bitcast(U32).indirect(user_list[:, first : first + users // 16]))
 
         def gather_key_scales():
             in_order = keep.tile([P, S], U8, name="key_scales_in_order", align_bytes=256)
@@ -127,35 +134,6 @@ def tile_list_keyword_campaign_values_kernel(
                 key_words[g][:].rearrange("p (t m) -> p m t", t=PACK), key_table[:].bitcast(U32).indirect(entries)
             )
 
-        def quads_place(step):
-            return 2 * SILU_BYTES * step
-
-        def pairs_place(step):
-            return quads_place(step) + SILU_BYTES
-
-        def rounded_tile(g, q0, q1, over_silus=False):
-            name, shape = "wd_rounded%d_%d" % (g, q0), [P, QUARTER * (q1 - q0), PACK]
-            if over_silus:
-                tile = shared.tile(shape, BF16, name=name, align_bytes=256, offset=pairs_place(g) + SILU_BYTES // 2)
-            else:
-                tile = keep.tile(shape, BF16, name=name, align_bytes=256)
-            for q in range(q0, q1):
-                wd_rounded[g, q] = tile, q0, q1
-
-        def rounding_operands(g, q0, q1):
-            raw, raw0 = wd_raw[g, q0]
-            tile, first = wd_rounded[g, q0][0:2]
-            rounded = tile[:, QUARTER * (q0 - first) : QUARTER * (q1 - first), :]
-            return rounded, raw[:, :, QUARTER * q0 - raw0 : QUARTER * q1 - raw0]
-
-        def round_wd(g, q0, q1, copy):
-            rounded, rows = rounding_operands(g, q0, q1)
-            copy(rounded.rearrange("p (c x) t -> p c t x", x=4), rows.rearrange("p t (c x) -> p c t x", x=4))
-
-        def round_wd_on_gpsimd(g, q):
-            rounded, rows = rounding_operands(g, q, q + 1)
-            nc.gpsimd.tensor_scalar(rounded, rows.rearrange("p t n -> p n t"), 1.0, 0.0, ALU.mult, ALU.add)
-
         bid_bank = banks.tile([P, P], F32, name="bid_bank")
         bid_rows = keep.tile([P, PASSES, P, PACK], F32, name="bid_rows", align_bytes=256)
 
@@ -171,20 +149,27 @@ def tile_list_keyword_campaign_values_kernel(
             for g in range(PASSES):
                 nc.scalar.copy(bid_rows[:, g, :, :], bids_of(bid_tile, g).unsqueeze(1).to_broadcast([P, P, PACK]))
 
-        def quantise_wd(g, q0):
-            if g not in wd_codes:
-                name = "wd_codes%d" % g
-                if g == 0:
-                    wd_codes[g] = keep.tile([P, N], U32, name=name, align_bytes=256)
-                else:
-                    wd_codes[g] = shared.tile([P, N], U32, name=name, align_bytes=256, offset=pairs_place(g))
-                wd_scales[g] = keep.tile([P, N], U8, name="wd_scales%d" % g, align_bytes=256)
-            tile, first, last = wd_rounded[g, q0]
-            campaigns = slice(QUARTER * first, QUARTER * last)
+        def round_wd(g, side, copy, offset=None):
+            name, shape = "wd_rounded%d_%d" % (g, side), [P, SIDE, PACK]
+            if offset is None:
+                tile = keep.tile(shape, BF16, name=name, align_bytes=256)
+            else:
+                tile = shared.tile(shape, BF16, name=name, align_bytes=256, offset=offset)
+            wd_rounded[g, side] = tile
+            rows = wd_raw[g, side][:]
+            copy(tile[:].rearrange("p (c x) t -> p c t x", x=4), rows.rearrange("p t (c x) -> p c t x", x=4))
+
+        def quantise_wd(g, side, offset=None):
+            name = "wd_codes%d_%d" % (g, side)
+            if offset is None:
+                wd_codes[g, side] = keep.tile([P, SIDE], U32, name=name, align_bytes=256)
+            else:
+                wd_codes[g, side] = shared.tile([P, SIDE], U32, name=name, align_bytes=256, offset=offset)
+            wd_scales[g, side] = keep.tile([P, SIDE], U8, name="wd_scales%d_%d" % (g, side), align_bytes=256)
             nc.vector.quantize_mx(
-                out=wd_codes[g][:, campaigns].bitcast(FP8X4),
-                scales=wd_scales[g][:, campaigns],
-                in_=tile[:].rearrange("p n t -> p (n t)"),
+                out=wd_codes[g, side][:].bitcast(FP8X4),
+                scales=wd_scales[g, side][:],
+                in_=wd_rounded[g, side][:].rearrange("p n t -> p (n t)"),
             )
 
         def score_tile(step, slots, user0, users):
@@ -196,111 +181,108 @@ def tile_list_keyword_campaign_values_kernel(
                     out=scores[:, k, :],
                     lhsT=key_words[g][:, P * t : P * (t + 1)].bitcast(FP8X4),
                     lhsT_scale=key_scales[KEY_SCALE_ROW:P, PASS * g + P * t : PASS * g + P * (t + 1)],
-                    rhs=user_words[half][:, user0 : user0 + users].bitcast(FP8X4),
+                    rhs=user_words[half, user0 // GROUP][:, user0 % GROUP : user0 % GROUP + users].bitcast(FP8X4),
                     rhs_scale=user_scales[:, HALF * half + user0 : HALF * half + user0 + users],
                     start=True,
                     stop=True,
                 )
             return scores[:].rearrange("p t n -> p n t")
 
-        def score_quad(step, part):
+        SILU_BYTES = GROUP * PACK * 4
+
+        def quads_place(step):
+            return 2 * SILU_BYTES * step
+
+        def pairs_place(step):
+            return quads_place(step) + SILU_BYTES
+
+        def silu_quad(step, part):
             if step not in quad_silus:
-                name = "quad_silus%d" % step
-                quad_silus[step] = shared.tile([P, GROUP, PACK], F32, name=name, align_bytes=256, offset=quads_place(step))
-            return quad_silus[step][:, P * part : P * (part + 1), :], score_tile(step, range(PACK), P * part, P)
+                quad_silus[step] = shared.tile([P, GROUP, PACK], F32, name="quad_silus%d" % step, align_bytes=256, offset=quads_place(step))
+            nc.scalar.activation(quad_silus[step][:, P * part : P * (part + 1), :], score_tile(step, range(PACK), P * part, P), ACT.Silu)
 
-        def score_pair(step, u):
+        def silu_pair(step, u):
             if step not in pair_silus:
-                name = "pair_silus%d" % step
-                pair_silus[step] = shared.tile([P, 2, GROUP, 2], F32, name=name, align_bytes=256, offset=pairs_place(step))
-            return pair_silus[step][:, u, :, :], score_tile(step, (2 * u, 2 * u + 1), GROUP, GROUP)
+                pair_silus[step] = shared.tile([P, 2, GROUP, 2], F32, name="pair_silus%d" % step, align_bytes=256, offset=pairs_place(step))
+            nc.scalar.activation(pair_silus[step][:, u, :, :], score_tile(step, (2 * u, 2 * u + 1), GROUP, GROUP), ACT.Silu)
 
-        def apply_silu(silu_and_scores):
-            nc.scalar.activation(*silu_and_scores, ACT.Silu)
-
-        def make_silus(step):
-            if step > 0:
-                apply_silu(score_quad(step, 0))
-            apply_silu(score_pair(step, 0))
-            apply_silu(score_pair(step, 1))
-            if step == 0:
-                apply_silu(score_quad(step, 0))
-            apply_silu(score_quad(step, 1))
+        def make_silus(step, order):
+            for kind, k in order:
+                if kind == "q":
+                    silu_quad(step, k)
+                else:
+                    silu_pair(step, k)
 
         def multiply(step):
             g = step % PASSES
+            share = SHARES[step]
             pairs = h_slots.tile([P, GROUP, 2, 2], BF16, name="h_pairs", align_bytes=256)
             quads = h_slots.tile([P, GROUP, PACK], BF16, name="h_quads", align_bytes=256)
-            h_rounded[step] = pairs, quads
+            h_rounded[step] = quads, pairs
             bids = bids_of(bid_bank, g)
-            nc.gpsimd.tensor_tensor(quads[:, 0:P, :], quad_silus[step][:, 0:P, :], bid_rows[:, g, :, :], ALU.mult)
+            nc.gpsimd.tensor_tensor(quads[:, 0:share, :], quad_silus[step][:, 0:share, :], bid_rows[:, g, 0:share, :], ALU.mult)
             nc.vector.tensor_tensor(
                 pairs[:],
                 pair_silus[step][:].rearrange("p u n e -> p n u e"),
                 bids.rearrange("p (u e) -> p u e", u=2).unsqueeze(1).to_broadcast([P, GROUP, 2, 2]),
                 ALU.mult,
             )
-            nc.vector.tensor_tensor(
-                quads[:, P:GROUP, :], quad_silus[step][:, P:GROUP, :], bids.unsqueeze(1).to_broadcast([P, P, PACK]), ALU.mult
-            )
-
-        def quantise_h(step):
-            pairs, quads = h_rounded[step]
+            if share < GROUP:
+                nc.vector.tensor_tensor(
+                    quads[:, share:GROUP, :],
+                    quad_silus[step][:, share:GROUP, :],
+                    bids.unsqueeze(1).to_broadcast([P, GROUP - share, PACK]),
+                    ALU.mult,
+                )
             h_codes[step] = keep.tile([P, HALF], U32, name="h_codes%d" % step, align_bytes=256)
             h_scales[step] = keep.tile([P, HALF], U8, name="h_scales%d" % step, align_bytes=256)
-            for users, rounded in (
-                (slice(GROUP, HALF), pairs[:].rearrange("p n u e -> p (n u e)")),
-                (slice(0, GROUP), quads[:].rearrange("p n t -> p (n t)")),
-            ):
-                nc.vector.quantize_mx(out=h_codes[step][:, users].bitcast(FP8X4), scales=h_scales[step][:, users], in_=rounded)
 
-        def add_w4(step, c, opens):
-            g = step % PASSES
+        def quantise_group(step, group):
+            users = slice(GROUP * group, GROUP * (group + 1))
+            rounded = h_rounded[step][group][:]
+            rounded = rounded.rearrange("p n u e -> p (n u e)") if group else rounded.rearrange("p n t -> p (n t)")
+            nc.vector.quantize_mx(out=h_codes[step][:, users].bitcast(FP8X4), scales=h_scales[step][:, users], in_=rounded)
+
+        def quantise_h(step):
+            quantise_group(step, 1)
+            quantise_group(step, 0)
+
+        def opens(step, c):
+            half = step // PASSES
+            if (half, c) in sums:
+                return False
+            sums[half, c] = banks.tile([P, HALF], F32, name="bank%d" % (SECOND_HALF_BANKS[c] if half else c))
+            return True
+
+        def add_w4(step, c):
+            g, half = step % PASSES, step // PASSES
+            first = opens(step, c)
             nc.tensor.matmul_mx(
-                out=sums[step // PASSES, c][:],
+                out=sums[half, c][:],
                 lhsT=w4_codes[:, g, 2 * P * c : 2 * P * (c + 1)].bitcast(FP4X4),
                 lhsT_scale=w4_scale_tile[:, g, :].bitcast(U8)[:, P * c : P * (c + 1)],
                 rhs=h_codes[step][:].bitcast(FP8X4),
                 rhs_scale=h_scales[step][:],
-                start=opens,
+                start=first,
                 stop=False,
             )
 
-        def add_wd(step, c, users, opens):
-            g = step % PASSES
+        def add_wd(step, c, closes):
+            g, side, c0 = step % PASSES, c // 2, P * (c % 2)
+            first = opens(step, c)
             nc.tensor.matmul_mx(
-                out=sums[step // PASSES, c][:, users],
-                lhsT=wd_codes[g][:, P * c : P * (c + 1)].bitcast(FP8X4),
-                lhsT_scale=wd_scales[g][:, P * c : P * (c + 1)],
-                rhs=h_codes[step][:, users].bitcast(FP8X4),
-                rhs_scale=h_scales[step][:, users],
-                start=opens,
-                stop=(g == PASSES - 1),
+                out=sums[step // PASSES, c][:],
+                lhsT=wd_codes[g, side][:, c0 : c0 + P].bitcast(FP8X4),
+                lhsT_scale=wd_scales[g, side][:, c0 : c0 + P],
+                rhs=h_codes[step][:].bitcast(FP8X4),
+                rhs_scale=h_scales[step][:],
+                start=first,
+                stop=closes,
             )
-
-        def add_first_pass():
-            for c in range(N_TILES):
-                sums[0, c] = banks.tile([P, HALF], F32, name="bank%d" % c)
-            for users in (slice(GROUP, HALF), slice(0, GROUP)):
-                for c in range(N_TILES):
-                    add_wd(0, c, users, opens=(users.start == GROUP))
-            for c in range(N_TILES):
-                add_w4(0, c, opens=False)
-
-        def add_pass(step, tiles=range(N_TILES)):
-            for c in tiles:
-                if step == PASSES:
-                    sums[1, c] = banks.tile([P, HALF], F32, name="bank%d" % SECOND_HALF_BANKS[c])
-                add_w4(step, c, opens=(step == PASSES))
-                add_wd(step, c, slice(0, HALF), opens=False)
 
         def store(half, c, on_vector=False, piece=HALF):
             for j0 in range(0, HALF, piece):
-                name = "result%d_%d_%d" % (half, c, j0)
-                if (half, c) == (0, N_TILES - 1):
-                    result = shared.tile([P, piece], F32, name=name, align_bytes=256, offset=quads_place(LAST))
-                else:
-                    result = keep.tile([P, piece], F32, name=name)
+                result = keep.tile([P, piece], F32, name="result%d_%d_%d" % (half, c, j0))
                 bank = sums[half, c][:, j0 : j0 + piece]
                 if on_vector:
                     nc.vector.tensor_scalar(result[:], bank, bias_tile[:, c : c + 1], None, ALU.add)
@@ -309,67 +291,108 @@ def tile_list_keyword_campaign_values_kernel(
                 nc.sync.dma_start(out[P * c : P * (c + 1), HALF * half + j0 : HALF * half + j0 + piece], result[:])
 
         gather_key_scales()
-        load_wd(1, 0, N // 2)
-        load_wd(1, N // 2, N // 2)
+        load_wd(0, 0)
+        load_wd(1, 0)
         for r in range(ROWS):
             nc.sync.dma_start(
                 w4_scale_tile[r:P:QUADRANT, :, :], w4_scales[:, r:16:ROWS, :].rearrange("g q c -> q g c").bitcast(I32)
             )
         nc.sync.dma_start(w4_codes[:].bitcast(I32), w4_words.rearrange("g p c -> p g c").bitcast(I32))
-        load_wd(2, 0, N // 2)
-        load_wd(2, N // 2, N // 2)
+        for g, side in ((2, 0), (0, 1), (1, 1), (2, 1)):
+            load_wd(g, side)
         with nc.allow_non_contiguous_dma(reason="one bias value to a partition and campaign tile"):
             nc.sync.dma_start(bias_tile[:], b.rearrange("(c p) -> p c", p=P))
 
         place_bids()
         nc.vector.tensor_copy(user_scales[:], user_table_scales[:].bitcast(U8).indirect(user_list[:]))
-        gather_user_words(0)
+        gather_user_words(0, 0, HALF)
         gather_key_words(0)
-        rounded_tile(0, 0, 4)
-        round_wd(0, 0, 2, nc.scalar.copy)
-        round_wd(0, 2, 4, nc.scalar.copy)
-        quantise_wd(0, 0)
-        rounded_tile(1, 0, 2)
-        round_wd_on_gpsimd(1, 0)
-        round_wd_on_gpsimd(1, 1)
         gather_key_words(1)
         gather_key_words(2)
-        gather_user_words(1)
+        gather_user_words(1, 0, GROUP, TABLE_AT)
 
-        for step in range(PASSES):
-            make_silus(step)
-        rounded_tile(2, 0, 2)
-        round_wd(2, 0, 2, nc.scalar.copy)
-        for step in range(PASSES, LAST):
-            make_silus(step)
-        last_scores = [score_quad(LAST, 0), score_pair(LAST, 0), score_pair(LAST, 1)]
+        def vector_wd(step, rounds, quantises):
+            for g, side in rounds:
+                round_wd(g, side, nc.vector.tensor_copy, offset=pairs_place(step) + SILU_BYTES // 2)
+            for k, (g, side) in enumerate(quantises):
+                quantise_wd(g, side, offset=pairs_place(step) + 1024 * k)
 
+        def rounded_tile(g, side):
+            if (g, side) not in wd_rounded:
+                wd_rounded[g, side] = keep.tile([P, SIDE, PACK], BF16, name="wd_rounded%d_%d" % (g, side), align_bytes=256)
+            return wd_rounded[g, side]
+
+        def round_on_gpsimd(g, side, n0):
+            rows = wd_raw[g, side][:, :, n0 : n0 + P].rearrange("p t n -> p n t")
+            nc.gpsimd.tensor_scalar(rounded_tile(g, side)[:, n0 : n0 + P, :], rows, 1.0, 0.0, ALU.mult, ALU.add)
+
+        def round_on_scalar(g, side, n0):
+            rows = wd_raw[g, side][:, :, n0 : n0 + P].rearrange("p t (c x) -> p c t x", x=4)
+            nc.scalar.copy(rounded_tile(g, side)[:, n0 : n0 + P, :].rearrange("p (c x) t -> p c t x", x=4), rows)
+
+        def w4_pass(step, tiles=range(N_TILES)):
+            for c in tiles:
+                add_w4(step, c)
+
+        def wd_pass(step, side):
+            for c in (2 * side, 2 * side + 1):
+                add_wd(step, c, closes=(step % PASSES == PASSES - 1))
+
+        round_on_gpsimd(0, 0, 0)
+        round_on_gpsimd(0, 0, P)
+        make_silus(0, FIRST)
+        make_silus(1, PLAIN)
         multiply(0)
+        round_on_gpsimd(1, 0, 0)
+        vector_wd(0, (), ((0, 0),))
         quantise_h(0)
-        add_first_pass()
-        for step in range(1, PASSES):
-            multiply(step)
-            rounded_tile(step, 2, 4, over_silus=True)
-            round_wd(step, 2, 4, nc.vector.tensor_copy)
-            quantise_wd(step, 0)
-            quantise_wd(step, 2)
-            quantise_h(step)
-            add_pass(step)
-        multiply(PASSES)
+        gather_user_words(1, GROUP, GROUP, quads_place(0))
+        round_on_scalar(1, 0, P)
+        make_silus(2, PLAIN)
+        wd_pass(0, 0)
+        w4_pass(0)
+        multiply(1)
+        vector_wd(1, (), ((1, 0),))
+        quantise_h(1)
+        round_wd(2, 0, nc.scalar.copy)
+        make_silus(3, PLAIN)
+        w4_pass(1)
+        wd_pass(1, 0)
+        multiply(2)
+        vector_wd(2, ((0, 1),), ((2, 0), (0, 1)))
+        quantise_h(2)
+        round_wd(1, 1, nc.scalar.copy)
+        make_silus(4, PLAIN)
+        wd_pass(0, 1)
+        for c in (0, 1):
+            add_w4(2, c)
+            add_wd(2, c, closes=True)
+        w4_pass(2, (2, 3))
         store(0, 0)
-        store(0, 1)
-        quantise_h(PASSES)
-        for silu_and_scores in last_scores:
-            apply_silu(silu_and_scores)
+        multiply(3)
+        vector_wd(3, ((2, 1),), ((1, 1), (2, 1)))
+        quantise_h(3)
+        store(0, 1, on_vector=True)
+        make_silus(5, PLAIN)
+        for c in (2, 3):
+            add_wd(1, c, closes=False)
+            add_wd(2, c, closes=True)
         store(0, 2)
-        apply_silu(score_quad(LAST, 1))
-        add_pass(PASSES)
-        for step in (LAST - 1, LAST):
-            multiply(step)
-            quantise_h(step)
-        store(0, N_TILES - 1)
-        for tiles in (range(N_TILES - 1), (N_TILES - 1,)):
-            add_pass(LAST - 1, tiles)
-            add_pass(LAST, tiles)
+        store(0, 3)
+        w4_pass(3, (0, 1))
+        wd_pass(3, 0)
+        multiply(4)
+        quantise_h(4)
+        w4_pass(4, (0, 1))
+        wd_pass(4, 0)
+        multiply(5)
+        quantise_h(5)
+        for c in (0, 1):
+            add_w4(LAST, c)
+            add_wd(LAST, c, closes=True)
+        for c in (2, 3):
+            for step in range(PASSES, STEPS):
+                add_w4(step, c)
+                add_wd(step, c, closes=(step == LAST))
         for c in range(N_TILES):
             store(1, c, on_vector=(c % 2 == 1), piece=GROUP)

@@ -33,14 +33,23 @@ SIDE = N // 2
 KEY_LOAD_ROW = P - 16
 KEY_SCALE_ROW = 4
 SCORE_BANKS = 3
-TABLE_AT = STEPS * 8192
-BID_STEP = 8
-SHARE = 160
-SHARES = (128, 128, 128, 128, 128, 128)
-FIRST = (("p", 0), ("q", 0), ("p", 1), ("q", 1))
-WIDE = (("q", 0), ("q", 1), ("p", 0), ("p", 1))
+BID_ROW = P - PASSES
+SHARES = (256, 160, 160, 160, 160, 160)
+BID_ROW_USERS = 160
+FIRST = (("q", 0), ("p", 0), ("q", 1), ("p", 1))
+WIDE = (("p", 0), ("p", 1), ("q", 0), ("q", 1))
 PLAIN = (("q", 0), ("p", 0), ("p", 1), ("q", 1))
-SECOND_HALF_BANKS = (0, 1, 2, 3)
+SECOND_HALF_BANKS = (6, 4, 5, 0)
+SILU_BYTES = GROUP * PACK * 4
+H_BYTES = GROUP * PACK * 2
+H_PLACE = 2 * SILU_BYTES * STEPS
+PAIR_SLOT = (0, 1, 1, 1, 2, 0)
+QUAD_SLOT = (1, 0, 0, 0, 1, 2)
+CARRIED_PLACE = H_PLACE + 3 * H_BYTES
+LAST_RAW_PLACE = CARRIED_PLACE + H_BYTES
+FIRST_RAW_PLACE = LAST_RAW_PLACE + 2 * SILU_BYTES
+PAIRS_AT = (H_PLACE, FIRST_RAW_PLACE, H_PLACE, LAST_RAW_PLACE, H_PLACE, H_PLACE + H_BYTES)
+QUADS_AT = (H_PLACE + H_BYTES, SILU_BYTES, FIRST_RAW_PLACE, 4 * SILU_BYTES + H_BYTES, LAST_RAW_PLACE, H_PLACE)
 
 
 def bank_of_scores(index):
@@ -56,30 +65,37 @@ def tile_list_keyword_campaign_values_kernel(
     with ExitStack() as ctx:
         keep = ctx.enter_context(tc.tile_pool(name="keep", bufs=1))
         shared = ctx.enter_context(tc.tile_pool(name="shared", bufs=1))
-        h_slots = ctx.enter_context(tc.tile_pool(name="h_slots", bufs=1))
         banks = ctx.enter_context(tc.psum_pool(name="banks", bufs=1))
 
         key_list = keep.tile([P, S // 16], U16, name="key_list")
         user_list = keep.tile([P, S2 // 16], U16, name="user_list")
-        key_table = shared.tile([P, T], I32, name="key_table", align_bytes=256, offset=TABLE_AT)
+        key_table = keep.tile([P, T], I32, name="key_table", align_bytes=256)
         user_table = keep.tile([P, T2], I32, name="user_table", align_bytes=256)
         key_table_scales = keep.tile([P, T // 4], I32, name="key_table_scales", align_bytes=256)
         user_table_scales = keep.tile([P, T2 // 4], I32, name="user_table_scales", align_bytes=256)
         w4_codes = keep.tile([P, PASSES, 2 * N], U8, name="w4_codes", align_bytes=256)
         w4_scale_tile = keep.tile([P, PASSES, N // 4], I32, name="w4_scale_tile", align_bytes=256)
-        bid_tile = keep.tile([P, P], F32, name="bid_tile", align_bytes=256)
+        bid_in_rows = keep.tile([P, PASS], F32, name="bid_in_rows", align_bytes=256)
         identity = keep.tile([P, P], F32, name="identity", align_bytes=256)
         bias_tile = keep.tile([P, N_TILES], F32, name="bias_tile")
         wd_raw = {}
 
-        def load_wd(g, side):
-            wd_raw[g, side] = keep.tile([P, PACK, SIDE], F32, name="wd_raw%d_%d" % (g, side), align_bytes=256)
-            rows = wd[PASS * g : PASS * (g + 1), SIDE * side : SIDE * (side + 1)]
-            nc.sync.dma_start(wd_raw[g, side][:], rows.rearrange("(p t) n -> p t n", t=PACK))
+        def load_wd(g, n0=0, n1=N):
+            name, shape = "wd_raw%d_%d" % (g, n0), [P, PACK, n1 - n0]
+            if g != 1:
+                raw = shared.tile(shape, F32, name=name, align_bytes=256, offset=LAST_RAW_PLACE if g else FIRST_RAW_PLACE)
+            else:
+                raw = keep.tile(shape, F32, name=name, align_bytes=256)
+            for n in range(n0, n1, SIDE):
+                wd_raw[g, n] = raw, n0
+            rows = wd[PASS * g : PASS * (g + 1), n0:n1]
+            nc.sync.dma_start(raw[:], rows.rearrange("(p t) n -> p t n", t=PACK))
 
+        key_scales = keep.tile([P, S // 4], I32, name="key_scales", align_bytes=256)
         nc.vector.memset(user_table_scales[:], 0)
         nc.vector.memset(key_table_scales[0:KEY_LOAD_ROW, :], 0)
-        nc.vector.memset(bid_tile[:], 0.0)
+        nc.vector.memset(bid_in_rows[0:BID_ROW, :], 0.0)
+        nc.vector.memset(key_scales[:], 0)
         nc.vector.memset(w4_scale_tile[:], 0)
         make_identity(nc, identity[:])
         warm_up = keep.tile([P, 2], F32, name="warm_up")
@@ -89,43 +105,45 @@ def tile_list_keyword_campaign_values_kernel(
         nc.sync.dma_start(key_table_scales[KEY_LOAD_ROW:P, :], tab_scales[0].bitcast(I32))
         nc.sync.dma_start(user_list[:], offs2)
         nc.sync.dma_start(user_table[:], tab2_words[0].rearrange("p t i -> p (t i)").bitcast(I32))
+        bid_by_pass = bid.rearrange("(g i) -> g i", g=PASSES)
+        nc.sync.dma_start(bid_in_rows[BID_ROW : BID_ROW + 2, :], bid_by_pass[0:2, :])
+        nc.sync.dma_start(bid_in_rows[BID_ROW + 2 : P, :], bid_by_pass[2:PASSES, :])
         for r in range(ROWS):
             nc.sync.dma_start(user_table_scales[r:P:QUADRANT, :], tab2_scales[0, r:16:ROWS, :].bitcast(I32))
         nc.sync.dma_start(key_table[:], tab_words[0].rearrange("p t i -> p (t i)").bitcast(I32))
-        nc.sync.dma_start(
-            bid_tile[:, 0 : PASSES * BID_STEP].rearrange("p (g x) -> p g x", x=BID_STEP)[:, :, 0:PACK],
-            bid.rearrange("(g p t) -> p g t", g=PASSES, t=PACK),
-        )
+        for r in range(0, 2):
+            nc.sync.dma_start(
+                w4_scale_tile[r:P:QUADRANT, :, :], w4_scales[:, r:16:ROWS, :].rearrange("g q c -> q g c").bitcast(I32)
+            )
         nc.scalar.activation(warm_up[:, 1:2], warm_up[:, 0:1], ACT.Silu)
 
         user_scales = keep.tile([P, S2], U8, name="user_scales", align_bytes=256)
-        key_scales = keep.tile([P, S], U8, name="key_scales", align_bytes=256)
         user_words, key_words, wd_rounded, wd_codes, wd_scales = {}, {}, {}, {}, {}
         quad_silus, pair_silus, h_rounded, h_codes, h_scales, sums = {}, {}, {}, {}, {}, {}
         scored = []
 
-        def gather_user_words(half, user0, users, offset=None):
-            name = "user_words%d_%d" % (half, user0)
-            if offset is None:
-                words = keep.tile([P, users], U32, name=name, align_bytes=256)
+        def gather_user_words(half):
+            name = "user_words%d" % half
+            if half == 0:
+                user_words[half] = keep.tile([P, HALF], U32, name=name, align_bytes=256)
             else:
-                words = shared.tile([P, users], U32, name=name, align_bytes=256, offset=offset)
-            for u in range(user0, user0 + users, GROUP):
-                user_words[half, u // GROUP] = words[:, u - user0 : u - user0 + GROUP]
-            first = (HALF * half + user0) // 16
-            nc.vector.tensor_copy(words[:], user_table[:].bitcast(U32).indirect(user_list[:, first : first + users // 16]))
+                user_words[half] = shared.tile([P, HALF], U32, name=name, align_bytes=256, offset=CARRIED_PLACE)
+            entries = user_list[:, LIST_COLS * half : LIST_COLS * (half + 1)]
+            nc.vector.tensor_copy(user_words[half][:], user_table[:].bitcast(U32).indirect(entries))
 
         def gather_key_scales():
             in_order = keep.tile([P, S], U8, name="key_scales_in_order", align_bytes=256)
+            by_slot = shared.tile([P, S], U8, name="key_scales_by_slot", align_bytes=256, offset=CARRIED_PLACE)
             nc.vector.tensor_copy(in_order[:], key_table_scales[:].bitcast(U8).indirect(key_list[:]))
             for g0, g1 in ((0, 2), (2, PASSES)):
                 nc.vector.tensor_copy(
-                    key_scales[:, PASS * g0 : PASS * g1].rearrange("p (g t m) -> p g t m", t=PACK, m=P),
+                    by_slot[:, PASS * g0 : PASS * g1].rearrange("p (g t m) -> p g t m", t=PACK, m=P),
                     in_order[:, PASS * g0 : PASS * g1].rearrange("p (g m t) -> p g t m", t=PACK, m=P),
                 )
-            as_words = key_scales[:].bitcast(I32)
             for r in range(ROWS):
-                nc.sync.dma_start(as_words[KEY_SCALE_ROW + r : P : QUADRANT, :], as_words[KEY_LOAD_ROW + r : P : ROWS, :])
+                nc.sync.dma_start(
+                    key_scales[KEY_SCALE_ROW + r : P : QUADRANT, :], by_slot[:].bitcast(I32)[KEY_LOAD_ROW + r : P : ROWS, :]
+                )
 
         def gather_key_words(g):
             key_words[g] = keep.tile([P, PASS], U32, name="key_words%d" % g, align_bytes=256)
@@ -134,42 +152,48 @@ def tile_list_keyword_campaign_values_kernel(
                 key_words[g][:].rearrange("p (t m) -> p m t", t=PACK), key_table[:].bitcast(U32).indirect(entries)
             )
 
-        bid_bank = banks.tile([P, P], F32, name="bid_bank")
-        bid_rows = keep.tile([P, PASSES, P, PACK], F32, name="bid_rows", align_bytes=256)
-
-        def bids_of(tile, g):
-            return tile[:, BID_STEP * g : BID_STEP * g + PACK]
+        bid_bank = banks.tile([P, P, PACK], F32, name="bid_bank")
+        bid_rows = keep.tile([P, PASSES, BID_ROW_USERS, PACK], F32, name="bid_rows", align_bytes=256)
 
         def place_bids():
-            turned = banks.tile([P, P], F32, name="bank%d" % bank_of_scores(0))
-            nc.tensor.transpose(turned[:], bid_tile[:], identity[:])
-            turned_copy = keep.tile([P, P], F32, name="bids_turned", align_bytes=256)
-            nc.scalar.copy(turned_copy[:], turned[:])
-            nc.tensor.transpose(bid_bank[:], turned_copy[:], identity[:])
+            for t in range(PACK):
+                nc.tensor.transpose(bid_bank[:, :, t], bid_in_rows[:, t:PASS:PACK], identity[:])
             for g in range(PASSES):
-                nc.scalar.copy(bid_rows[:, g, :, :], bids_of(bid_tile, g).unsqueeze(1).to_broadcast([P, P, PACK]))
+                nc.scalar.copy(bid_rows[:, g, :, :], bid_bank[:, BID_ROW + g, :].unsqueeze(1).to_broadcast([P, BID_ROW_USERS, PACK]))
 
-        def round_wd(g, side, copy, offset=None):
-            name, shape = "wd_rounded%d_%d" % (g, side), [P, SIDE, PACK]
-            if offset is None:
-                tile = keep.tile(shape, BF16, name=name, align_bytes=256)
-            else:
-                tile = shared.tile(shape, BF16, name=name, align_bytes=256, offset=offset)
-            wd_rounded[g, side] = tile
-            rows = wd_raw[g, side][:]
-            copy(tile[:].rearrange("p (c x) t -> p c t x", x=4), rows.rearrange("p t (c x) -> p c t x", x=4))
+        def quads_place(step):
+            return 2 * SILU_BYTES * step
 
-        def quantise_wd(g, side, offset=None):
-            name = "wd_codes%d_%d" % (g, side)
+        def pairs_place(step):
+            return quads_place(step) + SILU_BYTES
+
+        def round_wd(g, n0, n1, copy, offset=None):
+            first = n0
+            if (g, first) not in wd_rounded:
+                name, shape = "wd_rounded%d_%d" % (g, first), [P, SIDE, PACK]
+                if offset is None:
+                    wd_rounded[g, first] = keep.tile(shape, BF16, name=name, align_bytes=256)
+                else:
+                    wd_rounded[g, first] = shared.tile(shape, BF16, name=name, align_bytes=256, offset=offset)
+            copy(
+                wd_rounded[g, first][:, n0 - first : n1 - first, :].rearrange("p (c x) t -> p c t x", x=4),
+                wd_raw[g, n0][0][:, :, n0 - wd_raw[g, n0][1] : n1 - wd_raw[g, n0][1]].rearrange("p t (c x) -> p c t x", x=4),
+            )
+
+        def quantise_wd(g, n0, n1, offset=None):
+            name = "wd_codes%d_%d" % (g, n0)
             if offset is None:
-                wd_codes[g, side] = keep.tile([P, SIDE], U32, name=name, align_bytes=256)
+                codes = keep.tile([P, n1 - n0], U32, name=name, align_bytes=256)
             else:
-                wd_codes[g, side] = shared.tile([P, SIDE], U32, name=name, align_bytes=256, offset=offset)
-            wd_scales[g, side] = keep.tile([P, SIDE], U8, name="wd_scales%d_%d" % (g, side), align_bytes=256)
+                codes = shared.tile([P, n1 - n0], U32, name=name, align_bytes=256, offset=offset)
+            scale_bytes = keep.tile([P, n1 - n0], U8, name="wd_scales%d_%d" % (g, n0), align_bytes=256)
+            for n in range(n0, n1, P):
+                wd_codes[g, n // P] = codes[:, n - n0 : n - n0 + P]
+                wd_scales[g, n // P] = scale_bytes[:, n - n0 : n - n0 + P]
             nc.vector.quantize_mx(
-                out=wd_codes[g, side][:].bitcast(FP8X4),
-                scales=wd_scales[g, side][:],
-                in_=wd_rounded[g, side][:].rearrange("p n t -> p (n t)"),
+                out=codes[:].bitcast(FP8X4),
+                scales=scale_bytes[:],
+                in_=wd_rounded[g, n0][:].rearrange("p n t -> p (n t)"),
             )
 
         def score_tile(step, slots, user0, users):
@@ -180,47 +204,42 @@ def tile_list_keyword_campaign_values_kernel(
                 nc.tensor.matmul_mx(
                     out=scores[:, k, :],
                     lhsT=key_words[g][:, P * t : P * (t + 1)].bitcast(FP8X4),
-                    lhsT_scale=key_scales[KEY_SCALE_ROW:P, PASS * g + P * t : PASS * g + P * (t + 1)],
-                    rhs=user_words[half, user0 // GROUP][:, user0 % GROUP : user0 % GROUP + users].bitcast(FP8X4),
+                    lhsT_scale=key_scales[:].bitcast(U8)[KEY_SCALE_ROW:P, PASS * g + P * t : PASS * g + P * (t + 1)],
+                    rhs=user_words[half][:, user0 : user0 + users].bitcast(FP8X4),
                     rhs_scale=user_scales[:, HALF * half + user0 : HALF * half + user0 + users],
                     start=True,
                     stop=True,
                 )
             return scores[:].rearrange("p t n -> p n t")
 
-        SILU_BYTES = GROUP * PACK * 4
-
-        def quads_place(step):
-            return 2 * SILU_BYTES * step
-
-        def pairs_place(step):
-            return quads_place(step) + SILU_BYTES
-
-        def silu_quad(step, part):
-            if step not in quad_silus:
-                quad_silus[step] = shared.tile([P, GROUP, PACK], F32, name="quad_silus%d" % step, align_bytes=256, offset=quads_place(step))
-            nc.scalar.activation(quad_silus[step][:, P * part : P * (part + 1), :], score_tile(step, range(PACK), P * part, P), ACT.Silu)
-
-        def silu_pair(step, u):
+        def score_part(step, kind, k):
+            if kind == "q":
+                if step not in quad_silus:
+                    quad_silus[step] = shared.tile([P, GROUP, PACK], F32, name="quad_silus%d" % step, align_bytes=256, offset=quads_place(step))
+                return quad_silus[step][:, P * k : P * (k + 1), :], score_tile(step, range(PACK), P * k, P)
             if step not in pair_silus:
                 pair_silus[step] = shared.tile([P, 2, GROUP, 2], F32, name="pair_silus%d" % step, align_bytes=256, offset=pairs_place(step))
-            nc.scalar.activation(pair_silus[step][:, u, :, :], score_tile(step, (2 * u, 2 * u + 1), GROUP, GROUP), ACT.Silu)
+            return pair_silus[step][:, k, :, :], score_tile(step, (2 * k, 2 * k + 1), GROUP, GROUP)
+
+        def apply_silu(silu_and_scores):
+            nc.scalar.activation(silu_and_scores[0], silu_and_scores[1], ACT.Silu)
 
         def make_silus(step, order):
             for kind, k in order:
-                if kind == "q":
-                    silu_quad(step, k)
-                else:
-                    silu_pair(step, k)
+                apply_silu(score_part(step, kind, k))
 
         def multiply(step):
             g = step % PASSES
             share = SHARES[step]
-            pairs = h_slots.tile([P, GROUP, 2, 2], BF16, name="h_pairs", align_bytes=256)
-            quads = h_slots.tile([P, GROUP, PACK], BF16, name="h_quads", align_bytes=256)
+            pairs = shared.tile([P, GROUP, 2, 2], BF16, name="h_pairs%d" % step, align_bytes=256, offset=PAIRS_AT[step])
+            quads = shared.tile([P, GROUP, PACK], BF16, name="h_quads%d" % step, align_bytes=256, offset=QUADS_AT[step])
             h_rounded[step] = quads, pairs
-            bids = bids_of(bid_bank, g)
-            nc.gpsimd.tensor_tensor(quads[:, 0:share, :], quad_silus[step][:, 0:share, :], bid_rows[:, g, 0:share, :], ALU.mult)
+            bids = bid_bank[:, BID_ROW + g, :]
+            piece = P if share == GROUP else share
+            for u in range(0, share, piece):
+                nc.gpsimd.tensor_tensor(
+                    quads[:, u : u + piece, :], quad_silus[step][:, u : u + piece, :], bid_rows[:, g, 0:piece, :], ALU.mult
+                )
             nc.vector.tensor_tensor(
                 pairs[:],
                 pair_silus[step][:].rearrange("p u n e -> p n u e"),
@@ -268,12 +287,12 @@ def tile_list_keyword_campaign_values_kernel(
             )
 
         def add_wd(step, c, closes):
-            g, side, c0 = step % PASSES, c // 2, P * (c % 2)
+            g = step % PASSES
             first = opens(step, c)
             nc.tensor.matmul_mx(
                 out=sums[step // PASSES, c][:],
-                lhsT=wd_codes[g, side][:, c0 : c0 + P].bitcast(FP8X4),
-                lhsT_scale=wd_scales[g, side][:, c0 : c0 + P],
+                lhsT=wd_codes[g, c].bitcast(FP8X4),
+                lhsT_scale=wd_scales[g, c],
                 rhs=h_codes[step][:].bitcast(FP8X4),
                 rhs_scale=h_scales[step][:],
                 start=first,
@@ -291,108 +310,82 @@ def tile_list_keyword_campaign_values_kernel(
                 nc.sync.dma_start(out[P * c : P * (c + 1), HALF * half + j0 : HALF * half + j0 + piece], result[:])
 
         gather_key_scales()
-        load_wd(0, 0)
-        load_wd(1, 0)
-        for r in range(ROWS):
+        nc.sync.dma_start(w4_codes[:].bitcast(I32), w4_words.rearrange("g p c -> p g c").bitcast(I32))
+        for r in range(2, 4):
             nc.sync.dma_start(
                 w4_scale_tile[r:P:QUADRANT, :, :], w4_scales[:, r:16:ROWS, :].rearrange("g q c -> q g c").bitcast(I32)
             )
-        nc.sync.dma_start(w4_codes[:].bitcast(I32), w4_words.rearrange("g p c -> p g c").bitcast(I32))
-        for g, side in ((2, 0), (0, 1), (1, 1), (2, 1)):
-            load_wd(g, side)
+        load_wd(0)
+        load_wd(1, 0, SIDE)
+        load_wd(1, SIDE, N)
+        load_wd(2)
         with nc.allow_non_contiguous_dma(reason="one bias value to a partition and campaign tile"):
             nc.sync.dma_start(bias_tile[:], b.rearrange("(c p) -> p c", p=P))
 
         place_bids()
+        gather_user_words(0)
         nc.vector.tensor_copy(user_scales[:], user_table_scales[:].bitcast(U8).indirect(user_list[:]))
-        gather_user_words(0, 0, HALF)
-        gather_key_words(0)
-        gather_key_words(1)
-        gather_key_words(2)
-        gather_user_words(1, 0, GROUP, TABLE_AT)
+        for g in range(PASSES):
+            gather_key_words(g)
+        gather_user_words(1)
 
-        def vector_wd(step, rounds, quantises):
-            for g, side in rounds:
-                round_wd(g, side, nc.vector.tensor_copy, offset=pairs_place(step) + SILU_BYTES // 2)
-            for k, (g, side) in enumerate(quantises):
-                quantise_wd(g, side, offset=pairs_place(step) + 1024 * k)
-
-        def rounded_tile(g, side):
-            if (g, side) not in wd_rounded:
-                wd_rounded[g, side] = keep.tile([P, SIDE, PACK], BF16, name="wd_rounded%d_%d" % (g, side), align_bytes=256)
-            return wd_rounded[g, side]
-
-        def round_on_gpsimd(g, side, n0):
-            rows = wd_raw[g, side][:, :, n0 : n0 + P].rearrange("p t n -> p n t")
-            nc.gpsimd.tensor_scalar(rounded_tile(g, side)[:, n0 : n0 + P, :], rows, 1.0, 0.0, ALU.mult, ALU.add)
-
-        def round_on_scalar(g, side, n0):
-            rows = wd_raw[g, side][:, :, n0 : n0 + P].rearrange("p t (c x) -> p c t x", x=4)
-            nc.scalar.copy(rounded_tile(g, side)[:, n0 : n0 + P, :].rearrange("p (c x) t -> p c t x", x=4), rows)
-
-        def w4_pass(step, tiles=range(N_TILES)):
-            for c in tiles:
+        def w4_pass(step):
+            for c in range(N_TILES):
                 add_w4(step, c)
 
-        def wd_pass(step, side):
-            for c in (2 * side, 2 * side + 1):
+        def wd_pass(step):
+            for c in range(N_TILES):
                 add_wd(step, c, closes=(step % PASSES == PASSES - 1))
 
-        round_on_gpsimd(0, 0, 0)
-        round_on_gpsimd(0, 0, P)
         make_silus(0, FIRST)
-        make_silus(1, PLAIN)
+        make_silus(1, WIDE)
+        make_silus(2, WIDE)
+        round_wd(1, 0, SIDE, nc.scalar.copy)
+        make_silus(3, WIDE)
+        round_wd(1, SIDE, N, nc.scalar.copy)
+        make_silus(4, WIDE)
+        make_silus(LAST, WIDE)
         multiply(0)
-        round_on_gpsimd(1, 0, 0)
-        vector_wd(0, (), ((0, 0),))
-        quantise_h(0)
-        gather_user_words(1, GROUP, GROUP, quads_place(0))
-        round_on_scalar(1, 0, P)
-        make_silus(2, PLAIN)
-        wd_pass(0, 0)
+        quantise_group(0, 0)
+        quantise_group(0, 1)
+        round_wd(0, 0, SIDE, nc.vector.tensor_copy, offset=pairs_place(0))
+        round_wd(0, SIDE, N, nc.vector.tensor_copy, offset=pairs_place(0) + H_BYTES)
+        quantise_wd(0, 0, SIDE)
+        quantise_wd(0, SIDE, N)
         w4_pass(0)
+        wd_pass(0)
         multiply(1)
-        vector_wd(1, (), ((1, 0),))
         quantise_h(1)
-        round_wd(2, 0, nc.scalar.copy)
-        make_silus(3, PLAIN)
         w4_pass(1)
-        wd_pass(1, 0)
         multiply(2)
-        vector_wd(2, ((0, 1),), ((2, 0), (0, 1)))
         quantise_h(2)
-        round_wd(1, 1, nc.scalar.copy)
-        make_silus(4, PLAIN)
-        wd_pass(0, 1)
-        for c in (0, 1):
-            add_w4(2, c)
-            add_wd(2, c, closes=True)
-        w4_pass(2, (2, 3))
-        store(0, 0)
+        quantise_wd(1, 0, SIDE, offset=quads_place(2))
+        round_wd(2, 0, SIDE, nc.vector.tensor_copy, offset=pairs_place(2))
+        round_wd(2, SIDE, N, nc.vector.tensor_copy, offset=quads_place(2) + H_BYTES)
+        quantise_wd(2, 0, SIDE)
+        quantise_wd(2, SIDE, N)
+        quantise_wd(1, SIDE, N, offset=LAST_RAW_PLACE + H_BYTES)
+        w4_pass(2)
+        for g in (1, 2):
+            for c in (0, 1):
+                add_wd(g, c, closes=(g == 2))
+        for g in (2, 1):
+            for c in (2, 3):
+                add_wd(g, c, closes=(g == 1))
+        for c in range(N_TILES):
+            store(0, c)
         multiply(3)
-        vector_wd(3, ((2, 1),), ((1, 1), (2, 1)))
         quantise_h(3)
-        store(0, 1, on_vector=True)
-        make_silus(5, PLAIN)
-        for c in (2, 3):
-            add_wd(1, c, closes=False)
-            add_wd(2, c, closes=True)
-        store(0, 2)
-        store(0, 3)
-        w4_pass(3, (0, 1))
-        wd_pass(3, 0)
-        multiply(4)
-        quantise_h(4)
-        w4_pass(4, (0, 1))
-        wd_pass(4, 0)
-        multiply(5)
-        quantise_h(5)
-        for c in (0, 1):
-            add_w4(LAST, c)
-            add_wd(LAST, c, closes=True)
-        for c in (2, 3):
-            for step in range(PASSES, STEPS):
-                add_w4(step, c)
-                add_wd(step, c, closes=(step == LAST))
+        for c in range(N_TILES):
+            add_w4(3, c)
+            add_wd(3, c, closes=False)
+        for step in (4, 5):
+            multiply(step)
+            quantise_h(step)
+        for tiles in (range(N_TILES - 1), (N_TILES - 1,)):
+            for step in (4, 5):
+                for c in tiles:
+                    add_w4(step, c)
+                    add_wd(step, c, closes=(step == LAST))
         for c in range(N_TILES):
             store(1, c, on_vector=(c % 2 == 1), piece=GROUP)

@@ -46,7 +46,7 @@ H_PLACE = 2 * SILU_BYTES * STEPS
 PAIR_SLOT = (0, 1, 1, 1, 2, 0)
 QUAD_SLOT = (1, 0, 0, 0, 1, 2)
 CARRIED_PLACE = H_PLACE + 3 * H_BYTES
-LAST_RAW_PLACE = CARRIED_PLACE + H_BYTES
+LAST_RAW_PLACE = CARRIED_PLACE + 3 * H_BYTES
 FIRST_RAW_PLACE = LAST_RAW_PLACE + 2 * SILU_BYTES
 PAIRS_AT = (H_PLACE, FIRST_RAW_PLACE, H_PLACE, LAST_RAW_PLACE, H_PLACE, H_PLACE + H_BYTES)
 QUADS_AT = (H_PLACE + H_BYTES, SILU_BYTES, FIRST_RAW_PLACE, 4 * SILU_BYTES + H_BYTES, LAST_RAW_PLACE, H_PLACE)
@@ -104,13 +104,13 @@ def tile_list_keyword_campaign_values_kernel(
         nc.sync.dma_start(key_list[:], offs)
         nc.sync.dma_start(key_table_scales[KEY_LOAD_ROW:P, :], tab_scales[0].bitcast(I32))
         nc.sync.dma_start(user_list[:], offs2)
-        nc.sync.dma_start(user_table[:], tab2_words[0].rearrange("p t i -> p (t i)").bitcast(I32))
-        bid_by_pass = bid.rearrange("(g i) -> g i", g=PASSES)
-        nc.sync.dma_start(bid_in_rows[BID_ROW : BID_ROW + 2, :], bid_by_pass[0:2, :])
-        nc.sync.dma_start(bid_in_rows[BID_ROW + 2 : P, :], bid_by_pass[2:PASSES, :])
         for r in range(ROWS):
             nc.sync.dma_start(user_table_scales[r:P:QUADRANT, :], tab2_scales[0, r:16:ROWS, :].bitcast(I32))
         nc.sync.dma_start(key_table[:], tab_words[0].rearrange("p t i -> p (t i)").bitcast(I32))
+        bid_by_pass = bid.rearrange("(g i) -> g i", g=PASSES)
+        nc.sync.dma_start(bid_in_rows[BID_ROW : BID_ROW + 2, :], bid_by_pass[0:2, :])
+        nc.sync.dma_start(bid_in_rows[BID_ROW + 2 : P, :], bid_by_pass[2:PASSES, :])
+        nc.sync.dma_start(user_table[:], tab2_words[0].rearrange("p t i -> p (t i)").bitcast(I32))
         for r in range(0, 2):
             nc.sync.dma_start(
                 w4_scale_tile[r:P:QUADRANT, :, :], w4_scales[:, r:16:ROWS, :].rearrange("g q c -> q g c").bitcast(I32)
@@ -122,19 +122,24 @@ def tile_list_keyword_campaign_values_kernel(
         quad_silus, pair_silus, h_rounded, h_codes, h_scales, sums = {}, {}, {}, {}, {}, {}
         scored = []
 
+        in_order = keep.tile([P, S], U8, name="key_scales_in_order", align_bytes=256)
+
         def gather_user_words(half):
             name = "user_words%d" % half
             if half == 0:
                 user_words[half] = keep.tile([P, HALF], U32, name=name, align_bytes=256)
             else:
-                user_words[half] = shared.tile([P, HALF], U32, name=name, align_bytes=256, offset=CARRIED_PLACE)
-            entries = user_list[:, LIST_COLS * half : LIST_COLS * (half + 1)]
-            nc.vector.tensor_copy(user_words[half][:], user_table[:].bitcast(U32).indirect(entries))
+                user_words[half] = shared.tile([P, HALF], U32, name=name, align_bytes=256, offset=CARRIED_PLACE + 2 * H_BYTES)
+            piece = HALF if half else GROUP
+            for u in range(0, HALF, piece):
+                entries = user_list[:, (HALF * half + u) // 16 : (HALF * half + u + piece) // 16]
+                nc.vector.tensor_copy(user_words[half][:, u : u + piece], user_table[:].bitcast(U32).indirect(entries))
 
         def gather_key_scales():
-            in_order = keep.tile([P, S], U8, name="key_scales_in_order", align_bytes=256)
-            by_slot = shared.tile([P, S], U8, name="key_scales_by_slot", align_bytes=256, offset=CARRIED_PLACE)
-            nc.vector.tensor_copy(in_order[:], key_table_scales[:].bitcast(U8).indirect(key_list[:]))
+            by_slot = shared.tile([P, 3 * H_BYTES], U8, name="key_scales_by_slot", align_bytes=256, offset=CARRIED_PLACE)
+            for g0, g1 in ((0, 2), (2, PASSES)):
+                entries = key_list[:, LIST_COLS * g0 : LIST_COLS * g1]
+                nc.vector.tensor_copy(in_order[:, PASS * g0 : PASS * g1], key_table_scales[:].bitcast(U8).indirect(entries))
             for g0, g1 in ((0, 2), (2, PASSES)):
                 nc.vector.tensor_copy(
                     by_slot[:, PASS * g0 : PASS * g1].rearrange("p (g t m) -> p g t m", t=PACK, m=P),
@@ -142,11 +147,15 @@ def tile_list_keyword_campaign_values_kernel(
                 )
             for r in range(ROWS):
                 nc.sync.dma_start(
-                    key_scales[KEY_SCALE_ROW + r : P : QUADRANT, :], by_slot[:].bitcast(I32)[KEY_LOAD_ROW + r : P : ROWS, :]
+                    key_scales[KEY_SCALE_ROW + r : P : QUADRANT, :], by_slot[:, 0:S].bitcast(I32)[KEY_LOAD_ROW + r : P : ROWS, :]
                 )
 
         def gather_key_words(g):
-            key_words[g] = keep.tile([P, PASS], U32, name="key_words%d" % g, align_bytes=256)
+            if g == 0:
+                key_words[g] = keep.tile([P, PASS], U32, name="key_words0", align_bytes=256)
+            else:
+                place = CARRIED_PLACE + H_BYTES * (g - 1)
+                key_words[g] = shared.tile([P, PASS], U32, name="key_words%d" % g, align_bytes=256, offset=place)
             entries = key_list[:, LIST_COLS * g : LIST_COLS * (g + 1)]
             nc.vector.tensor_copy(
                 key_words[g][:].rearrange("p (t m) -> p m t", t=PACK), key_table[:].bitcast(U32).indirect(entries)
@@ -323,10 +332,11 @@ def tile_list_keyword_campaign_values_kernel(
             nc.sync.dma_start(bias_tile[:], b.rearrange("(c p) -> p c", p=P))
 
         place_bids()
-        gather_user_words(0)
         nc.vector.tensor_copy(user_scales[:], user_table_scales[:].bitcast(U8).indirect(user_list[:]))
-        for g in range(PASSES):
-            gather_key_words(g)
+        gather_key_words(0)
+        gather_user_words(0)
+        gather_key_words(1)
+        gather_key_words(2)
         gather_user_words(1)
 
         def w4_pass(step):

@@ -21,35 +21,53 @@ P = 128
 PACK = 4
 PASS = P * PACK
 PASSES = S // PASS
-LIST_COLS = PASS // 16
+ENTRIES = 16
 QUADRANT = 32
 ROWS = 4
 HALF = S2 // 2
 GROUP = HALF // 2
+QUADS, PAIRS = 0, 1
 STEPS = 2 * PASSES
 LAST = STEPS - 1
 N_TILES = N // P
 SIDE = N // 2
 KEY_LOAD_ROW = P - 16
 KEY_SCALE_ROW = 4
-SCORE_BANKS = 3
 BID_ROW = P - PASSES
-SHARES = (256, 160, 160, 160, 160, 160)
-BID_ROW_USERS = 160
-FIRST = (("q", 0), ("p", 0), ("q", 1), ("p", 1))
-WIDE = (("p", 0), ("p", 1), ("q", 0), ("q", 1))
-PLAIN = (("q", 0), ("p", 0), ("p", 1), ("q", 1))
+SHARE = 160
+H_SCALE_SHIFT, WD_SCALE_SHIFT = 128, 64
+FIRST_ORDER = ((QUADS, 0), (PAIRS, 0), (QUADS, 1), (PAIRS, 1))
+ORDER = ((PAIRS, 0), (PAIRS, 1), (QUADS, 0), (QUADS, 1))
+SCORE_BANKS = 3
 SECOND_HALF_BANKS = (6, 4, 5, 0)
+
 SILU_BYTES = GROUP * PACK * 4
-H_BYTES = GROUP * PACK * 2
+PIECE = GROUP * PACK * 2
 H_PLACE = 2 * SILU_BYTES * STEPS
-PAIR_SLOT = (0, 1, 1, 1, 2, 0)
-QUAD_SLOT = (1, 0, 0, 0, 1, 2)
-CARRIED_PLACE = H_PLACE + 3 * H_BYTES
-LAST_RAW_PLACE = CARRIED_PLACE + 3 * H_BYTES
-FIRST_RAW_PLACE = LAST_RAW_PLACE + 2 * SILU_BYTES
-PAIRS_AT = (H_PLACE, FIRST_RAW_PLACE, H_PLACE, LAST_RAW_PLACE, H_PLACE, H_PLACE + H_BYTES)
-QUADS_AT = (H_PLACE + H_BYTES, SILU_BYTES, FIRST_RAW_PLACE, 4 * SILU_BYTES + H_BYTES, LAST_RAW_PLACE, H_PLACE)
+CARRIED_PLACE = H_PLACE + 3 * PIECE
+RAW_PLACE = {2: CARRIED_PLACE + 3 * PIECE, 0: CARRIED_PLACE + 7 * PIECE}
+
+
+def silus_place(step, group):
+    return SILU_BYTES * (2 * step + group)
+
+
+QUADS_PLACE = (
+    H_PLACE + PIECE,
+    silus_place(0, PAIRS),
+    RAW_PLACE[0],
+    silus_place(2, QUADS) + PIECE,
+    RAW_PLACE[2],
+    H_PLACE,
+)
+PAIRS_PLACE = (
+    H_PLACE,
+    RAW_PLACE[0],
+    H_PLACE,
+    RAW_PLACE[2],
+    H_PLACE,
+    H_PLACE + PIECE,
+)
 
 
 def bank_of_scores(index):
@@ -67,8 +85,13 @@ def tile_list_keyword_campaign_values_kernel(
         shared = ctx.enter_context(tc.tile_pool(name="shared", bufs=1))
         banks = ctx.enter_context(tc.psum_pool(name="banks", bufs=1))
 
-        key_list = keep.tile([P, S // 16], U16, name="key_list")
-        user_list = keep.tile([P, S2 // 16], U16, name="user_list")
+        def tile_at(place, name, shape, dtype):
+            if place is None:
+                return keep.tile(shape, dtype, name=name, align_bytes=256)
+            return shared.tile(shape, dtype, name=name, align_bytes=256, offset=place)
+
+        key_list = keep.tile([P, S // ENTRIES], U16, name="key_list")
+        user_list = keep.tile([P, S2 // ENTRIES], U16, name="user_list")
         key_table = keep.tile([P, T], I32, name="key_table", align_bytes=256)
         user_table = keep.tile([P, T2], I32, name="user_table", align_bytes=256)
         key_table_scales = keep.tile([P, T // 4], I32, name="key_table_scales", align_bytes=256)
@@ -78,20 +101,23 @@ def tile_list_keyword_campaign_values_kernel(
         bid_in_rows = keep.tile([P, PASS], F32, name="bid_in_rows", align_bytes=256)
         identity = keep.tile([P, P], F32, name="identity", align_bytes=256)
         bias_tile = keep.tile([P, N_TILES], F32, name="bias_tile")
+        key_scales = keep.tile([P, S // 4], I32, name="key_scales", align_bytes=256)
         wd_raw = {}
 
-        def load_wd(g, n0=0, n1=N):
-            name, shape = "wd_raw%d_%d" % (g, n0), [P, PACK, n1 - n0]
-            if g != 1:
-                raw = shared.tile(shape, F32, name=name, align_bytes=256, offset=LAST_RAW_PLACE if g else FIRST_RAW_PLACE)
-            else:
-                raw = keep.tile(shape, F32, name=name, align_bytes=256)
-            for n in range(n0, n1, SIDE):
-                wd_raw[g, n] = raw, n0
-            rows = wd[PASS * g : PASS * (g + 1), n0:n1]
+        def load_wd(g, sides):
+            n0, width = SIDE * sides[0], SIDE * len(sides)
+            raw = tile_at(RAW_PLACE.get(g), "wd_raw%d_%d" % (g, n0), [P, PACK, width], F32)
+            for k, side in enumerate(sides):
+                wd_raw[g, side] = raw[:, :, SIDE * k : SIDE * (k + 1)]
+            rows = wd[PASS * g : PASS * (g + 1), n0 : n0 + width]
             nc.sync.dma_start(raw[:], rows.rearrange("(p t) n -> p t n", t=PACK))
 
-        key_scales = keep.tile([P, S // 4], I32, name="key_scales", align_bytes=256)
+        def load_w4_scales(rows):
+            for r in rows:
+                nc.sync.dma_start(
+                    w4_scale_tile[r:P:QUADRANT, :, :], w4_scales[:, r:16:ROWS, :].rearrange("g q c -> q g c").bitcast(I32)
+                )
+
         nc.vector.memset(user_table_scales[:], 0)
         nc.vector.memset(key_table_scales[0:KEY_LOAD_ROW, :], 0)
         nc.vector.memset(bid_in_rows[0:BID_ROW, :], 0.0)
@@ -111,200 +137,153 @@ def tile_list_keyword_campaign_values_kernel(
         nc.sync.dma_start(bid_in_rows[BID_ROW : BID_ROW + 2, :], bid_by_pass[0:2, :])
         nc.sync.dma_start(bid_in_rows[BID_ROW + 2 : P, :], bid_by_pass[2:PASSES, :])
         nc.sync.dma_start(user_table[:], tab2_words[0].rearrange("p t i -> p (t i)").bitcast(I32))
-        for r in range(0, 2):
-            nc.sync.dma_start(
-                w4_scale_tile[r:P:QUADRANT, :, :], w4_scales[:, r:16:ROWS, :].rearrange("g q c -> q g c").bitcast(I32)
-            )
+        load_w4_scales(range(0, ROWS // 2))
         nc.scalar.activation(warm_up[:, 1:2], warm_up[:, 0:1], ACT.Silu)
 
         user_scales = keep.tile([P, S2], U8, name="user_scales", align_bytes=256)
+        key_scales_in_order = keep.tile([P, S], U8, name="key_scales_in_order", align_bytes=256)
         user_words, key_words, wd_rounded, wd_codes, wd_scales = {}, {}, {}, {}, {}
-        quad_silus, pair_silus, h_rounded, h_codes, h_scales, sums = {}, {}, {}, {}, {}, {}
+        silus, h_rounded, h_codes, h_scales, sums = {}, {}, {}, {}, {}
         scored = []
 
-        in_order = keep.tile([P, S], U8, name="key_scales_in_order", align_bytes=256)
-
-        def gather_user_words(half):
-            name = "user_words%d" % half
-            if half == 0:
-                user_words[half] = keep.tile([P, HALF], U32, name=name, align_bytes=256)
-            else:
-                user_words[half] = shared.tile([P, HALF], U32, name=name, align_bytes=256, offset=CARRIED_PLACE + 2 * H_BYTES)
-            piece = HALF if half else GROUP
-            for u in range(0, HALF, piece):
-                entries = user_list[:, (HALF * half + u) // 16 : (HALF * half + u + piece) // 16]
-                nc.vector.tensor_copy(user_words[half][:, u : u + piece], user_table[:].bitcast(U32).indirect(entries))
-
         def gather_key_scales():
-            by_slot = shared.tile([P, 3 * H_BYTES], U8, name="key_scales_by_slot", align_bytes=256, offset=CARRIED_PLACE)
-            for g0, g1 in ((0, 2), (2, PASSES)):
-                entries = key_list[:, LIST_COLS * g0 : LIST_COLS * g1]
-                nc.vector.tensor_copy(in_order[:, PASS * g0 : PASS * g1], key_table_scales[:].bitcast(U8).indirect(entries))
-            for g0, g1 in ((0, 2), (2, PASSES)):
+            by_slot = tile_at(CARRIED_PLACE, "key_scales_by_slot", [P, 3 * PIECE], U8)
+            parts = (slice(0, 2 * PASS), slice(2 * PASS, S))
+            for part in parts:
+                entries = key_list[:, part.start // ENTRIES : part.stop // ENTRIES]
+                nc.vector.tensor_copy(key_scales_in_order[:, part], key_table_scales[:].bitcast(U8).indirect(entries))
+            for part in parts:
                 nc.vector.tensor_copy(
-                    by_slot[:, PASS * g0 : PASS * g1].rearrange("p (g t m) -> p g t m", t=PACK, m=P),
-                    in_order[:, PASS * g0 : PASS * g1].rearrange("p (g m t) -> p g t m", t=PACK, m=P),
+                    by_slot[:, part].rearrange("p (g t m) -> p g t m", t=PACK, m=P),
+                    key_scales_in_order[:, part].rearrange("p (g m t) -> p g t m", t=PACK, m=P),
                 )
+            as_words = by_slot[:, 0:S].bitcast(I32)
             for r in range(ROWS):
-                nc.sync.dma_start(
-                    key_scales[KEY_SCALE_ROW + r : P : QUADRANT, :], by_slot[:, 0:S].bitcast(I32)[KEY_LOAD_ROW + r : P : ROWS, :]
-                )
+                nc.sync.dma_start(key_scales[KEY_SCALE_ROW + r : P : QUADRANT, :], as_words[KEY_LOAD_ROW + r : P : ROWS, :])
 
-        def gather_key_words(g):
-            if g == 0:
-                key_words[g] = keep.tile([P, PASS], U32, name="key_words0", align_bytes=256)
-            else:
-                place = CARRIED_PLACE + H_BYTES * (g - 1)
-                key_words[g] = shared.tile([P, PASS], U32, name="key_words%d" % g, align_bytes=256, offset=place)
-            entries = key_list[:, LIST_COLS * g : LIST_COLS * (g + 1)]
+        def gather_key_words(g, place=None):
+            key_words[g] = tile_at(place, "key_words%d" % g, [P, PASS], U32)
+            entries = key_list[:, PASS * g // ENTRIES : PASS * (g + 1) // ENTRIES]
             nc.vector.tensor_copy(
                 key_words[g][:].rearrange("p (t m) -> p m t", t=PACK), key_table[:].bitcast(U32).indirect(entries)
             )
 
+        def gather_user_words(half, users, place=None):
+            user_words[half] = tile_at(place, "user_words%d" % half, [P, HALF], U32)
+            for u in range(0, HALF, users):
+                entries = user_list[:, (HALF * half + u) // ENTRIES : (HALF * half + u + users) // ENTRIES]
+                nc.vector.tensor_copy(user_words[half][:, u : u + users], user_table[:].bitcast(U32).indirect(entries))
+
         bid_bank = banks.tile([P, P, PACK], F32, name="bid_bank")
-        bid_rows = keep.tile([P, PASSES, BID_ROW_USERS, PACK], F32, name="bid_rows", align_bytes=256)
+        bid_rows = keep.tile([P, PASSES, SHARE, PACK], F32, name="bid_rows", align_bytes=256)
 
         def place_bids():
             for t in range(PACK):
                 nc.tensor.transpose(bid_bank[:, :, t], bid_in_rows[:, t:PASS:PACK], identity[:])
             for g in range(PASSES):
-                nc.scalar.copy(bid_rows[:, g, :, :], bid_bank[:, BID_ROW + g, :].unsqueeze(1).to_broadcast([P, BID_ROW_USERS, PACK]))
+                nc.scalar.copy(bid_rows[:, g, :, :], bid_bank[:, BID_ROW + g, :].unsqueeze(1).to_broadcast([P, SHARE, PACK]))
 
-        def quads_place(step):
-            return 2 * SILU_BYTES * step
-
-        def pairs_place(step):
-            return quads_place(step) + SILU_BYTES
-
-        def round_wd(g, n0, n1, copy, offset=None):
-            first = n0
-            if (g, first) not in wd_rounded:
-                name, shape = "wd_rounded%d_%d" % (g, first), [P, SIDE, PACK]
-                if offset is None:
-                    wd_rounded[g, first] = keep.tile(shape, BF16, name=name, align_bytes=256)
-                else:
-                    wd_rounded[g, first] = shared.tile(shape, BF16, name=name, align_bytes=256, offset=offset)
+        def round_wd(g, side, copy, place=None):
+            wd_rounded[g, side] = tile_at(place, "wd_rounded%d_%d" % (g, side), [P, SIDE, PACK], BF16)
             copy(
-                wd_rounded[g, first][:, n0 - first : n1 - first, :].rearrange("p (c x) t -> p c t x", x=4),
-                wd_raw[g, n0][0][:, :, n0 - wd_raw[g, n0][1] : n1 - wd_raw[g, n0][1]].rearrange("p t (c x) -> p c t x", x=4),
+                wd_rounded[g, side][:].rearrange("p (c x) t -> p c t x", x=4),
+                wd_raw[g, side].rearrange("p t (c x) -> p c t x", x=4),
             )
 
-        def quantise_wd(g, n0, n1, offset=None):
-            name = "wd_codes%d_%d" % (g, n0)
-            if offset is None:
-                codes = keep.tile([P, n1 - n0], U32, name=name, align_bytes=256)
-            else:
-                codes = shared.tile([P, n1 - n0], U32, name=name, align_bytes=256, offset=offset)
-            scale_bytes = keep.tile([P, n1 - n0], U8, name="wd_scales%d_%d" % (g, n0), align_bytes=256)
-            for n in range(n0, n1, P):
-                wd_codes[g, n // P] = codes[:, n - n0 : n - n0 + P]
-                wd_scales[g, n // P] = scale_bytes[:, n - n0 : n - n0 + P]
+        def quantise_wd(g, side, place=None):
+            wd_codes[g, side] = tile_at(place, "wd_codes%d_%d" % (g, side), [P, SIDE], U32)
+            plane = keep.tile([P, WD_SCALE_SHIFT + SIDE], U8, name="wd_scales%d_%d" % (g, side), align_bytes=256)
+            wd_scales[g, side] = plane[:, WD_SCALE_SHIFT:]
             nc.vector.quantize_mx(
-                out=codes[:].bitcast(FP8X4),
-                scales=scale_bytes[:],
-                in_=wd_rounded[g, n0][:].rearrange("p n t -> p (n t)"),
+                out=wd_codes[g, side][:].bitcast(FP8X4),
+                scales=wd_scales[g, side],
+                in_=wd_rounded[g, side][:].rearrange("p n t -> p (n t)"),
             )
-
-        def score_tile(step, slots, user0, users):
-            g, half = step % PASSES, step // PASSES
-            scores = banks.tile([P, len(slots), users], F32, name="bank%d" % bank_of_scores(len(scored)))
-            scored.append(scores)
-            for k, t in enumerate(slots):
-                nc.tensor.matmul_mx(
-                    out=scores[:, k, :],
-                    lhsT=key_words[g][:, P * t : P * (t + 1)].bitcast(FP8X4),
-                    lhsT_scale=key_scales[:].bitcast(U8)[KEY_SCALE_ROW:P, PASS * g + P * t : PASS * g + P * (t + 1)],
-                    rhs=user_words[half][:, user0 : user0 + users].bitcast(FP8X4),
-                    rhs_scale=user_scales[:, HALF * half + user0 : HALF * half + user0 + users],
-                    start=True,
-                    stop=True,
-                )
-            return scores[:].rearrange("p t n -> p n t")
-
-        def score_part(step, kind, k):
-            if kind == "q":
-                if step not in quad_silus:
-                    quad_silus[step] = shared.tile([P, GROUP, PACK], F32, name="quad_silus%d" % step, align_bytes=256, offset=quads_place(step))
-                return quad_silus[step][:, P * k : P * (k + 1), :], score_tile(step, range(PACK), P * k, P)
-            if step not in pair_silus:
-                pair_silus[step] = shared.tile([P, 2, GROUP, 2], F32, name="pair_silus%d" % step, align_bytes=256, offset=pairs_place(step))
-            return pair_silus[step][:, k, :, :], score_tile(step, (2 * k, 2 * k + 1), GROUP, GROUP)
-
-        def apply_silu(silu_and_scores):
-            nc.scalar.activation(silu_and_scores[0], silu_and_scores[1], ACT.Silu)
 
         def make_silus(step, order):
-            for kind, k in order:
-                apply_silu(score_part(step, kind, k))
+            g, half = step % PASSES, step // PASSES
+            for group, k in order:
+                if (step, group) not in silus:
+                    shape = [P, 2, GROUP, 2] if group == PAIRS else [P, GROUP, PACK]
+                    silus[step, group] = tile_at(silus_place(step, group), "silus%d_%d" % (step, group), shape, F32)
+                if group == PAIRS:
+                    slots, user0, users, silu = (2 * k, 2 * k + 1), GROUP, GROUP, silus[step, group][:, k, :, :]
+                else:
+                    slots, user0, users, silu = range(PACK), P * k, P, silus[step, group][:, P * k : P * (k + 1), :]
+                scores = banks.tile([P, len(slots), users], F32, name="bank%d" % bank_of_scores(len(scored)))
+                scored.append(scores)
+                in_list = HALF * half + user0
+                for j, t in enumerate(slots):
+                    nc.tensor.matmul_mx(
+                        out=scores[:, j, :],
+                        lhsT=key_words[g][:, P * t : P * (t + 1)].bitcast(FP8X4),
+                        lhsT_scale=key_scales[:].bitcast(U8)[KEY_SCALE_ROW:P, PASS * g + P * t : PASS * g + P * (t + 1)],
+                        rhs=user_words[half][:, user0 : user0 + users].bitcast(FP8X4),
+                        rhs_scale=user_scales[:, in_list : in_list + users],
+                        start=True,
+                        stop=True,
+                    )
+                nc.scalar.activation(silu, scores[:].rearrange("p t n -> p n t"), ACT.Silu)
 
         def multiply(step):
             g = step % PASSES
-            share = SHARES[step]
-            pairs = shared.tile([P, GROUP, 2, 2], BF16, name="h_pairs%d" % step, align_bytes=256, offset=PAIRS_AT[step])
-            quads = shared.tile([P, GROUP, PACK], BF16, name="h_quads%d" % step, align_bytes=256, offset=QUADS_AT[step])
-            h_rounded[step] = quads, pairs
+            share, at_once = (SHARE, SHARE) if step else (GROUP, P)
+            pairs = tile_at(PAIRS_PLACE[step], "h_pairs%d" % step, [P, GROUP, 2, 2], BF16)
+            quads = tile_at(QUADS_PLACE[step], "h_quads%d" % step, [P, GROUP, PACK], BF16)
+            h_rounded[step, QUADS] = quads[:].rearrange("p n t -> p (n t)")
+            h_rounded[step, PAIRS] = pairs[:].rearrange("p n u e -> p (n u e)")
             bids = bid_bank[:, BID_ROW + g, :]
-            piece = P if share == GROUP else share
-            for u in range(0, share, piece):
-                nc.gpsimd.tensor_tensor(
-                    quads[:, u : u + piece, :], quad_silus[step][:, u : u + piece, :], bid_rows[:, g, 0:piece, :], ALU.mult
-                )
+            for u in range(0, share, at_once):
+                users = slice(u, u + at_once)
+                nc.gpsimd.tensor_tensor(quads[:, users, :], silus[step, QUADS][:, users, :], bid_rows[:, g, 0:at_once, :], ALU.mult)
             nc.vector.tensor_tensor(
                 pairs[:],
-                pair_silus[step][:].rearrange("p u n e -> p n u e"),
+                silus[step, PAIRS][:].rearrange("p u n e -> p n u e"),
                 bids.rearrange("p (u e) -> p u e", u=2).unsqueeze(1).to_broadcast([P, GROUP, 2, 2]),
                 ALU.mult,
             )
             if share < GROUP:
                 nc.vector.tensor_tensor(
                     quads[:, share:GROUP, :],
-                    quad_silus[step][:, share:GROUP, :],
+                    silus[step, QUADS][:, share:GROUP, :],
                     bids.unsqueeze(1).to_broadcast([P, GROUP - share, PACK]),
                     ALU.mult,
                 )
-            h_codes[step] = keep.tile([P, HALF], U32, name="h_codes%d" % step, align_bytes=256)
-            h_scales[step] = keep.tile([P, HALF], U8, name="h_scales%d" % step, align_bytes=256)
-
-        def quantise_group(step, group):
-            users = slice(GROUP * group, GROUP * (group + 1))
-            rounded = h_rounded[step][group][:]
-            rounded = rounded.rearrange("p n u e -> p (n u e)") if group else rounded.rearrange("p n t -> p (n t)")
-            nc.vector.quantize_mx(out=h_codes[step][:, users].bitcast(FP8X4), scales=h_scales[step][:, users], in_=rounded)
 
         def quantise_h(step):
-            quantise_group(step, 1)
-            quantise_group(step, 0)
-
-        def opens(step, c):
-            half = step // PASSES
-            if (half, c) in sums:
-                return False
-            sums[half, c] = banks.tile([P, HALF], F32, name="bank%d" % (SECOND_HALF_BANKS[c] if half else c))
-            return True
+            h_codes[step] = keep.tile([P, HALF], U32, name="h_codes%d" % step, align_bytes=256)
+            plane = keep.tile([P, H_SCALE_SHIFT + HALF], U8, name="h_scales%d" % step, align_bytes=256)
+            h_scales[step] = plane[:, H_SCALE_SHIFT:]
+            for group in (PAIRS, QUADS) if step else (QUADS, PAIRS):
+                users = slice(GROUP * group, GROUP * (group + 1))
+                nc.vector.quantize_mx(
+                    out=h_codes[step][:, users].bitcast(FP8X4), scales=h_scales[step][:, users], in_=h_rounded[step, group]
+                )
 
         def add_w4(step, c):
             g, half = step % PASSES, step // PASSES
-            first = opens(step, c)
+            if g == 0:
+                sums[half, c] = banks.tile([P, HALF], F32, name="bank%d" % (SECOND_HALF_BANKS[c] if half else c))
             nc.tensor.matmul_mx(
                 out=sums[half, c][:],
                 lhsT=w4_codes[:, g, 2 * P * c : 2 * P * (c + 1)].bitcast(FP4X4),
                 lhsT_scale=w4_scale_tile[:, g, :].bitcast(U8)[:, P * c : P * (c + 1)],
                 rhs=h_codes[step][:].bitcast(FP8X4),
-                rhs_scale=h_scales[step][:],
-                start=first,
+                rhs_scale=h_scales[step],
+                start=(g == 0),
                 stop=False,
             )
 
-        def add_wd(step, c, closes):
-            g = step % PASSES
-            first = opens(step, c)
+        def add_wd(step, c, closes=False):
+            g, side = step % PASSES, P * c // SIDE
+            campaigns = slice(P * c % SIDE, P * c % SIDE + P)
             nc.tensor.matmul_mx(
                 out=sums[step // PASSES, c][:],
-                lhsT=wd_codes[g, c].bitcast(FP8X4),
-                lhsT_scale=wd_scales[g, c],
+                lhsT=wd_codes[g, side][:, campaigns].bitcast(FP8X4),
+                lhsT_scale=wd_scales[g, side][:, campaigns],
                 rhs=h_codes[step][:].bitcast(FP8X4),
-                rhs_scale=h_scales[step][:],
-                start=first,
+                rhs_scale=h_scales[step],
+                start=False,
                 stop=closes,
             )
 
@@ -320,80 +299,73 @@ def tile_list_keyword_campaign_values_kernel(
 
         gather_key_scales()
         nc.sync.dma_start(w4_codes[:].bitcast(I32), w4_words.rearrange("g p c -> p g c").bitcast(I32))
-        for r in range(2, 4):
-            nc.sync.dma_start(
-                w4_scale_tile[r:P:QUADRANT, :, :], w4_scales[:, r:16:ROWS, :].rearrange("g q c -> q g c").bitcast(I32)
-            )
-        load_wd(0)
-        load_wd(1, 0, SIDE)
-        load_wd(1, SIDE, N)
-        load_wd(2)
+        load_w4_scales(range(ROWS // 2, ROWS))
+        load_wd(0, (0, 1))
+        load_wd(1, (0,))
+        load_wd(1, (1,))
+        load_wd(2, (0, 1))
         with nc.allow_non_contiguous_dma(reason="one bias value to a partition and campaign tile"):
             nc.sync.dma_start(bias_tile[:], b.rearrange("(c p) -> p c", p=P))
 
         place_bids()
         nc.vector.tensor_copy(user_scales[:], user_table_scales[:].bitcast(U8).indirect(user_list[:]))
         gather_key_words(0)
-        gather_user_words(0)
-        gather_key_words(1)
-        gather_key_words(2)
-        gather_user_words(1)
+        gather_user_words(0, GROUP)
+        gather_key_words(1, CARRIED_PLACE)
+        gather_key_words(2, CARRIED_PLACE + PIECE)
+        gather_user_words(1, HALF, CARRIED_PLACE + 2 * PIECE)
 
-        def w4_pass(step):
-            for c in range(N_TILES):
-                add_w4(step, c)
+        make_silus(0, FIRST_ORDER)
+        make_silus(1, ORDER)
+        make_silus(2, ORDER)
+        round_wd(1, 0, nc.scalar.copy)
+        make_silus(3, ORDER)
+        round_wd(1, 1, nc.scalar.copy)
+        make_silus(4, ORDER)
+        make_silus(LAST, ORDER)
 
-        def wd_pass(step):
-            for c in range(N_TILES):
-                add_wd(step, c, closes=(step % PASSES == PASSES - 1))
-
-        make_silus(0, FIRST)
-        make_silus(1, WIDE)
-        make_silus(2, WIDE)
-        round_wd(1, 0, SIDE, nc.scalar.copy)
-        make_silus(3, WIDE)
-        round_wd(1, SIDE, N, nc.scalar.copy)
-        make_silus(4, WIDE)
-        make_silus(LAST, WIDE)
         multiply(0)
-        quantise_group(0, 0)
-        quantise_group(0, 1)
-        round_wd(0, 0, SIDE, nc.vector.tensor_copy, offset=pairs_place(0))
-        round_wd(0, SIDE, N, nc.vector.tensor_copy, offset=pairs_place(0) + H_BYTES)
-        quantise_wd(0, 0, SIDE)
-        quantise_wd(0, SIDE, N)
-        w4_pass(0)
-        wd_pass(0)
+        quantise_h(0)
+        for side in (0, 1):
+            round_wd(0, side, nc.vector.tensor_copy, silus_place(0, PAIRS) + PIECE * side)
+        for side in (0, 1):
+            quantise_wd(0, side)
+        for c in range(N_TILES):
+            add_w4(0, c)
+        for c in range(N_TILES):
+            add_wd(0, c)
         multiply(1)
         quantise_h(1)
-        w4_pass(1)
+        for c in range(N_TILES):
+            add_w4(1, c)
+
         multiply(2)
         quantise_h(2)
-        quantise_wd(1, 0, SIDE, offset=quads_place(2))
-        round_wd(2, 0, SIDE, nc.vector.tensor_copy, offset=pairs_place(2))
-        round_wd(2, SIDE, N, nc.vector.tensor_copy, offset=quads_place(2) + H_BYTES)
-        quantise_wd(2, 0, SIDE)
-        quantise_wd(2, SIDE, N)
-        quantise_wd(1, SIDE, N, offset=LAST_RAW_PLACE + H_BYTES)
-        w4_pass(2)
-        for g in (1, 2):
-            for c in (0, 1):
-                add_wd(g, c, closes=(g == 2))
-        for g in (2, 1):
-            for c in (2, 3):
-                add_wd(g, c, closes=(g == 1))
+        quantise_wd(1, 0, silus_place(2, QUADS))
+        round_wd(2, 0, nc.vector.tensor_copy, silus_place(2, PAIRS))
+        round_wd(2, 1, nc.vector.tensor_copy, silus_place(2, QUADS) + PIECE)
+        quantise_wd(2, 0)
+        quantise_wd(2, 1)
+        quantise_wd(1, 1, RAW_PLACE[2] + PIECE)
+        for c in range(N_TILES):
+            add_w4(2, c)
+        for tiles, steps in (((0, 1), (1, 2)), ((2, 3), (2, 1))):
+            for step in steps:
+                for c in tiles:
+                    add_wd(step, c, closes=(step == steps[-1]))
         for c in range(N_TILES):
             store(0, c)
-        multiply(3)
-        quantise_h(3)
+
+        multiply(PASSES)
+        quantise_h(PASSES)
         for c in range(N_TILES):
-            add_w4(3, c)
-            add_wd(3, c, closes=False)
-        for step in (4, 5):
+            add_w4(PASSES, c)
+            add_wd(PASSES, c)
+        for step in (LAST - 1, LAST):
             multiply(step)
             quantise_h(step)
         for tiles in (range(N_TILES - 1), (N_TILES - 1,)):
-            for step in (4, 5):
+            for step in (LAST - 1, LAST):
                 for c in tiles:
                     add_w4(step, c)
                     add_wd(step, c, closes=(step == LAST))

from contextlib import ExitStack

import concourse.mybir as mybir
from concourse.masks import make_identity

K, T, S, T2, S2, N = 512, 4096, 1536, 2048, 1024, 512
FLOPS = 2 * K * S * S2 + 2 * 2 * S * N * S2

F32 = mybir.dt.float32
BF16 = mybir.dt.bfloat16
I32 = mybir.dt.int32
U32 = mybir.dt.uint32
U16 = mybir.dt.uint16
U8 = mybir.dt.uint8
FP8X4 = mybir.dt.float8_e4m3fn_x4
FP4X4 = mybir.dt.float4_e2m1fn_x4
ACT = mybir.ActivationFunctionType
ALU = mybir.AluOpType

P = 128
PACK = 4
PASS = P * PACK
PASSES = S // PASS
ENTRIES = 16
QUADRANT = 32
ROWS = 4
HALF = S2 // 2
GROUP = HALF // 2
QUADS, PAIRS = 0, 1
STEPS = 2 * PASSES
LAST = STEPS - 1
N_TILES = N // P
SIDE = N // 2
KEY_LOAD_ROW = P - 16
KEY_SCALE_ROW = 4
BID_ROW = P - PASSES
SHARE = 160
H_SCALE_SHIFT, WD_SCALE_SHIFT = 128, 64
FIRST_ORDER = ((QUADS, 0), (PAIRS, 0), (QUADS, 1), (PAIRS, 1))
ORDER = ((PAIRS, 0), (PAIRS, 1), (QUADS, 0), (QUADS, 1))
SCORE_BANKS = 3
SECOND_HALF_BANKS = (6, 4, 5, 0)

SILU_BYTES = GROUP * PACK * 4
PIECE = GROUP * PACK * 2
H_PLACE = 2 * SILU_BYTES * STEPS
CARRIED_PLACE = H_PLACE + 3 * PIECE
RAW_PLACE = {2: CARRIED_PLACE + 3 * PIECE, 0: CARRIED_PLACE + 7 * PIECE}


def silus_place(step, group):
    return SILU_BYTES * (2 * step + group)


QUADS_PLACE = (
    H_PLACE + PIECE,
    silus_place(0, PAIRS),
    RAW_PLACE[0],
    silus_place(2, QUADS) + PIECE,
    RAW_PLACE[2],
    H_PLACE,
)
PAIRS_PLACE = (
    H_PLACE,
    RAW_PLACE[0],
    H_PLACE,
    RAW_PLACE[2],
    H_PLACE,
    H_PLACE + PIECE,
)


def bank_of_scores(index):
    if index < N_TILES:
        return index
    return N_TILES + (index - N_TILES) % SCORE_BANKS


def tile_list_keyword_campaign_values_kernel(
    tc, tab_words, tab_scales, tab2_words, tab2_scales, offs, offs2, bid, w4_words, w4_scales, wd, b, out
):
    nc = tc.nc
    with ExitStack() as ctx:
        keep = ctx.enter_context(tc.tile_pool(name="keep", bufs=1))
        shared = ctx.enter_context(tc.tile_pool(name="shared", bufs=1))
        banks = ctx.enter_context(tc.psum_pool(name="banks", bufs=1))

        def tile_at(place, name, shape, dtype):
            if place is None:
                return keep.tile(shape, dtype, name=name, align_bytes=256)
            return shared.tile(shape, dtype, name=name, align_bytes=256, offset=place)

        key_list = keep.tile([P, S // ENTRIES], U16, name="key_list")
        user_list = keep.tile([P, S2 // ENTRIES], U16, name="user_list")
        key_table = keep.tile([P, T], I32, name="key_table", align_bytes=256)
        user_table = keep.tile([P, T2], I32, name="user_table", align_bytes=256)
        key_table_scales = keep.tile([P, T // 4], I32, name="key_table_scales", align_bytes=256)
        user_table_scales = keep.tile([P, T2 // 4], I32, name="user_table_scales", align_bytes=256)
        w4_codes = keep.tile([P, PASSES, 2 * N], U8, name="w4_codes", align_bytes=256)
        w4_scale_tile = keep.tile([P, PASSES, N // 4], I32, name="w4_scale_tile", align_bytes=256)
        bid_in_rows = keep.tile([P, PASS], F32, name="bid_in_rows", align_bytes=256)
        identity = keep.tile([P, P], F32, name="identity", align_bytes=256)
        bias_tile = keep.tile([P, N_TILES], F32, name="bias_tile")
        key_scales = keep.tile([P, S // 4], I32, name="key_scales", align_bytes=256)
        wd_raw = {}

        def load_wd(g, sides):
            n0, width = SIDE * sides[0], SIDE * len(sides)
            raw = tile_at(RAW_PLACE.get(g), "wd_raw%d_%d" % (g, n0), [P, PACK, width], F32)
            for k, side in enumerate(sides):
                wd_raw[g, side] = raw[:, :, SIDE * k : SIDE * (k + 1)]
            rows = wd[PASS * g : PASS * (g + 1), n0 : n0 + width]
            nc.sync.dma_start(raw[:], rows.rearrange("(p t) n -> p t n", t=PACK))

        def load_w4_scales(rows):
            for r in rows:
                nc.sync.dma_start(
                    w4_scale_tile[r:P:QUADRANT, :, :], w4_scales[:, r:16:ROWS, :].rearrange("g q c -> q g c").bitcast(I32)
                )

        nc.vector.memset(user_table_scales[:], 0)
        nc.vector.memset(key_table_scales[0:KEY_LOAD_ROW, :], 0)
        nc.vector.memset(bid_in_rows[0:BID_ROW, :], 0.0)
        nc.vector.memset(key_scales[:], 0)
        nc.vector.memset(w4_scale_tile[:], 0)
        make_identity(nc, identity[:])
        warm_up = keep.tile([P, 2], F32, name="warm_up")
        nc.vector.memset(warm_up[:, 0:1], 0.0)

        nc.sync.dma_start(key_list[:], offs)
        nc.sync.dma_start(key_table_scales[KEY_LOAD_ROW:P, :], tab_scales[0].bitcast(I32))
        nc.sync.dma_start(user_list[:], offs2)
        for r in range(ROWS):
            nc.sync.dma_start(user_table_scales[r:P:QUADRANT, :], tab2_scales[0, r:16:ROWS, :].bitcast(I32))
        nc.sync.dma_start(key_table[:], tab_words[0].rearrange("p t i -> p (t i)").bitcast(I32))
        bid_by_pass = bid.rearrange("(g i) -> g i", g=PASSES)
        nc.sync.dma_start(bid_in_rows[BID_ROW : BID_ROW + 2, :], bid_by_pass[0:2, :])
        nc.sync.dma_start(bid_in_rows[BID_ROW + 2 : P, :], bid_by_pass[2:PASSES, :])
        nc.sync.dma_start(user_table[:], tab2_words[0].rearrange("p t i -> p (t i)").bitcast(I32))
        load_w4_scales(range(0, ROWS // 2))
        nc.scalar.activation(warm_up[:, 1:2], warm_up[:, 0:1], ACT.Silu)

        user_scales = keep.tile([P, S2], U8, name="user_scales", align_bytes=256)
        key_scales_in_order = keep.tile([P, S], U8, name="key_scales_in_order", align_bytes=256)
        user_words, key_words, wd_rounded, wd_codes, wd_scales = {}, {}, {}, {}, {}
        silus, h_rounded, h_codes, h_scales, sums = {}, {}, {}, {}, {}
        scored = []

        def gather_key_scales():
            by_slot = tile_at(CARRIED_PLACE, "key_scales_by_slot", [P, 3 * PIECE], U8)
            parts = (slice(0, 2 * PASS), slice(2 * PASS, S))
            for part in parts:
                entries = key_list[:, part.start // ENTRIES : part.stop // ENTRIES]
                nc.vector.tensor_copy(key_scales_in_order[:, part], key_table_scales[:].bitcast(U8).indirect(entries))
            for part in parts:
                nc.vector.tensor_copy(
                    by_slot[:, part].rearrange("p (g t m) -> p g t m", t=PACK, m=P),
                    key_scales_in_order[:, part].rearrange("p (g m t) -> p g t m", t=PACK, m=P),
                )
            as_words = by_slot[:, 0:S].bitcast(I32)
            for r in range(ROWS):
                nc.sync.dma_start(key_scales[KEY_SCALE_ROW + r : P : QUADRANT, :], as_words[KEY_LOAD_ROW + r : P : ROWS, :])

        def gather_key_words(g, place=None):
            key_words[g] = tile_at(place, "key_words%d" % g, [P, PASS], U32)
            entries = key_list[:, PASS * g // ENTRIES : PASS * (g + 1) // ENTRIES]
            nc.vector.tensor_copy(
                key_words[g][:].rearrange("p (t m) -> p m t", t=PACK), key_table[:].bitcast(U32).indirect(entries)
            )

        def gather_user_words(half, users, place=None):
            user_words[half] = tile_at(place, "user_words%d" % half, [P, HALF], U32)
            for u in range(0, HALF, users):
                entries = user_list[:, (HALF * half + u) // ENTRIES : (HALF * half + u + users) // ENTRIES]
                nc.vector.tensor_copy(user_words[half][:, u : u + users], user_table[:].bitcast(U32).indirect(entries))

        bid_bank = banks.tile([P, P, PACK], F32, name="bid_bank")
        bid_rows = keep.tile([P, PASSES, SHARE, PACK], F32, name="bid_rows", align_bytes=256)

        def place_bids():
            for t in range(PACK):
                nc.tensor.transpose(bid_bank[:, :, t], bid_in_rows[:, t:PASS:PACK], identity[:])
            for g in range(PASSES):
                nc.scalar.copy(bid_rows[:, g, :, :], bid_bank[:, BID_ROW + g, :].unsqueeze(1).to_broadcast([P, SHARE, PACK]))

        def round_wd(g, side, copy, place=None):
            wd_rounded[g, side] = tile_at(place, "wd_rounded%d_%d" % (g, side), [P, SIDE, PACK], BF16)
            copy(
                wd_rounded[g, side][:].rearrange("p (c x) t -> p c t x", x=4),
                wd_raw[g, side].rearrange("p t (c x) -> p c t x", x=4),
            )

        def quantise_wd(g, side, place=None):
            wd_codes[g, side] = tile_at(place, "wd_codes%d_%d" % (g, side), [P, SIDE], U32)
            plane = keep.tile([P, WD_SCALE_SHIFT + SIDE], U8, name="wd_scales%d_%d" % (g, side), align_bytes=256)
            wd_scales[g, side] = plane[:, WD_SCALE_SHIFT:]
            nc.vector.quantize_mx(
                out=wd_codes[g, side][:].bitcast(FP8X4),
                scales=wd_scales[g, side],
                in_=wd_rounded[g, side][:].rearrange("p n t -> p (n t)"),
            )

        def make_silus(step, order):
            g, half = step % PASSES, step // PASSES
            for group, k in order:
                if (step, group) not in silus:
                    shape = [P, 2, GROUP, 2] if group == PAIRS else [P, GROUP, PACK]
                    silus[step, group] = tile_at(silus_place(step, group), "silus%d_%d" % (step, group), shape, F32)
                if group == PAIRS:
                    slots, user0, users, silu = (2 * k, 2 * k + 1), GROUP, GROUP, silus[step, group][:, k, :, :]
                else:
                    slots, user0, users, silu = range(PACK), P * k, P, silus[step, group][:, P * k : P * (k + 1), :]
                scores = banks.tile([P, len(slots), users], F32, name="bank%d" % bank_of_scores(len(scored)))
                scored.append(scores)
                in_list = HALF * half + user0
                for j, t in enumerate(slots):
                    nc.tensor.matmul_mx(
                        out=scores[:, j, :],
                        lhsT=key_words[g][:, P * t : P * (t + 1)].bitcast(FP8X4),
                        lhsT_scale=key_scales[:].bitcast(U8)[KEY_SCALE_ROW:P, PASS * g + P * t : PASS * g + P * (t + 1)],
                        rhs=user_words[half][:, user0 : user0 + users].bitcast(FP8X4),
                        rhs_scale=user_scales[:, in_list : in_list + users],
                        start=True,
                        stop=True,
                    )
                nc.scalar.activation(silu, scores[:].rearrange("p t n -> p n t"), ACT.Silu)

        def multiply(step):
            g = step % PASSES
            share, at_once = (SHARE, SHARE) if step else (GROUP, P)
            pairs = tile_at(PAIRS_PLACE[step], "h_pairs%d" % step, [P, GROUP, 2, 2], BF16)
            quads = tile_at(QUADS_PLACE[step], "h_quads%d" % step, [P, GROUP, PACK], BF16)
            h_rounded[step, QUADS] = quads[:].rearrange("p n t -> p (n t)")
            h_rounded[step, PAIRS] = pairs[:].rearrange("p n u e -> p (n u e)")
            bids = bid_bank[:, BID_ROW + g, :]
            for u in range(0, share, at_once):
                users = slice(u, u + at_once)
                nc.gpsimd.tensor_tensor(quads[:, users, :], silus[step, QUADS][:, users, :], bid_rows[:, g, 0:at_once, :], ALU.mult)
            nc.vector.tensor_tensor(
                pairs[:],
                silus[step, PAIRS][:].rearrange("p u n e -> p n u e"),
                bids.rearrange("p (u e) -> p u e", u=2).unsqueeze(1).to_broadcast([P, GROUP, 2, 2]),
                ALU.mult,
            )
            if share < GROUP:
                nc.vector.tensor_tensor(
                    quads[:, share:GROUP, :],
                    silus[step, QUADS][:, share:GROUP, :],
                    bids.unsqueeze(1).to_broadcast([P, GROUP - share, PACK]),
                    ALU.mult,
                )

        def quantise_h(step):
            h_codes[step] = keep.tile([P, HALF], U32, name="h_codes%d" % step, align_bytes=256)
            plane = keep.tile([P, H_SCALE_SHIFT + HALF], U8, name="h_scales%d" % step, align_bytes=256)
            h_scales[step] = plane[:, H_SCALE_SHIFT:]
            for group in (PAIRS, QUADS) if step else (QUADS, PAIRS):
                users = slice(GROUP * group, GROUP * (group + 1))
                nc.vector.quantize_mx(
                    out=h_codes[step][:, users].bitcast(FP8X4), scales=h_scales[step][:, users], in_=h_rounded[step, group]
                )

        def add_w4(step, c):
            g, half = step % PASSES, step // PASSES
            if g == 0:
                sums[half, c] = banks.tile([P, HALF], F32, name="bank%d" % (SECOND_HALF_BANKS[c] if half else c))
            nc.tensor.matmul_mx(
                out=sums[half, c][:],
                lhsT=w4_codes[:, g, 2 * P * c : 2 * P * (c + 1)].bitcast(FP4X4),
                lhsT_scale=w4_scale_tile[:, g, :].bitcast(U8)[:, P * c : P * (c + 1)],
                rhs=h_codes[step][:].bitcast(FP8X4),
                rhs_scale=h_scales[step],
                start=(g == 0),
                stop=False,
            )

        def add_wd(step, c, closes=False):
            g, side = step % PASSES, P * c // SIDE
            campaigns = slice(P * c % SIDE, P * c % SIDE + P)
            nc.tensor.matmul_mx(
                out=sums[step // PASSES, c][:],
                lhsT=wd_codes[g, side][:, campaigns].bitcast(FP8X4),
                lhsT_scale=wd_scales[g, side][:, campaigns],
                rhs=h_codes[step][:].bitcast(FP8X4),
                rhs_scale=h_scales[step],
                start=False,
                stop=closes,
            )

        def store(half, c, on_vector=False, piece=HALF):
            for j0 in range(0, HALF, piece):
                result = keep.tile([P, piece], F32, name="result%d_%d_%d" % (half, c, j0))
                bank = sums[half, c][:, j0 : j0 + piece]
                if on_vector:
                    nc.vector.tensor_scalar(result[:], bank, bias_tile[:, c : c + 1], None, ALU.add)
                else:
                    nc.scalar.activation(result[:], bank, ACT.Identity, bias=bias_tile[:, c : c + 1])
                nc.sync.dma_start(out[P * c : P * (c + 1), HALF * half + j0 : HALF * half + j0 + piece], result[:])

        gather_key_scales()
        nc.sync.dma_start(w4_codes[:].bitcast(I32), w4_words.rearrange("g p c -> p g c").bitcast(I32))
        load_w4_scales(range(ROWS // 2, ROWS))
        load_wd(0, (0, 1))
        load_wd(1, (0,))
        load_wd(1, (1,))
        load_wd(2, (0, 1))
        with nc.allow_non_contiguous_dma(reason="one bias value to a partition and campaign tile"):
            nc.sync.dma_start(bias_tile[:], b.rearrange("(c p) -> p c", p=P))

        place_bids()
        nc.vector.tensor_copy(user_scales[:], user_table_scales[:].bitcast(U8).indirect(user_list[:]))
        gather_key_words(0)
        gather_user_words(0, GROUP)
        gather_key_words(1, CARRIED_PLACE)
        gather_key_words(2, CARRIED_PLACE + PIECE)
        gather_user_words(1, HALF, CARRIED_PLACE + 2 * PIECE)

        make_silus(0, FIRST_ORDER)
        make_silus(1, ORDER)
        make_silus(2, ORDER)
        round_wd(1, 0, nc.scalar.copy)
        make_silus(3, ORDER)
        round_wd(1, 1, nc.scalar.copy)
        make_silus(4, ORDER)
        make_silus(LAST, ORDER)

        multiply(0)
        quantise_h(0)
        for side in (0, 1):
            round_wd(0, side, nc.vector.tensor_copy, silus_place(0, PAIRS) + PIECE * side)
        for side in (0, 1):
            quantise_wd(0, side)
        for c in range(N_TILES):
            add_w4(0, c)
        for c in range(N_TILES):
            add_wd(0, c)
        multiply(1)
        quantise_h(1)
        for c in range(N_TILES):
            add_w4(1, c)

        multiply(2)
        quantise_h(2)
        quantise_wd(1, 0, silus_place(2, QUADS))
        round_wd(2, 0, nc.vector.tensor_copy, silus_place(2, PAIRS))
        round_wd(2, 1, nc.vector.tensor_copy, silus_place(2, QUADS) + PIECE)
        quantise_wd(2, 0)
        quantise_wd(2, 1)
        quantise_wd(1, 1, RAW_PLACE[2] + PIECE)
        for c in range(N_TILES):
            add_w4(2, c)
        for tiles, steps in (((0, 1), (1, 2)), ((2, 3), (2, 1))):
            for step in steps:
                for c in tiles:
                    add_wd(step, c, closes=(step == steps[-1]))
        for c in range(N_TILES):
            store(0, c)

        multiply(PASSES)
        quantise_h(PASSES)
        for c in range(N_TILES):
            add_w4(PASSES, c)
            add_wd(PASSES, c)
        for step in (LAST - 1, LAST):
            multiply(step)
            quantise_h(step)
        for tiles in (range(N_TILES - 1), (N_TILES - 1,)):
            for step in (LAST - 1, LAST):
                for c in tiles:
                    add_w4(step, c)
                    add_wd(step, c, closes=(step == LAST))
        for c in range(N_TILES):
            store(1, c, on_vector=(c % 2 == 1), piece=GROUP)
